import numpy as np, ml_dtypes
CORES = [2,3,42,43,82,83,122,123]
N = 8
BF = ml_dtypes.bfloat16
def gentries(a):
    return np.ascontiguousarray(a.reshape(8, 16, -1).transpose(0, 2, 1)).reshape(8, -1)
def gtable(e):
    e = np.asarray(e); return np.ascontiguousarray(e.reshape(8, -1, 16).transpose(0, 2, 1)).reshape(128, -1).astype(np.int32)
V, TL, FM, LM = 2048, 8, 15, 256
NT = 8 // TL
def pick(a, i):
    return np.take_along_axis(a, i, -1)
def turn(x):
    return np.argsort(x, axis=-1)
def put(P, a, b, g, p):
    P[min(a, b), max(a, b), g] = p if a < b else turn(p)
def setw(W, a, b, t, w):
    W[min(a, b), max(a, b), t] = w
def same():
    P = np.empty((N, N, 8, V), np.int64); P[...] = np.arange(V)
    return P
def noise(rng, part):
    p = np.tile(np.arange(V), (len(part), 1))
    for i in range(len(part)):
        x = rng.permutation(V)[:max(2, int(part[i] * V))]; p[i, x] = np.roll(x, 1)
    return p
def twins(rng, share, n):
    return np.arange(V)[None, :] ^ np.repeat((rng.random((n, V // 2)) < share).astype(np.int64), 2, axis=1)
def swaps(n):
    p = np.arange(V); p[n] = n.reshape(-1, 2)[:, ::-1].reshape(-1)
    return p
def paired(rng, b):
    c = np.where(rng.random(b.shape) < 0.4, np.where(b < FM, b + 1, b - 1), b)
    f = np.tile(np.stack([b, c], -1).reshape(8, 16, V), (N, 1, 1, 1))
    return np.clip(f + (rng.random(f.shape) < 0.05) * rng.integers(-1, 2, f.shape), 0, FM)
def scene(rng, P, W, lo, hi):
    def good():
        return noise(rng, lo * (0.25 + 0.75 * rng.random(TL)))
    def bad():
        return noise(rng, hi + 0.2 * rng.random(TL))
    kinds = min(3, NT * (N // 4)); s = int(rng.integers(0, kinds))
    for t in range(NT):
        g = slice(t * TL, t * TL + TL)
        for a in range(N):
            for b in range(a + 1, N): put(P, a, b, g, bad())
        for q in range(N // 4):
            m = int(rng.integers(0, 4)); L = [4 * q + (i ^ m) for i in range(4)]; kind = (t * (N // 4) + q + s) % kinds
            if kind < 2:
                for i, k in (((0, 3), (3, 1), (1, 2)), ((0, 2), (2, 1), (1, 3)))[kind]: put(P, L[i], L[k], g, good())
            else:
                for i in range(4):
                    for k in range(i): put(P, L[i], L[k], g, good())
                x = twins(rng, 0.5, TL); put(P, L[0], L[2], g, x); put(P, L[1], L[3], g, x)
                setw(W, L[0], L[1], t, LM); setw(W, L[2], L[3], t, 0)
        if N == 8:
            for d in (4, 6):
                h = int(rng.integers(0, 2)); b = (2 * h) ^ int(rng.integers(0, 2)); put(P, b, b ^ (d + 1), g, good())
                a = 2 - 2 * h; x = twins(rng, 0.5, TL)
                put(P, a, a ^ d, g, good()); put(P, a ^ 1, a ^ 1 ^ d, g, good()); put(P, a, a ^ d ^ 1, g, x); put(P, a ^ 1, a ^ d, g, x)
                setw(W, a, a ^ d, t, LM); setw(W, a ^ 1, a ^ 1 ^ d, t, 0)
def pack(Q, f, P, W):
    ft = pick(f, Q[:, :, None, :]); back = turn(Q); X = np.empty((N, 8, N - 1, V), np.int64); lam = np.empty((N, NT, N - 1), np.int32)
    for a in range(N):
        for b in range(a + 1, N):
            x = pick(back[b], pick(P[a, b], Q[a])); d = a ^ b
            X[a, :, d - 1] = x; X[b, :, d - 1] = turn(x); lam[a, :, d - 1] = W[a, b]; lam[b, :, d - 1] = W[a, b]
    return {"ft": np.ascontiguousarray(ft.reshape(N, 128, V)).astype(np.float32).astype(BF), "mp": np.stack([gtable(x.reshape(8, -1)) for x in X]), "lam": lam}
def setup_inputs(rng):
    Q = np.argsort(rng.random((N, 8, V)), axis=-1); f = paired(rng, rng.integers(0, FM + 1, (8, 16, V // 2)))
    P = same(); W = rng.integers(0, LM + 1, (N, N, NT)); scene(rng, P, W, 0.04, 0.7)
    return pack(Q, f, P, W)
def setup_inputs_spread(rng):
    Q = np.argsort(rng.random((N, 8, V)), axis=-1)
    b = np.minimum(((FM + 1) * rng.random((8, 16, V // 2)) ** np.exp2(rng.integers(-2, 4, (8, 16, 1)))).astype(np.int64), FM); f = paired(rng, b)
    P = same(); W = np.clip(np.exp2(rng.random((N, N, NT)) * np.log2(LM + 2.0)).astype(np.int64) - 1, 0, LM); scene(rng, P, W, 0.06, 0.55)
    return pack(Q, f, P, W)
def setup_inputs_ends(rng):
    h = V // 2; x = np.arange(V)
    f = np.tile(FM * ((x & 1) ^ rng.integers(0, 2, (8, 16, 1))), (N, 1, 1, 1))
    Q = np.empty((N, 8, V), np.int64); Q[..., 0::2] = 2 * np.argsort(rng.random((N, 8, h)), axis=-1); Q[..., 1::2] = 2 * np.argsort(rng.random((N, 8, h)), axis=-1) + 1
    P = same(); W = LM * rng.integers(0, 2, (N, N, NT))
    for a in range(N):
        for b in range(a + 1, N):
            k = (a ^ b) & 1
            P[a, b, :, 0::2] = 2 * np.argsort(rng.random((8, h)), axis=-1) + k; P[a, b, :, 1::2] = 2 * np.argsort(rng.random((8, h)), axis=-1) + 1 - k
            for g in range(8):
                m = int(rng.choice(np.array([0, 0, 1, 3, V // 16]))); i = 2 * rng.permutation(h)[:m]; o = 2 * rng.permutation(h)[:m] + 1
                u = P[a, b, g, i].copy(); P[a, b, g, i] = P[a, b, g, o]; P[a, b, g, o] = u
    for r in range(N): setw(W, r, r ^ 1, slice(0, NT), LM); setw(W, r, r ^ 2, slice(0, NT), 0)
    L = N - 4
    for g in range(8 - TL, 8):
        o = 2 * int(rng.integers(0, h)) + 1; y = 2 * int(rng.integers(1, V // 8)); z = h + 2 * int(rng.integers(0, V // 8))
        t02 = 2 * int(rng.integers(0, h)); t12 = 2 * int(rng.integers(0, h)) + 1; t23 = o; t03 = o + y + t02; t13 = o + z + t12
        t01 = t03 - t23 - t12 + (0 if g == 8 - TL else y)
        for i, k, s in ((0, 1, t01), (0, 2, t02), (0, 3, t03), (1, 2, t12), (1, 3, t13), (2, 3, t23)): P[L + i, L + k, g] = (x + s) % V
    for i, k, w in ((0, 1, LM), (0, 2, LM), (0, 3, 0), (1, 2, 0), (1, 3, 0), (2, 3, LM)): setw(W, L + i, L + k, NT - 1, w)
    return pack(Q, f, P, W)
def plain(rng):
    x = np.arange(V); e = x.copy(); e[0] = V - 1; e[V - 1] = 0
    S = [x, x[::-1], (x + 1) % V, (x - 1) % V, x ^ 1, e]
    Q = np.tile(x, (N, 8, 1)); P = same(); W = rng.choice(np.array([0, 1, LM - 1, LM]), (N, N, NT))
    for a in range(N):
        for b in range(a + 1, N):
            for g in range(8):
                i = int(rng.integers(0, 8)); P[a, b, g] = S[i] if i < 6 else rng.permutation(V)
    f = rng.integers(0, FM + 1, (N, 8, 16, V)); k = rng.permutation(8)
    f[:, k[0]] = FM * rng.integers(0, 2, (N, 16, 1)); f[:, k[1]] = FM * (x == V - 1); f[:, k[2]] = x * (FM + 1) // V; f[:, k[3]] = FM * rng.integers(0, 2, (N, 16, V)); f[:, k[4]] = f[:1, k[4]]
    return Q, f, P, W
def late(rng, f, P, W):
    x = np.arange(V); S = [x, x[::-1], (x + 1) % V, (x - 1) % V, x ^ 1]; k = int(rng.integers(0, TL)); ramp = x * (FM + 1) // V
    for g in range(TL):
        if g == k:
            p, q, a, y, o = [rng.permutation(V) for i in range(5)]; s = np.empty(V, np.int64); s[o] = np.roll(o, -1)
            b = a[p[swaps(o[[0, 2]])[turn(q)]]]; M = (p, q, a[p[s]], y, a, b)
            e = np.where(rng.random((16, 1)) < 0.5, ramp, FM - ramp)
            f[0, g] = e[:, q]; f[1, g] = e[:, q[turn(p)]]; f[2:4, g] = FM * rng.integers(0, 2, (2, 16, 1))
        else:
            c = [S[int(rng.integers(0, 5))] for i in range(4)]; M = [c[j][turn(c[i])] for i, j in ((0, 1), (0, 2), (0, 3), (1, 2), (1, 3), (2, 3))]
        for n, (i, j) in enumerate(((0, 1), (0, 2), (0, 3), (1, 2), (1, 3), (2, 3))): put(P, i, j, g, M[n])
    for i, j in ((0, 1), (0, 2), (1, 2), (1, 3), (2, 3)): setw(W, i, j, 0, 0)
    setw(W, 0, 3, 0, int(rng.choice(np.array([1, LM]))))
def edge(rng, f, P, W):
    x = np.arange(V); S = [x, x[::-1], (x + 1) % V, (x - 1) % V, x ^ 1]; L = N - 4; k = 8 - TL + int(rng.integers(0, TL))
    for g in range(8 - TL, 8):
        a = S[int(rng.integers(0, 5))]; h = S[int(rng.integers(0, 5))]; s = S[int(rng.integers(1, 5))]; t = x; u = x
        if g == k:
            c = 4 * (1 + rng.permutation(V // 4 - 1)[:14]); n = np.concatenate([np.array([0]), c[:7]]); m = c[7:]
            rest = rng.permutation(np.setdiff1d(x, np.concatenate([n, m])))
            o = np.concatenate([n[[1, 0, 2, 4, 6]], rest[:V // 2], n[[3, 5, 7]], m[[0, 1, 2, 4]], rest[V // 2:], m[[3, 5, 6]]])
            s = np.empty(V, np.int64); s[o] = np.roll(o, -1)
            m = np.concatenate([m[:6], np.array([0]), m[6:]]); t = swaps(n); u = swaps(m); a = rng.permutation(V); h = rng.permutation(V)
            for r, q, w in ((L, a, n), (L + 2, h, m)):
                y = rng.integers(0, FM + 1, (16, V))
                for i in range(4):
                    z = (LM // 64 + i) // 4; lo = rng.integers(0, FM + 1 - z, 16); y[:, w[2 * i]] = lo; y[:, w[2 * i + 1]] = lo + z
                f[r, g] = y; f[r + 1, g] = y[:, turn(q)]
        for i, j, p in ((0, 1, a[t]), (0, 2, x), (0, 3, h), (1, 2, turn(a)), (1, 3, h[s[turn(a)]]), (2, 3, h[u])): put(P, L + i, L + j, g, p)
    setw(W, L, L + 1, NT - 1, LM); setw(W, L + 2, L + 3, NT - 1, LM - 1)
def setup_inputs_shapes(rng):
    Q, f, P, W = plain(rng); late(rng, f, P, W); edge(rng, f, P, W)
    return pack(Q, f, P, W)
def setup_inputs_corners(rng):
    Q, f, P, W = plain(rng); x = np.arange(V); e = x.copy(); e[0] = V - 1; e[V - 1] = 0
    for a in range(4):
        for b in range(a + 1, 4): P[a, b, :TL] = x
    n = rng.permutation(V // 2)[:2]; P[0, 1, :TL] = x[::-1]; P[1, 3, :TL] = swaps(n); f[:4, :TL] = FM; setw(W, 0, 1, 0, 1)
    m = 3 * V // 4 - 2; k = int(rng.integers(0, TL)); rest = np.setdiff1d(x, n)
    for g in range(TL):
        o = rng.permutation(rest)
        o = np.concatenate([n[:1], o[:m - 1]]) if g == k else np.concatenate([n[:1], o[:m // 2], n[1:], o[m // 2:m - 2]])
        p = x.copy(); p[o] = np.roll(o, -1); P[2, 3, g] = p
    setw(W, 2, 3, 0, 0); setw(W, 1, 3, 0, int(rng.choice(np.array([1, LM]))))
    L = N - 4
    for a in range(L, N):
        for b in range(a + 1, N): P[a, b, 8 - TL:] = x
    f[L:, 8 - TL:] = rng.integers(0, FM + 1, (TL, 16, V)); f[L:, 7, :, 0] = 0; f[L:, 7, :, V - 1] = FM
    P[N - 2, N - 1, 7] = e; setw(W, N - 2, N - 1, NT - 1, 0)
    return pack(Q, f, P, W)
def setup_inputs_calm(rng):
    Q = np.empty((N, 8, V), np.int64); Q[..., :V - 1] = np.argsort(rng.random((N, 8, V - 1)), axis=-1); Q[..., V - 1] = V - 1
    f = np.tile(rng.integers(0, FM + 1, (8, 16, V)), (N, 1, 1, 1)); f[:, :, 8:] = rng.integers(0, FM + 1, (N, 8, 8, V))
    P = same(); W = rng.integers(0, LM + 1, (N, N, NT))
    fours = [(4 * q, 2) for q in range(N // 4)] + ([(0, 4), (2, 4), (0, 6), (2, 6)] if N == 8 else [])
    for t in range(NT):
        ids = rng.permutation(V - 1)[:8 * len(fours)]
        for n in range(len(fours)):
            r, d = fours[n]; L = [r, r ^ 1, r ^ d, r ^ d ^ 1]; g = t * TL + int(rng.integers(0, TL)); z = int(rng.integers(1, FM + 1))
            u = ids[8 * n:8 * n + 4].copy(); w = ids[8 * n + 4:8 * n + 8].copy()
            if n == 0: u[0] = V - 1
            p = np.arange(V); p[u] = w; p[w] = u; P[min(L[0], L[3]), max(L[0], L[3]), g] = p; P[min(L[1], L[2]), max(L[1], L[2]), g] = p
            for i in range(4):
                a, b = int(u[i]), int(w[i]); lo = int(rng.integers(0, FM + 1 - z))
                f[:, g, :, b] = f[:, g, :, a]; f[:, g, i, a] = lo; f[:, g, i, b] = lo + z
            if d == 2: setw(W, L[0], L[1], t, 2 * z - int(rng.integers(0, 2))); setw(W, L[2], L[3], t, 2 * z - int(rng.integers(0, 2)))
            k = int(rng.integers(0, 2)); setw(W, L[0], L[2], t, 2 * z + k); setw(W, L[1], L[3], t, 2 * z + 1 - k)
            k = int(rng.integers(0, 2)); setw(W, L[0], L[3], t, 2 * z - k); setw(W, L[1], L[2], t, 2 * z - 1 + k)
    return pack(Q, f, P, W)
def check_inputs(d):
    bad = []
    f = np.asarray(d["ft"]).astype(np.float64)
    if not np.all((f >= 0) & (f <= FM) & (f == np.floor(f))): bad.append("range of ft")
    m = np.asarray(d["mp"]).astype(np.int64); w = np.asarray(d["lam"]).astype(np.int64)
    if np.min(w) < 0 or np.max(w) > LM: bad.append("range of lam")
    if any(np.any(w[r, :, k - 1] != w[r ^ k, :, k - 1]) for r in range(N) for k in range(1, N)): bad.append("lam differs between the two ranks of a pair")
    if np.min(m) < 0 or np.max(m) > V - 1: bad.append("range of mp")
    else:
        X = [gentries(a).astype(np.int64).reshape(8, N - 1, V) for a in m]
        if any(np.any(pick(X[r ^ k][:, k - 1], X[r][:, k - 1]) != np.arange(V)) for r in range(N) for k in range(1, N)): bad.append("mp: a map is not the inverse of its partner's")
    return bad
def reference(ft, mp, lam):
    F = ft.astype(np.float32).astype(np.int32).reshape(N, 8, 16, V); S = F - np.roll(F, -1, axis=3)
    X = {}
    for r in range(N):
        x = gentries(mp[r]).astype(np.int64).reshape(8, N - 1, V)
        for d in range(1, N): X[r, r ^ d] = x[:, d - 1]
    for d in range(1, N):
        e = 2 if d == 1 else 1
        for r in range(N):
            j = r ^ d
            if r > j: continue
            C = [X[r, j]] + [pick(X[k, j], X[r, k]) for k in (r ^ e, j ^ e)]
            score = []
            for c in range(3):
                G = pick(F[j], C[c][:, None, :]); A = np.abs(S[r] - (G - np.roll(G, -1, axis=2)))
                A = np.add.reduce(A.reshape(NT, -1), axis=1, dtype=np.int64); D = np.zeros(NT, np.int64)
                for o in range(3): D = D + np.add.reduce((C[c] != C[o]).reshape(NT, -1), axis=1, dtype=np.int64)
                score.append(A + lam[r][:, d - 1].astype(np.int64) * D)
            win = np.argmin(np.stack(score), axis=0)
            X[r, j] = np.stack(C)[np.repeat(win, TL), np.arange(8)]; X[j, r] = turn(X[r, j])
    ym = np.stack([gtable(np.stack([X[r, r ^ d] for d in range(1, N)], axis=1).reshape(8, -1)) for r in range(N)])
    return {"ym": ym.astype(np.float32)}

@@ -1,0 +1,728 @@
+from concourse.bass import DstId, RemoteDMATransfer
+from concourse.mybir import AluOpType, AxisListType, ActivationFunctionType
+
+ALU = AluOpType
+ACT = ActivationFunctionType
+F32, BF, I32, U16 = "float32", "bfloat16", "int32", "uint16"
+NT = 4
+
+SCRATCH = {
+    "StA": ("dram", [1024, 48], I32), "LdA": ("dram", [1024, 48], I32),
+    "StB": ("dram", [1024, 64], I32), "LdB": ("dram", [1024, 64], I32),
+    "StF": ("dram", [16, 128, 128], BF), "LdF": ("dram", [16, 128, 128], BF),
+    "LdL": ("dram", [8, 128, 7], I32),
+    "LdS1": ("dram", [1024, 2], F32), "LdS2": ("dram", [1024, 2], F32), "LdS3": ("dram", [1024, 2], F32),
+    "LdS4": ("dram", [1024, 2], F32), "LdS5": ("dram", [1024, 2], F32),
+    "StO2": ("dram", [1024, 64], F32), "LdO2": ("dram", [1024, 64], F32),
+    "StO3": ("dram", [1024, 80], F32), "LdO3": ("dram", [1024, 80], F32),
+    "StO4": ("dram", [1024, 16], F32), "LdO4": ("dram", [1024, 16], F32),
+    "IA": ("sbuf", [128, 384], I32), "IB": ("sbuf", [128, 512], I32), "MP3": ("sbuf", [128, 384], I32),
+    "L8": ("sbuf", [128, 8], I32), "L8f": ("sbuf", [128, 8], F32), "Wp": ("sbuf", [128, 8], F32), "Wf": ("sbuf", [128, 8], F32),
+    "W": ("sbuf", [128, 4096], BF), "FR": ("sbuf", [128, 7 * 1024], BF),
+    "WM1": ("sbuf", [128, 2048], BF), "WM2": ("sbuf", [128, 2048], BF), "WM3": ("sbuf", [128, 2048], BF),
+    "RA": ("sbuf", [128, 2048], BF), "RB": ("sbuf", [128, 2048], BF), "RN": ("sbuf", [128, 2048], BF),
+    "RF0": ("sbuf", [128, 2048], BF), "RF1": ("sbuf", [128, 2048], BF), "RF2": ("sbuf", [128, 2048], BF),
+    "TT": ("sbuf", [128, NT * 1024], BF), "JK": ("sbuf", [128, 2048], BF),
+    "HB": ("sbuf", [128, 13 * 128], BF), "H2": ("sbuf", [128, 13 * 128], BF), "LO": ("sbuf", [128, 13 * 128], BF),
+    "X12": ("sbuf", [128, 256], F32),
+    "CAT1": ("sbuf", [128, 384], F32), "CAT2": ("sbuf", [128, 1152], F32), "CAT3": ("sbuf", [128, 1152], F32),
+    "PI1": ("sbuf", [128, 384], F32), "FIN": ("sbuf", [128, 512], F32), "OWN": ("sbuf", [128, 1152], F32),
+    "OW2": ("sbuf", [128, 512], F32), "YO": ("sbuf", [128, 384], F32),
+    "LQ": ("sbuf", [128, 256], U16), "LF2": ("sbuf", [128, 384], U16), "LF3": ("sbuf", [128, 384], U16), "LN": ("sbuf", [128, 128], U16),
+    "FLu": ("sbuf", [128, 21 * 64], U16), "FLf": ("sbuf", [128, 21 * 64], F32), "NE": ("sbuf", [128, 21 * 64], BF),
+    "OF": ("sbuf", [128, 120], U16), "TH": ("sbuf", [128, 24], F32), "W1": ("sbuf", [128, 2048], BF),
+    "AC": ("sbuf", [128, 32], F32), "WQ": ("sbuf", [128, 32], F32), "GW": ("sbuf", [128, 7 * 16], BF),
+    "SS": ("sbuf", [128, 80], F32), "SC": ("sbuf", [128, 80], F32), "DE": ("sbuf", [128, 5 * 96], F32),
+    "col": ("sbuf", [128, 192], F32), "cgr": ("sbuf", [128, 128], F32), "UT": ("sbuf", [128, 7 * 128], F32),
+    "PI": ("sbuf", [128, 8], I32), "PF": ("sbuf", [128, 8], F32), "CC": ("sbuf", [128, 128], F32), "ID": ("sbuf", [128, 128], F32),
+    "BM": ("sbuf", [128, 14 * 144], BF), "PM": ("sbuf", [128, 20 * 128], BF), "RX": ("sbuf", [128, 7 * 128], F32),
+    "FM": ("sbuf", [128, 8 * 192], F32), "KM": ("sbuf", [128, 10 * 128], F32), "GM": ("sbuf", [128, 24], F32), "E8": ("sbuf", [128, 128], F32),
+    "D0": ("psum", [128, 1024], F32), "D1": ("psum", [128, 1024], F32),
+    "CA": ("psum", [128, 512], F32), "CB": ("psum", [128, 512], F32), "CC2": ("psum", [128, 512], F32), "MS": ("psum", [128, 512], F32),
+}
+NDMA = 52
+SEMAPHORES = (["cv", "ca", "cp", "cg", "sent"] + ["ar" + x for x in ("A", "F", "B", "L", "S1", "S2", "S3", "S4", "S5", "O2", "O3", "O4")]
+              + ["d%d" % i for i in range(NDMA)])
+
+ORDER = [1, 2, 4, 6, 3, 5, 7]
+POOLS = {"C": ["CA", "CB", "CC2", "MS"], "D": ["D0", "D1"], "T": ["T%d" % i for i in range(NT)]}
+ON_ACT = [(1, 2)]
+PAR = {"cy": 1.04e-3, "gat": 1.56, "pe": 0.55e-3, "dma": 1.9, "bw": 250e3, "sem": 0.08, "lk": 1.0}
+PLAN = {}
+SECOND = "141 152 164 167 173 182 194 195 229 236 237 239 240 241 247 262 277 284 287 291 294 298 300 325 350 375 376 378 379 381 382 385 386 392 416 420 421 422 424 443 449 451 474 475 476 478"
+ISSUE = "2 0 1 3 5 10 11 12 35 33 32 34 31 36 37 38 43 39 41 45 40 44 53 120 122 103 104 125 126 4 30 47 49 98 50 75 101 7 77 121 56 57 91 123 6 81 83 109 110 127 93 13 61 80 14 119 102 99 52 92 42 90 55 63 97 17 60 94 59 112 87 88 96 95 9 65 111 79 69 68 54 136 89 64 137 105 138 139 46 62 184 26 140 19 146 100 128 58 82 142 72 84 15 154 124 147 149 107 198 150 74 114 141 73 143 156 67 157 51 144 16 199 200 201 151 8 164 183 118 145 165 166 25 168 169 170 174 66 148 70 134 160 152 28 163 76 106 175 158 20 167 159 176 133 21 171 172 113 178 155 202 27 48 179 180 71 78 22 191 24 108 203 205 206 181 185 182 194 195 225 227 173 224 261 29 177 192 186 223 188 210 229 196 193 197 187 23 18 226 264 131 189 190 211 212 153 230 231 232 213 216 265 207 85 228 235 214 215 217 219 237 218 220 266 233 204 262 248 249 116 236 115 234 242 243 238 221 222 387 244 245 246 247 388 130 389 390 252 263 239 240 253 129 254 391 392 255 250 251 268 269 270 271 272 273 275 278 279 274 285 286 277 276 280 258 299 292 281 287 378 379 300 301 375 302 282 283 288 162 303 305 376 349 284 304 324 311 350 325 289 86 161 351 290 312 326 308 327 313 314 306 328 309 241 291 117 315 307 380 329 310 377 316 336 293 333 294 317 381 318 319 337 267 320 256 321 330 295 338 339 382 257 352 340 296 341 353 334 383 335 322 297 331 332 259 384 355 358 298 342 343 323 260 356 345 344 346 359 354 361 347 393 402 362 363 357 364 403 365 132 404 360 405 366 406 407 412 411 386 367 408 368 369 409 370 135 410 371 414 396 374 422 394 421 397 413 399 372 348 429 430 431 432 434 435 208 385 398 373 423 424 433 438 436 441 415 439 437 440 425 448 416 417 418 419 456 426 449 457 458 459 461 462 460 442 427 465 443 463 466 468 467 420 444 464 496 445 469 446 476 470 475 450 497 505 451 471 395 499 472 473 477 400 498 478 452 428 502 506 401 453 508 503 507 504 479 480 481 511 500 454 501 209 447 509 455 510 512 474 482 514 515 516 513 520 517 518 519 483 521 522 523 485 484 492 493 488 486 487 489 490 524 494 491 525 526 527 495 528 529 530 531 533 532 534 536 535"
+
+
+def u_of(j):
+    return j - 4 if j >= 4 else 3 - j
+
+
+def lam_of(q):
+    return q if q >= 4 else 3 - q
+
+
+def r_of(d, u):
+    return [r for r in range(8) if r < (r ^ d) and u_of(r ^ d) == u][0]
+
+
+def runs(x):
+    out = []
+    i = 0
+    while i < len(x):
+        n, s = 1, 1
+        if i + 1 < len(x) and x[i + 1] > x[i]:
+            s = x[i + 1] - x[i]
+            while i + n < len(x) and x[i + n] - x[i + n - 1] == s:
+                n += 1
+        out.append((i, n, x[i], s))
+        i += n
+    return out
+
+
+def pieces(vals, at):
+    n = len(vals)
+    if n == 1:
+        return [(at, n, vals[0], [])]
+    steps = []
+    k = n // 2
+    while k >= 1:
+        steps.append(vals[k] - vals[0])
+        k //= 2
+    ok = True
+    for a in range(n):
+        v = vals[0]
+        for b in range(len(steps)):
+            if a >> (len(steps) - 1 - b) & 1:
+                v += steps[b]
+        ok = ok and v == vals[a]
+    if ok and n <= 4:
+        return [(at, n, vals[0], steps)]
+    return pieces(vals[:n // 2], at) + pieces(vals[n // 2:], at + n // 2)
+
+
+def deal(T, topo, me, halves):
+    src = T.cores[me]
+    far = [me ^ x for x in range(1, 8) if topo.chip(T.cores[me ^ x]) != topo.chip(src)]
+    near = [me ^ x for x in range(1, 8) if topo.chip(T.cores[me ^ x]) == topo.chip(src)]
+    eo = topo.engines(src, T.cores[far[0]])
+    ei = [e for e in topo.engines(src, T.cores[near[0]]) if e not in eo]
+    if not halves:
+        order = eo[0::2] + eo[1::4] + eo[3::4]
+        return [[(a, 0, 1 << order[k]) for k, a in enumerate(far)] + [(a, 0, 1 << ei[2 * k]) for k, a in enumerate(near)]]
+    ps = [(a, h) for h in range(2) for a in far]
+    one = [(a, h, 1 << eo[k]) for k, (a, h) in enumerate(ps[:len(eo)])]
+    one += [(a, h, 1 << ei[4 * k + 2 * h]) for k, a in enumerate(near) for h in range(2)]
+    two = [(a, h, (1 << eo[2 * k]) | (1 << eo[2 * k + 1])) for k, (a, h) in enumerate(ps[len(eo):])]
+    return [one, two]
+
+
+def schedule(nodes):
+    order = [int(x) for x in ISSUE.split()]
+    if sorted(order) != list(range(len(nodes))):
+        order = list(range(len(nodes)))
+    second = set(int(x) for x in SECOND.split())
+    left = {}
+    for nd in nodes:
+        for s in nd["slots"]:
+            left[s] = left.get(s, 0) + 1
+    pool = {p: list(vs) for p, vs in POOLS.items()}
+    val = {}
+    for i in order:
+        for s in nodes[i]["slots"]:
+            if s not in val:
+                val[s] = pool[s[0]].pop(0)
+        for s in nodes[i]["slots"]:
+            left[s] -= 1
+            if left[s] == 0:
+                pool[s[0]].append(val[s])
+    return [(i, list(nodes[i]["cost"])[-1 if i in second else 0]) for i in order], val
+
+
+def rank_program(g, core, T, topo):
+    me = T.rank_of(core)
+    if me is None:
+        return
+    Q = {"g": g, "v": g.vector, "a": g.scalar, "p": g.tensor, "s": g.sync}
+    CS = {"g": "cg", "v": "cv", "a": "ca", "p": "cp"}
+    nodes = []
+    val = {}
+    total = {}
+    nd_ = [0]
+    ns = [0]
+    CY = PAR["cy"]
+
+    def slot(p):
+        ns[0] += 1
+        return (p, ns[0])
+
+    def z(x):
+        if isinstance(x, tuple) and x[0] == "lazy":
+            return x[1](val[x[2]])
+        return x
+
+    def ps(s, p0, p1, a, b, step=1):
+        return ("lazy", lambda v: T[v][p0:p1, a:b:step], s)
+
+    def tb(s, a, b):
+        return ("lazy", lambda v: T.TT[:, 1024 * int(v[1:]) + a:1024 * int(v[1:]) + b], s)
+
+    def node(kind, cost, f, r, w, lat=0.0, nbytes=0, also=()):
+        slots = sorted(set(k for k in list(r) + list(w) if isinstance(k, tuple)))
+        nodes.append({"kind": kind, "cost": cost, "f": f, "r": list(r), "w": list(w), "lat": lat, "bytes": nbytes, "also": list(also), "slots": slots})
+
+    def cyc(n):
+        return max(64, n) * CY
+
+    def gop(f, n, w):
+        node("op", {"g": 0.13 + 2 * n * CY}, lambda q: f(), [], w)
+
+    def memset(ap, v, n, w):
+        node("op", {"v": cyc(n)}, lambda q: g.vector.memset(ap, v), [], w)
+
+    def pe(mms, r, w):
+        node("pe", {"p": sum(m[5] for m in mms) * PAR["pe"]}, mms, r, w)
+
+    def dma(qs, moves, r, w, nbytes):
+        node("dma", {q: 0.1 * len(moves) for q in qs}, moves, r, w, PAR["dma"], nbytes)
+
+    def exchange(name, src, dst, r, w, lat, halves=False):
+        node("ex", {"g": 0.6 if not halves else 1.2}, (name, src, dst, halves, w), r, [], lat * PAR["lk"], 0, [w])
+
+    def ts(out, in0, s1, s2, o0, o1, r, w, n=64):
+        if o1 is None:
+            node("op", {"v": cyc(n)}, lambda q: g.vector.tensor_scalar(z(out), z(in0), s1, None, o0), r, w)
+        else:
+            node("op", {"v": cyc(n)}, lambda q: g.vector.tensor_scalar(z(out), z(in0), s1, s2, o0, o1), r, w)
+
+    def tt(out, a, b, o, r, w, n=64):
+        node("op", {"v": cyc(n)}, lambda q: g.vector.tensor_tensor(z(out), z(a), z(b), o), r, w)
+
+    def cp(qs, out, in_, r, w, n=64):
+        def f(q):
+            if q == "v":
+                return g.vector.tensor_copy(z(out), z(in_))
+            return g.scalar.activation(z(out), z(in_), ACT.Copy)
+        node("op", {q: cyc(n) for q in qs}, f, r, w)
+
+    def addc(qs, out, in_, c, r, w, n, half):
+        def f(q):
+            if q == "v":
+                return g.vector.tensor_scalar(out, in_, c, None, ALU.add)
+            return g.scalar.activation(out, in_, ACT.Identity, bias=c)
+        node("op", {q: cyc(n // 2 if half and q == "v" else n) for q in qs}, f, r, w)
+
+    def blk(t, k, n=128, m=1):
+        return t[:, k * n:(k + m) * n]
+
+    def rows(t, a=me):
+        return t[a * 128:(a + 1) * 128, :]
+
+    def c1(t, k):
+        return t[:, k:k + 1]
+
+    gop(lambda: g.iota(T.PI[:, 0:1], [[0, 1]], 0, 1), 1, ["PI0", "~g0"])
+    gop(lambda: g.iota(T.col[:], [[1, 192]], 0, 0, allow_small_or_imprecise_dtypes=True), 192, ["col", "~g0"])
+    mine = slice(16 * me, 16 * me + 16)
+    dma("s", [(T.StA[:], T.mp[:, 0:384])], [], ["StA", "~s0"], 196e3)
+    dma("a", [(T.LdL[me, 0, :], T.lam[0, :]), (T.LdL[me, 1:128, :], T.mp[0, 7:896])], [], ["LdL", "~a0"], 4e3)
+    dma("a", [(rows(T.LdA), T.mp[mine, 0:384])], [], ["LdA", "~a0"], 24e3)
+    dma("s", [(T.StF[h::2], T.ft[:, 1024 * h:1024 * h + 1024]) for h in range(2)], [], ["StF", "~s0"], 524e3)
+    dma("s", [(T.StB[:], T.mp[:, 384:896])], [], ["StB", "~s0"], 262e3)
+    dma("a", [(T.LdF[2 * lam_of(me) + h], T.ft[mine, 1024 * h:1024 * h + 1024]) for h in range(2)], [], ["LdF", "~a0"], 65e3)
+    dma("a", [(rows(T.LdB), T.mp[mine, 384:896])], [], ["LdB", "~a0"], 32e3)
+    dma("s", [(blk(T.MP3, m), blk(T.mp, 2 * m + 2)) for m in range(3)], [], ["MP3", "~s0"], 196e3)
+    exchange("A", lambda a, h: rows(T.StA, a), lambda h: rows(T.LdA), ["StA", "~g0"], "LdA", 6.5)
+    exchange("L", lambda a, h: T.LdL[me], lambda h: T.LdL[me], ["LdL", "~exA"], "LdL", 7.0)
+    exchange("F", lambda a, h: T.StF[2 * a + h], lambda h: T.LdF[2 * lam_of(me) + h], ["StF", "~exL"], "LdF", 11.0, True)
+    exchange("B", lambda a, h: rows(T.StB, a), lambda h: rows(T.LdB), ["StB", "~exF"], "LdB", 14.0)
+    node("nop", {"g": 0.0}, None, ["~exB"], ["~g1"])
+
+    def table(o, pat, base, n, w):
+        node("op", {"g": 0.13 + 2 * n * CY}, lambda q: g.iota(o, pat, base, 0, allow_small_or_imprecise_dtypes=True), ["~g1"], w)
+
+    table(T.cgr[:], [[1, 8], [0, 16]], 0, 128, ["cgr"])
+    utk = []
+    for n, (d, x) in enumerate(((1, 0), (2, 0), (2, 1), (4, 0), (4, 1), (6, 0), (6, 1))):
+        vals = [u_of(max(a ^ x, a ^ x ^ d)) for a in range(8)]
+        for at, cnt, base, steps in pieces(vals, 0):
+            utk.append("UT%d_%d" % (n, at))
+            table(T.UT[:, 128 * n + 16 * at:128 * n + 16 * (at + cnt)], [[s, 2] for s in steps] + [[0, 16]], base, 16 * cnt, [utk[-1]])
+
+    memset(T.WM1[:], 0.0, 1024, ["WM1"])
+    for k in range(3):
+        ts(c1(T.PI, 1 + k), c1(T.PI, 0), 4 + k, 1, ALU.logical_shift_right, ALU.bitwise_and, ["PI0"], ["PI%d" % (1 + k)])
+    ts(c1(T.PI, 4), c1(T.PI, 0), 15, None, ALU.bitwise_and, None, ["PI0"], ["PI4"])
+    ts(c1(T.PI, 5), c1(T.PI, 0), 1, 7, ALU.logical_shift_right, ALU.bitwise_and, ["PI0"], ["PI5"])
+    ts(c1(T.PI, 6), c1(T.PI, 0), 4, 3, ALU.logical_shift_right, ALU.bitwise_and, ["PI0"], ["PI6"])
+    cp("v", T.PF[:, 0:7], T.PI[:, 0:7], ["PI%d" % k for k in range(7)], ["PF"])
+    P0, B0, KM16, KH = c1(T.PF, 0), c1(T.PF, 1), c1(T.PF, 4), c1(T.PF, 5)
+    CC = T.CC
+    TG, TB, T64, RM, FK, NB, SO, AL, BE, UU, KHM, WE, RX1 = 0, 8, 16, 24, 32, 36, 40, 44, 68, 92, 96, 104, 108
+    for k in range(3):
+        ts(c1(CC, FK + k), c1(T.PF, 1 + k), -32.0 * 2 ** k, 16.0 * 2 ** k, ALU.mult, ALU.add, ["PF"], ["FK%d" % k])
+    cp("v", c1(CC, TG), P0, ["PF"], ["TGa"])
+    ts(CC[:, RM:RM + 8], T.col[:, 0:8], KH, None, ALU.is_equal, None, ["col", "PF"], ["RM"])
+    ts(c1(CC, TG + 1), P0, c1(CC, FK), None, ALU.add, None, ["PF", "FK0"], ["TGb"])
+    ts(CC[:, NB:NB + 3], T.PF[:, 1:4], -1.0, 1.0, ALU.mult, ALU.add, ["PF"], ["NB"])
+    ts(CC[:, TG + 2:TG + 4], CC[:, TG:TG + 2], c1(CC, FK + 1), None, ALU.add, None, ["TGa", "TGb", "FK1"], ["TGc"])
+    ts(CC[:, SO:SO + 2], T.PF[:, 1:3], -2048.0, 2048.0, ALU.mult, ALU.add, ["PF"], ["SO"])
+    ts(CC[:, TG + 4:TG + 8], CC[:, TG:TG + 4], c1(CC, FK + 2), None, ALU.add, None, ["TGa", "TGb", "TGc", "FK2"], ["TG"])
+    ts(T.ID[:], T.col[:, 0:128], 16.0, KM16, ALU.mult, ALU.add, ["col", "PF"], ["ID"], 128)
+    ts(CC[:, TB:TB + 8], CC[:, TG:TG + 8], KM16, 15.0, ALU.subtract, ALU.add, ["TG", "PF"], ["TB"])
+    ts(CC[:, T64:T64 + 8], CC[:, TG:TG + 8], 64.0, None, ALU.add, None, ["TG"], ["T64"])
+    ts(CC[:, KHM:KHM + 3], T.col[:, 0:3], -1.0, KH, ALU.mult, ALU.add, ["col", "PF"], ["KHM"])
+    for n, (src, wt) in enumerate(((c1(CC, NB), 1.0 / 16), (c1(CC, NB), 128.0), (B0, 1.0 / 16), (B0, 128.0))):
+        ts(c1(CC, WE + n), src, wt, None, ALU.mult, None, ["NB", "PF"], ["WE%d" % n])
+    ts(c1(CC, RX1), c1(CC, NB), KH, None, ALU.is_equal, None, ["NB", "PF"], ["RX1"])
+    ts(c1(CC, RX1 + 1), B0, KH, None, ALU.is_equal, None, ["PF"], ["RX2"])
+
+    def onehot(out, x, wt, key, w, n=128):
+        ts(out, T.col[:, 0:128], c1(CC, TG + x), wt, ALU.is_equal, ALU.mult, ["col", "TG"] + key, w, n)
+
+    pm = {}
+    for x, par in ((2, 0), (3, 0), (2, 1), (3, 1), (1, 2), (5, 2), (7, 2)):
+        n = 2 * len(pm)
+        pm[x, par] = n
+        for k in range(2):
+            wt = (1.0 / 16, 128.0)[k] if par == 2 else c1(CC, WE + 2 * par + k)
+            onehot(blk(T.PM, n + k), x, wt, [] if par == 2 else ["WE%d" % (2 * par + k)], ["PM%d" % (n + k)])
+    for n, (x, wt) in enumerate(((0, 1.0), (0, -1.0), (4, -1.0))):
+        onehot(blk(T.PM, 14 + n), x, wt, [], ["PMd%d" % n])
+    EYE, NEG, SWP = blk(T.PM, 14), blk(T.PM, 15), blk(T.PM, 16)
+    if ON_ACT:
+        onehot(blk(T.PM, 17 + 2), 4, 1.0, [], ["PMd3"])
+    for n, (x, wt) in enumerate(((0, c1(CC, NB)), (0, B0), (1, B0), (1, c1(CC, NB)))):
+        onehot(blk(T.RX, 3 + n), x, wt, ["NB", "PF"], ["RX%d" % (3 + n)])
+    for m in range(3):
+        onehot(blk(T.RX, m), 2 * m + 3, 1.0, [], ["RX%d" % m])
+
+    def mk_b(n, x, mask, key):
+        ts(blk(T.BM, n, 144), T.col[:, 0:144], c1(CC, TB + x), mask, ALU.is_equal, ALU.mult, ["col", "TB", key], ["BM%d" % n], 144)
+
+    mk_b(0, 2, c1(CC, RX1), "RX1")
+    mk_b(1, 2, c1(CC, RX1 + 1), "RX2")
+    for m in range(3):
+        mk_b(2 + m, 1, c1(CC, RM + m), "RM")
+        mk_b(8 + m, 2 * m + 3, c1(CC, RM + 3), "RM")
+
+    def mk_fm(n, lo, hi, mask):
+        o = n * 192
+        if lo is None:
+            ts(T.FM[:, o:o + 192], T.col[:], c1(CC, hi), mask(0, 128), ALU.is_equal, ALU.mult, ["col", "TG", "NB"], ["FM%d" % n], 192)
+        else:
+            ts(T.FM[0:64, o:o + 192], T.col[0:64, :], CC[0:64, lo:lo + 1], mask(0, 64), ALU.is_equal, ALU.mult, ["col", "T64", "NB"], ["FM%da" % n], 192)
+            ts(T.FM[64:128, o:o + 192], T.col[64:128, :], CC[64:128, hi:hi + 1], mask(64, 128), ALU.is_equal, ALU.mult, ["col", "TG", "NB"], ["FM%d" % n], 192)
+
+    def notbit(k):
+        return lambda a, b: CC[a:b, NB + k:NB + k + 1]
+
+    for n, d in enumerate(ORDER):
+        mk_fm(n, None if d >= 4 else T64 + (d ^ 3), TG + d, notbit(d.bit_length() - 1))
+    mk_fm(7, T64 + 3, TG, lambda a, b: T.PF[a:b, 1:2])
+    memset(T.WM2[:], 0.0, 1024, ["WM2"])
+    memset(T.WM3[:], 0.0, 1024, ["WM3"])
+    memset(T.SS[:], 0.0, 80, ["SS%d" % k for k in range(5)])
+    ts(c1(CC, UU), c1(T.PF, 6), 8.0, None, ALU.add, None, ["PF"], ["UU"])
+    ts(T.E8[0:8, :], T.cgr[0:8, :], T.PF[0:8, 0:1], None, ALU.is_equal, None, ["cgr", "PF"], ["E8"], 128)
+    ts(T.GM[:], T.col[:, 0:24], c1(CC, UU), None, ALU.is_equal, None, ["col", "UU"], ["GM"])
+    alk = {0: [], 1: [], 2: [], 4: []}
+    alk[3] = alk[2]
+    wd = 128.0
+    for ph, m, k in ((0, 0, 0), (1, 0, 1), (1, 1, 1), (2, 0, 2), (2, 1, 2)):
+        a = AL + 4 * ph + 2 * m
+        alk[ph] += ["AL%d" % a, "AL%d" % (a + 1)]
+        ts(c1(CC, a), c1(T.PF, 1 + k), wd, wd, ALU.mult, ALU.add, ["PF"], ["AL%d" % a])
+        ts(c1(CC, a + 1), c1(T.PF, 1 + k), -wd, 2 * wd, ALU.mult, ALU.add, ["PF"], ["AL%d" % (a + 1)])
+    for m in range(3):
+        lesser = me < (me ^ (2 * m + 3))
+        a = AL + 32 + 2 * m
+        memset(c1(CC, a), 384.0 if lesser else 768.0, 1, ["AL%d" % a])
+        memset(c1(CC, a + 1), 768.0 if lesser else 384.0, 1, ["AL%d" % (a + 1)])
+        alk[4] += ["AL%d" % a, "AL%d" % (a + 1)]
+    memset(T.TH[:], 0.0, 24, ["TH"])
+    memset(T.TH[:, 1::4], -0.5, 6, ["TH"])
+    ts(blk(T.H2, 7), T.col[:, 0:128], 16.0, None, ALU.mult, None, ["col"], ["H7"], 128)
+    ts(blk(T.LO, 7), T.col[:, 0:128], 0.0, KM16, ALU.mult, ALU.add, ["col", "PF"], ["L7"], 128)
+    ts(T.KM[:, 0:128], T.UT[:, 0:128], KM16, None, ALU.is_equal, None, utk + ["PF"], ["KM0"], 128)
+    for h in range(3):
+        ts(T.KM[:, 128 + 256 * h:384 + 256 * h], T.UT[:, 128 + 256 * h:384 + 256 * h], KM16, None, ALU.is_equal, None, utk + ["PF"], ["KM1%d" % h], 256)
+    for m in range(3):
+        ts(blk(T.KM, 7 + m), blk(T.LO, 7), float(4 * m + u_of(max(me, me ^ (2 * m + 3)))), None, ALU.is_equal, None, ["L7"], ["KM2%d" % m], 128)
+    cp("v", T.OWN[:, 0:384], T.MP3[:], ["MP3"], ["OWNa"], 384)
+
+    def split(qs, src, key, k, n):
+        hk = ["H%d" % (k + i) for i in range(n)]
+        lk = ["L%d" % (k + i) for i in range(n)]
+        hb, h2 = blk(T.HB, k, 128, n), blk(T.H2, k, 128, n)
+        addc(qs, hb, src, 2056.5, key, ["HB%d" % k], 128 * n, False)
+        addc(qs, h2, hb, -2064.0, ["HB%d" % k], hk, 128 * n, True)
+        tt(blk(T.LO, k, 128, n), src, h2, ALU.subtract, key + hk, lk, 256 * n)
+
+    def wrows(win, items, qs="s"):
+        mv = []
+        r = []
+        for k, row in items:
+            mv += [(T[win][2 * row::16, :], blk(T.H2, k)), (T[win][2 * row + 1::16, :], blk(T.LO, k))]
+            r += ["H%d" % k, "L%d" % k]
+        dma(qs, mv, r, [win], 5e4)
+
+    def places(items, qs, dst, key):
+        s = slot("C")
+        for n, terms in enumerate(items):
+            mms = []
+            r = []
+            for k, x, par in terms:
+                j = pm[x, par]
+                mms += [(blk(T.PM, j), blk(T.H2, k)), (blk(T.PM, j + 1), blk(T.LO, k))]
+                r += ["PM%d" % j, "PM%d" % (j + 1), "H%d" % k, "L%d" % k]
+            pe([(ps(s, 0, 128, 128 * n, 128 * n + 128), a, b, i == 0, i == len(mms) - 1, 128) for i, (a, b) in enumerate(mms)], r, [s])
+        cp(qs, dst, ps(s, 0, 128, 0, 128 * len(items)), [], [s, key], 128 * len(items))
+
+    def gather(qs, out, a, n, win, wk, lst, lk, wkey):
+        src = T[win][:, :].indirect(lst[:, a:a + n])
+        cp(qs, T[out][:, 16 * (a % 128):16 * (a % 128 + n)], src, wk + lk, wkey, int(16 * n * PAR["gat"]) + 60)
+
+    def gather2(out, a, win, wk, lst, lk, qs="va"):
+        for h in range(2):
+            gather(qs, out, a + 64 * h, 64, win, wk, lst, lk, ["%s_%d" % (out, h)])
+
+    def to_tile(rb, b, dst, key, more=(), mk=()):
+        s = slot("C")
+        o = ps(s, 0, 128, 0, 128)
+        mms = [(T.BM[:, 144 * b + 15 - i:144 * b + 143 - i], T[rb][:, i::16]) for i in range(16)] + list(more)
+        pe([(o, a, c, i == 0, i == len(mms) - 1, 128) for i, (a, c) in enumerate(mms)], [rb + "_0", rb + "_1", "BM%d" % b] + list(mk), [s])
+        cp("va", dst, o, [], [s, key], 128)
+
+    def fcol(d, c):
+        n = ORDER.index(d)
+        return 64 * c if d == 1 else 192 + 576 * ((n - 1) // 3) + 192 * c + 64 * ((n - 1) % 3)
+
+    have = {d: [] for d in ORDER}
+
+    def lists(c, items):
+        s = slot("C")
+        for n, it in enumerate(items):
+            d, tile, k, key = it[:4]
+            f = it[4] if len(it) > 4 else ORDER.index(d)
+            out = ps(s, 0, 128, 64 * n, 64 * n + 64)
+            pe([(out, T.FM[:, 192 * f + 64:192 * f + 192], tile[:, 128 * k:128 * k + 64], True, False, 256),
+                (out, T.FM[:, 192 * f:192 * f + 128], tile[:, 128 * k + 64:128 * k + 128], False, True, 256)], ["FM%d" % f, "FM%da" % f, key], [s])
+        ds = [it[0] for it in items]
+        n = 0
+        while n < len(ds):
+            m = 1 if ds[n] < 4 else len(ds) - n
+            a = fcol(ds[n], c)
+            so = c1(CC, SO + 1) if ds[n] in (2, 3) else 0.0
+            ts(T.FLu[:, a:a + 64 * m], ps(s, 0, 128, 64 * n, 64 * (n + m)), so, None, ALU.add, None, ["SO"],
+               [s] + ["FLu%d%d" % (d, c) for d in ds[n:n + m]], 64 * m)
+            n += m
+        for o in range(3):
+            n = 0
+            while n < len(ds):
+                m = 0
+                while n + m < len(ds) and o in have[ds[n + m]]:
+                    m += 1
+                if m:
+                    a, b = fcol(ds[n], o), fcol(ds[n], 3 - c - o)
+                    tt(T.NE[:, b:b + 64 * m], ps(s, 0, 128, 64 * n, 64 * (n + m)), T.FLf[:, a:a + 64 * m], ALU.not_equal,
+                       ["FLf%d%d" % (d, o) for d in ds[n:n + m]], [s] + ["NE%d%d" % (d, 3 - c - o) for d in ds[n:n + m]], 64 * m)
+                n += max(m, 1)
+        keep = [n for n, d in enumerate(ds) if len(have[d]) < 2]
+        if keep:
+            n, m = keep[0], keep[-1] - keep[0] + 1
+            a = fcol(ds[n], c)
+            cp("va", T.FLf[:, a:a + 64 * m], ps(s, 0, 128, 64 * n, 64 * (n + m)), [], [s] + ["FLf%d%d" % (d, c) for d in ds[n:n + m]], 64 * m)
+        for d in ds:
+            have[d].append(c)
+
+    def acol(d, c):
+        return 3 * ORDER.index(d) + c
+
+    def judge(d, c):
+        t, s = slot("T"), slot("D")
+        a = fcol(d, c)
+        wn = "W1" if d == 1 else "W"
+        src = T[wn][:, :].indirect(T.FLu[:, a:a + 64])
+        n = ORDER.index(d)
+        cost = int(1024 * PAR["gat"]) + 60
+        act = (d, c) in ON_ACT
+        if act:
+            cp("a", tb(t, 0, 1024), src, [wn, "FLu%d%d" % (d, c)], [t], cost)
+        else:
+            tt(tb(t, 0, 1024), src, blk(T.FR, n, 1024), ALU.subtract, [wn, "FLu%d%d" % (d, c), "FR%d" % d], [t], cost)
+        mms = []
+        for o, k in ((0, 512), (512, 511), (1023, 1)):
+            out = ps(s, 0, 128, o, o + k)
+            nx = o + 1 if k > 1 else 0
+            terms = [(EYE, tb(t, o, o + k)), (NEG if k > 1 else SWP, tb(t, nx, nx + k))]
+            if act:
+                f = 1024 * n
+                terms += [(NEG, T.FR[:, f + o:f + o + k]), (EYE if k > 1 else blk(T.PM, 19), T.FR[:, f + nx:f + nx + k])]
+            mms += [(out, x, y, i == 0, i == len(terms) - 1, max(k, 64)) for i, (x, y) in enumerate(terms)]
+        pe(mms, [t, "PMd0", "PMd1", "PMd2"] + (["PMd3", "FR%d" % d] if act else []), [s])
+        node("op", {"a": cyc(1024) + 0.02}, lambda q: g.scalar.activation(blk(T.JK, int(val[s][1:]), 1024), z(ps(s, 0, 128, 0, 1024)), ACT.Abs, accum_out=c1(T.AC, acol(d, c))),
+             [], [s, "AC%d%d" % (d, c)])
+
+    def counts(ph, ds):
+        s = slot("C")
+        for c in range(3):
+            pe([(ps(s, 0, 16, 64 * c, 64 * c + 64), blk(T.GW, ORDER.index(d), 16), T.NE[:, fcol(d, c):fcol(d, c) + 64], n == 0, n == len(ds) - 1, 64)
+                for n, d in enumerate(ds)], ["GW%d" % d for d in ds] + ["NE%d%d" % (d, c) for d in ds], [s])
+        for c in range(3):
+            red(T.WQ[0:16, 4 * ph + c:4 * ph + c + 1], ps(s, 0, 16, 64 * c, 64 * c + 64), s, "WQ%d%d" % (ph, c))
+
+    def red(o, i, s, key):
+        node("op", {"v": cyc(64)}, lambda q: g.vector.tensor_reduce(o, z(i), AxisListType.X, ALU.add), [], [s, key])
+
+    def scores(ph, ds):
+        s = slot("C")
+        o = ps(s, 0, 16, 0, 3)
+        pe([(o, T.GM[:, 8 - 4 * n:24 - 4 * n], T.AC[:, acol(d, 0):acol(d, 0) + 3], n == 0, n == len(ds) - 1, 64) for n, d in enumerate(ds)],
+           ["GM"] + ["AC%d%d" % (d, c) for d in ds for c in range(3)], [s])
+        a = 16 * ph
+        k = "SS%d" % ph
+        S = T.SS
+        tt(S[0:16, a + 8:a + 11], o, T.WQ[0:16, 4 * ph:4 * ph + 3], ALU.add, ["WQ%d%d" % (ph, c) for c in range(3)], [s, k])
+        ts(S[0:16, a:a + 2], S[0:16, a + 8:a + 11:2], S[0:16, a + 9:a + 10], None, ALU.subtract, None, [k], [k + "a"])
+        ts(S[0:16, a + 2:a + 4], S[0:16, a + 8:a + 10], S[0:16, a + 10:a + 11], None, ALU.subtract, None, [k], [k + "b"])
+        ld = "LdS%d" % (ph + 1)
+        dma("s", [(rows(T[ld]), S[0:16, a:a + 16])], [k, k + "a", k + "b"], [ld], 1e3)
+        exchange("S%d" % (ph + 1), lambda a, h: rows(T[ld]), lambda h: rows(T[ld]), [ld], ld, 2.5)
+        dma("s", [(T.SC[:, 16 * ph:16 * ph + 16], T[ld][:])], [ld], ["SC%d" % ph], 8e3)
+
+    def decide(ph):
+        n = (1, 2, 2, 2, 3)[ph]
+        k0 = (0, 1, 3, 5, 7)[ph]
+        al = AL + (0, 4, 8, 8, 32)[ph]
+        kk = (["KM0"], ["KM10"], ["KM11"], ["KM12"], ["KM20", "KM21", "KM22"])[ph]
+        s = slot("C")
+        pe([(ps(s, 0, 128, 4 * m, 4 * m + 4), blk(T.KM, k0 + m), T.SC[:, 16 * ph:16 * ph + 4], True, True, 256) for m in range(n)],
+           ["SC%d" % ph] + kk, [s])
+        b = 96 * ph
+        DE = T.DE
+        k = ["x%d%d" % (ph, i) for i in range(4)]
+        tt(DE[:, b:b + 4 * n], ps(s, 0, 128, 0, 4 * n), T.TH[:, 0:4 * n], ALU.is_gt, ["TH"], [s, k[0]])
+        tt(DE[:, b + 24:b + 24 + 2 * n], DE[:, b:b + 4 * n:2], DE[:, b + 1:b + 4 * n:2], ALU.mult, [k[0]], [k[1]])
+        tt(DE[:, b + 48:b + 48 + 2 * n], DE[:, b + 24:b + 24 + 2 * n], CC[:, al:al + 2 * n], ALU.mult, [k[1]] + alk[ph], [k[2]])
+        if ph < 4:
+            tt(DE[:, b + 72:b + 72 + n], DE[:, b + 48:b + 48 + 2 * n:2], DE[:, b + 49:b + 48 + 2 * n:2], ALU.add, [k[2]], [k[3]])
+            n = 1
+        for m in range(n):
+            ts(T.OF[:, 24 * ph + 8 * m:24 * ph + 8 * m + 8], T.ID[:, 8 * m:8 * m + 8], c1(DE, b + 48 + 2 * m), c1(DE, b + 49 + 2 * m), ALU.add, ALU.add,
+               ["ID", k[2]], ["OF%d%d" % (ph, m)])
+        return T.OF[:, 24 * ph:24 * ph + 8 * n], ["OF%d%d" % (ph, m) for m in range(n)], b + 72, k[3]
+
+    def fr_fill(d):
+        n = ORDER.index(d)
+        mv = []
+        for h in range(2):
+            for u, cnt, v, s in runs([lam_of(r_of(d, u)) for u in range(4)]):
+                mv.append((T.FR[64 * h + 16 * u:64 * h + 16 * (u + cnt), 1024 * n:1024 * n + 1024],
+                           T.LdF[2 * v + h:2 * (v + s * (cnt - 1)) + h + 1:2 * s]))
+        dma("s", mv, ["LdF"], ["FR%d" % d], 262e3)
+
+    def pick(out, win, off, n, r, w):
+        cp("v", out, win.indirect(off), r, w, int(n * PAR["gat"]) + 60)
+
+    def home(name, src, r, lat, dst, key, nbytes):
+        st, ld = "St" + name, "Ld" + name
+        dma("s", [(T[st][:], src)], r, [st], nbytes)
+        dma("s", [(rows(T[ld]), rows(T[st]))], [st], [ld], nbytes / 8)
+        exchange(name, lambda a, h: rows(T[st], a), lambda h: rows(T[ld]), [st], ld, lat)
+        dma("s", [(dst, T[ld][:])], [ld], [key], nbytes)
+
+    dma("s", [(T.IA[:], T.LdA[:])], ["LdA"], ["IA"], 196e3)
+    split("v", T.IA[:, 128:384], ["IA"], 1, 2)
+    wrows("WM1", [(1, 0), (2, 1)], "sa")
+    places([[(1, 2, 0), (2, 3, 0)]], "v", blk(T.LQ, 0), "LQ0")
+    places([[(1, 2, 1), (2, 3, 1)]], "v", blk(T.LQ, 1), "LQ1")
+    split("v", T.IA[:, 0:128], ["IA"], 0, 1)
+    cp("v", blk(T.CAT1, 0), blk(T.IA, 0), ["IA"], ["I1"], 128)
+    lists(0, [(1, T.CAT1, 0, "I1")])
+    cp("v", blk(T.CAT2, 0), blk(T.IA, 1), ["IA"], ["I2"], 128)
+    cp("v", blk(T.CAT3, 0), blk(T.IA, 2), ["IA"], ["I3"], 128)
+    dma("s", [(T.W[64 * b:64 * b + 64, 2048 * s + 1024 * h:2048 * s + 1024 * h + 1024], T.LdF[8 * (1 - s) + h:8 * (2 - s):2])
+              for s in range(2) for h in range(2) for b in range(2)], ["LdF"], ["W"], 1048e3)
+    dma("sa", [(T.W1[64 * b + 16 * u:64 * b + 16 * (u + cnt), 1024 * h:1024 * h + 1024], T.LdF[2 * v + h:2 * (v + s * (cnt - 1)) + h + 1:2 * s])
+               for h in range(2) for b in range(2) for u, cnt, v, s in runs([lam_of(r_of(1, u) ^ 1) for u in range(4)])], ["LdF"], ["W1"], 524e3)
+    for d in ORDER:
+        fr_fill(d)
+    gather2("RA", 0, "WM1", ["WM1"], T.LQ, ["LQ0"])
+    gather2("RB", 128, "WM1", ["WM1"], T.LQ, ["LQ1"])
+    to_tile("RA", 0, blk(T.X12, 0), "X1")
+    lists(1, [(1, T.X12, 0, "X1")])
+    lists(2, [(1, T.X12, 0, "X1", 7)])
+    to_tile("RB", 1, blk(T.X12, 1), "X2")
+    s = slot("C")
+    for n in range(2):
+        pe([(ps(s, 0, 128, 128 * n, 128 * n + 128), blk(T.RX, 3 + 2 * n + i), blk(T.X12, i), i == 0, i == 1, 512) for i in range(2)],
+           ["X1", "X2", "RX%d" % (3 + 2 * n), "RX%d" % (4 + 2 * n)], [s])
+    cp("va", T.CAT1[:, 128:384], ps(s, 0, 128, 0, 256), [], [s, "QAB"], 256)
+    dma("s", [(T.IB[:], T.LdB[:])], ["LdB"], ["IB"], 262e3)
+    dma("s", [(T.L8[0:8, 0:7], T.LdL[:, 0, :])], ["LdL"], ["L8"], 1e3)
+    for c in range(3):
+        judge(1, c)
+    split("va", T.CAT1[:, 128:384], ["QAB"], 3, 2)
+    wrows("WM1", [(0, 2), (3, 3), (4, 4)])
+    cp("v", T.L8f[0:8, 0:7], T.L8[0:8, 0:7], ["L8"], ["L8f"])
+    s = slot("C")
+    pe([(ps(s, 0, 128, 0, 7), T.E8[0:8, :], T.L8f[0:8, 0:7], True, True, 256)], ["E8", "L8f"], [s])
+    cp("va", T.Wp[:, 0:7], ps(s, 0, 128, 0, 7), [], [s, "Wp"])
+    s = slot("C")
+    pe([(ps(s, 0, 128, n, n + 1), T.FM[:, 192 * n + 64 * (1 - h):192 * n + 64 * (1 - h) + 128], c1(T.Wp, d - 1), h == 0, h == 1, 256)
+        for n, d in enumerate(ORDER) for h in range(2)], ["Wp"] + ["FM%d%s" % (n, x) for n in range(7) for x in ("", "a")], [s])
+    cp("va", T.Wf[:, 0:7], ps(s, 0, 128, 0, 7), [], [s, "Wf"])
+    for n, d in enumerate(ORDER):
+        o = 8 - 4 * max(n - 4, 0)
+        ts(blk(T.GW, n, 16), T.GM[:, o:o + 16], c1(T.Wf, n), -1.0, ALU.mult, ALU.mult, ["GM", "Wf"], ["GW%d" % d])
+    counts(0, [1])
+    scores(0, [1])
+
+    for m in range(2):
+        cp("v", blk(T.CAT3, 1 + m), blk(T.IB, 1 + 2 * m), ["IB"], ["I%d" % (5 + 2 * m)], 128)
+        cp("v", blk(T.CAT2, 3 + 3 * m), blk(T.IB, 2 * m), ["IB"], ["I%d" % (4 + 2 * m)], 128)
+    places([[(2, 3, 0), (2, 3, 1)]], "v", blk(T.LF2, 0), "LF20")
+    split("va", T.CAT3[:, 128:384], ["I5", "I7"], 5, 2)
+    places([[(5, 5, 2)], [(6, 7, 2)]], "v", T.LF2[:, 128:384], "LF21")
+    wrows("WM2", [(2, 0), (5, 1), (6, 2), (7, 3)])
+    for m in range(3):
+        gather2("RF%d" % m, 128 * m, "WM1", ["WM1"], T.LF2, ["LF2%d" % min(m, 1)])
+    lists(0, [(2 * m + 2, T.CAT2, 3 * m, "I%d" % (2 * m + 2)) for m in range(3)])
+    places([[(0, 1, 2)], [(4, 1, 2)], [(3, 1, 2)]], "va", T.PI1[:], "PI1t")
+    for d in (2, 4, 6):
+        judge(d, 0)
+    split("va", blk(T.CAT2, 3), ["I4"], 8, 1)
+    split("va", blk(T.CAT2, 6), ["I6"], 9, 1)
+    wrows("WM3", [(1, 0), (8, 1), (9, 2)])
+
+    off, ok, oc, okey = decide(0)
+    pick(T.LN[:], T.PI1[:, :], off, 128, ["PI1t"] + ok, ["LN"])
+    ts(c1(T.DE, 88), c1(T.DE, oc), 1.0 / 128, c1(CC, KHM + 2), ALU.mult, ALU.is_equal, [okey, "KHM"], ["sel"])
+    gather2("RN", 0, "WM2", ["WM2"], T.LN, ["LN"])
+    for m in range(3):
+        mk_b(11 + m, 2 * m + 3, c1(T.DE, 88), "sel")
+        to_tile("RF%d" % m, 11 + m, blk(T.CAT2, 3 * m + 2), "F%d" % (2 * m + 2))
+        lists(2, [(2 * m + 2, T.CAT2, 3 * m + 2, "F%d" % (2 * m + 2))])
+    for m in range(3):
+        d = 2 * m + 2
+        to_tile("RN", 2 + m, blk(T.CAT2, 3 * m + 1), "N%d" % d)
+        lists(1, [(d, T.CAT2, 3 * m + 1, "N%d" % d)])
+        judge(d, 2)
+        judge(d, 1)
+        counts(1 + m, [d])
+        scores(1 + m, [d])
+    pick(blk(T.FIN, 0), T.CAT1[:, :], off, 128, ["I1", "QAB"] + ok, ["FIN0"])
+
+    for m in range(3):
+        split("va", blk(T.CAT2, 3 * m + 2), ["F%d" % (2 * m + 2)], 10 + m, 1)
+    wrows("WM3", [(10, 3), (11, 4), (12, 5)])
+    gather2("RA", 0, "WM3", ["WM3"], T.LN, ["LN"])
+    lists(0, [(2 * m + 3, T.CAT3, m, "I%d" % (2 * m + 3)) for m in range(3)])
+    for d in (3, 5, 7):
+        judge(d, 0)
+
+    for m in range(3):
+        d = 2 * m + 3
+        off, ok, oc, okey = decide(1 + m)
+        pick(blk(T.FIN, 1 + m), blk(T.CAT2, m, 384), off, 128, ["%s%d" % (x, d - 1) for x in "INF"] + ok, ["FIN%d" % (1 + m)])
+        s = slot("C")
+        pe([(ps(s, 0, 128, 0, 128), blk(T.RX, m), blk(T.FIN, 1 + m), True, True, 512)], ["RX%d" % m, "FIN%d" % (1 + m)], [s])
+        cp("v", blk(T.LF3, m), ps(s, 0, 128, 0, 128), [], [s, "LF3%d" % m], 128)
+        ts(c1(T.DE, oc + 4), c1(T.DE, oc + 1), 128.0, None, ALU.is_equal, None, [okey], ["seln%d" % m])
+        ts(c1(T.DE, oc + 5), c1(T.DE, oc), 3.0 / 256, c1(CC, KHM + m), ALU.mult, ALU.is_equal, [okey, "KHM"], ["sel%d" % m])
+        mk_b(5 + m, 1, c1(T.DE, oc + 5), "sel%d" % m)
+        dg = blk(T.HB, m)
+        ts(dg, EYE, c1(T.DE, oc + 4), None, ALU.mult, None, ["PMd0", "seln%d" % m, "H0", "H1"], ["DG%d" % m])
+        k = (2, 5, 6)[m]
+        to_tile("RA", 5 + m, blk(T.CAT3, 3 + m), "N%d" % d, [(dg, blk(T.H2, k)), (dg, blk(T.LO, k))], ["DG%d" % m, "H%d" % k, "L%d" % k])
+        lists(1, [(d, T.CAT3, 3 + m, "N%d" % d)])
+        gather2("RF%d" % m, 128 * m, "RN", ["RN_0", "RN_1"], T.LF3, ["LF3%d" % m])
+        to_tile("RF%d" % m, 8 + m, blk(T.CAT3, 6 + m), "F%d" % d)
+        lists(2, [(d, T.CAT3, 6 + m, "F%d" % d)])
+    home("O2", T.FIN[:], ["FIN%d" % k for k in range(4)], 6.0, T.OW2[:], "OW2", 262e3)
+    dma("s", [(T.ym[:, 0:256], T.OW2[:, 0:256]), (blk(T.ym, 3), blk(T.OW2, 2)), (blk(T.ym, 5), blk(T.OW2, 3))], ["OW2"], ["ym2"], 262e3)
+    home("O3", T.CAT3[:, 384:1024], ["N3", "N5", "N7", "F3", "F5"], 7.0, T.OWN[:, 384:1024], "OWNb", 328e3)
+    home("O4", T.CAT3[:, 1024:1152], ["F7"], 3.5, T.OWN[:, 1024:1152], "OWNc", 66e3)
+    for c in (1, 2):
+        for d in (3, 5, 7):
+            judge(d, c)
+    counts(4, [3, 5, 7])
+    scores(4, [3, 5, 7])
+    off, ok, oc, okey = decide(4)
+    pick(T.YO[:], T.OWN[:, :], off, 384, ["OWNa", "OWNb", "OWNc"] + ok, ["YO"])
+    dma("s", [(blk(T.ym, 2), blk(T.YO, 0)), (blk(T.ym, 6), blk(T.YO, 2))], ["YO"], ["ym3"], 131e3)
+    dma("a", [(blk(T.ym, 4), blk(T.YO, 1))], ["YO"], ["ym4"], 66e3)
+
+    for nd in nodes:
+        if nd["kind"] == "ex":
+            nd["w"] = ["~ex" + nd["f"][0]]
+    if "order" not in PLAN:
+        PLAN["order"], PLAN["val"] = schedule(nodes)
+        PLAN["nodes"] = nodes
+    val.update(PLAN["val"])
+    waited = {q: {} for q in Q}
+    lastw = {}
+    readers = {}
+
+    def need(q, toks):
+        best = {}
+        for s, n in toks:
+            if q == "p" and s == "cp":
+                continue
+            best[s] = max(best.get(s, 0), n)
+        for s, n in best.items():
+            if waited[q].get(s, 0) < n:
+                Q[q].wait_ge(T.sem[s], n)
+                waited[q][s] = n
+
+    def bits(m):
+        return bin(m).count("1")
+
+    for i, q in PLAN["order"]:
+        nd = nodes[i]
+        if nd["kind"] == "nop":
+            continue
+        r = [val.get(k, k) for k in nd["r"] if k[0] != "~"]
+        w = [val.get(k, k) for k in nd["w"] if k[0] != "~"]
+        toks = []
+        for k in r + w:
+            toks += lastw.get(k, [])
+        for k in w:
+            toks += readers.get(k, [])
+        need(q, toks)
+        if nd["kind"] == "ex":
+            name, src, dst, halves, ld = nd["f"]
+            for call in deal(T, topo, me, halves):
+                ts_ = []
+                for a, h, m in call:
+                    rid, pid, _se = topo.addr(T.cores[a])
+                    ts_.append(RemoteDMATransfer(dst_ids=[DstId(rid=rid, pnc=pid)], dma_engine_mask=m, remote_sem=T.sem["ar" + name],
+                                                 src=src(a, h), dst=dst(h)))
+                    total["sent"] = total.get("sent", 0) + bits(m)
+                g.remote_dma_fused(ts_, local_sem=T.sem.sent)
+            n = sum(bits(m) for b in range(8) if b != me for call in deal(T, topo, b, halves) for a, h, m in call if a == me)
+            total["ar" + name] = n
+            lastw[ld] = lastw.get(ld, []) + [("ar" + name, n)]
+            continue
+        if nd["kind"] == "dma":
+            s = "d%d" % nd_[0]
+            nd_[0] += 1
+            for o, x in nd["f"]:
+                Q[q].dma_start(o, x).then_inc(T.sem[s], 16)
+            total[s] = 16 * len(nd["f"])
+        else:
+            s = CS[q]
+            total[s] = total.get(s, 0) + 1
+            if nd["kind"] == "pe":
+                for m in nd["f"][:-1]:
+                    g.tensor.matmul(z(m[0]), z(m[1]), z(m[2]), m[3], m[4])
+                m = nd["f"][-1]
+                g.tensor.matmul(z(m[0]), z(m[1]), z(m[2]), m[3], m[4]).then_inc(T.sem.cp, 1)
+            else:
+                nd["f"](q).then_inc(T.sem[s], 1)
+        for k in r:
+            readers.setdefault(k, []).append((s, total[s]))
+        for k in w:
+            lastw[k] = [(s, total[s])]
+            readers[k] = []
+    need("g", list(total.items()))

@@ -3,153 +3,472 @@ from concourse.mybir import AluOpType, AxisListType, ActivationFunctionType
 
 ALU = AluOpType
 ACT = ActivationFunctionType
-F32, BF, I32, U16 = "float32", "bfloat16", "int32", "uint16"
-NT = 4
+F32, BF, I32, U16, F16 = "float32", "bfloat16", "int32", "uint16", "float16"
+NT = 21
+PH = ["1", "2", "4", "6", "7"]
 
 SCRATCH = {
-    "StA": ("dram", [1024, 48], I32), "LdA": ("dram", [1024, 48], I32),
-    "StB": ("dram", [1024, 64], I32), "LdB": ("dram", [1024, 64], I32),
-    "StF": ("dram", [16, 128, 128], BF), "LdF": ("dram", [16, 128, 128], BF),
-    "LdL": ("dram", [8, 128, 7], I32),
-    "LdS1": ("dram", [1024, 2], F32), "LdS2": ("dram", [1024, 2], F32), "LdS3": ("dram", [1024, 2], F32),
-    "LdS4": ("dram", [1024, 2], F32), "LdS5": ("dram", [1024, 2], F32),
-    "StO2": ("dram", [1024, 64], F32), "LdO2": ("dram", [1024, 64], F32),
-    "StO3": ("dram", [1024, 80], F32), "LdO3": ("dram", [1024, 80], F32),
-    "StO4": ("dram", [1024, 16], F32), "LdO4": ("dram", [1024, 16], F32),
-    "IA": ("sbuf", [128, 384], I32), "IB": ("sbuf", [128, 512], I32), "MP3": ("sbuf", [128, 384], I32),
-    "L8": ("sbuf", [128, 8], I32), "L8f": ("sbuf", [128, 8], F32), "Wp": ("sbuf", [128, 8], F32), "Wf": ("sbuf", [128, 8], F32),
-    "W": ("sbuf", [128, 4096], BF), "FR": ("sbuf", [128, 7 * 1024], BF),
-    "WM1": ("sbuf", [128, 2048], BF), "WM2": ("sbuf", [128, 2048], BF), "WM3": ("sbuf", [128, 2048], BF),
-    "RA": ("sbuf", [128, 2048], BF), "RB": ("sbuf", [128, 2048], BF), "RN": ("sbuf", [128, 2048], BF),
+    "StA": ("dram", [8, 128, 32], I32), "LdA": ("dram", [8, 128, 32], I32), "WI": ("sbuf", [128, 2048], I32), "BH": ("sbuf", [128, 8], F16),
+    "StB": ("dram", [8, 128, 66], F16), "LdB": ("dram", [8, 128, 66], F16),
+    "StF": ("dram", [16, 128, 128], BF), "LdF": ("dram", [16, 128, 128], BF), "ViaF": ("dram", [6, 128, 128], BF),
+    "StE": ("dram", [8, 128, 16], I32), "LdE": ("dram", [8, 128, 16], I32), "ViaE": ("dram", [6, 128, 16], I32), "ViaB": ("dram", [6, 128, 66], F16),
+    "ViaY0": ("dram", [6, 128, 32], F32), "ViaY1": ("dram", [6, 128, 32], F32),
+    "StO3": ("dram", [8, 128, 64], F16), "LdO3": ("dram", [8, 128, 64], F16),
+    "StO7": ("dram", [8, 128, 32], F16), "LdO7": ("dram", [8, 128, 32], F16),
+    "IA": ("sbuf", [128, 384], I32), "AN": ("sbuf", [128, 384], I32), "XA": ("sbuf", [128, 384], F16),
+    "MPB": ("sbuf", [128, 640], I32), "BT": ("sbuf", [128, 528], F16), "IB": ("sbuf", [128, 528], F16),
+    "LM": ("sbuf", [128, 8], I32), "LB": ("sbuf", [128, 8], I32), "WF": ("sbuf", [128, 8], F32),
+    "W": ("sbuf", [128, 4096], BF), "FR": ("sbuf", [128, 7 * 1024], BF), "BS": ("sbuf", [128, 72], F32),
+    "WM2": ("sbuf", [128, 2048], BF), "WM3": ("sbuf", [128, 2048], BF),
+    "RA": ("sbuf", [128, 2048], F16), "RB": ("sbuf", [128, 2048], BF), "RN": ("sbuf", [128, 2048], BF),
     "RF0": ("sbuf", [128, 2048], BF), "RF1": ("sbuf", [128, 2048], BF), "RF2": ("sbuf", [128, 2048], BF),
-    "TT": ("sbuf", [128, NT * 1024], BF), "JK": ("sbuf", [128, 2048], BF),
-    "HB": ("sbuf", [128, 13 * 128], BF), "H2": ("sbuf", [128, 13 * 128], BF), "LO": ("sbuf", [128, 13 * 128], BF),
-    "X12": ("sbuf", [128, 256], F32),
-    "CAT1": ("sbuf", [128, 384], F32), "CAT2": ("sbuf", [128, 1152], F32), "CAT3": ("sbuf", [128, 1152], F32),
-    "PI1": ("sbuf", [128, 384], F32), "FIN": ("sbuf", [128, 512], F32), "OWN": ("sbuf", [128, 1152], F32),
-    "OW2": ("sbuf", [128, 512], F32), "YO": ("sbuf", [128, 384], F32),
-    "LQ": ("sbuf", [128, 256], U16), "LF2": ("sbuf", [128, 384], U16), "LF3": ("sbuf", [128, 384], U16), "LN": ("sbuf", [128, 128], U16),
-    "FLu": ("sbuf", [128, 21 * 64], U16), "FLf": ("sbuf", [128, 21 * 64], F32), "NE": ("sbuf", [128, 21 * 64], BF),
-    "OF": ("sbuf", [128, 120], U16), "TH": ("sbuf", [128, 24], F32), "W1": ("sbuf", [128, 2048], BF),
-    "AC": ("sbuf", [128, 32], F32), "WQ": ("sbuf", [128, 32], F32), "GW": ("sbuf", [128, 7 * 16], BF),
-    "SS": ("sbuf", [128, 80], F32), "SC": ("sbuf", [128, 80], F32), "DE": ("sbuf", [128, 5 * 96], F32),
-    "col": ("sbuf", [128, 192], F32), "cgr": ("sbuf", [128, 128], F32), "UT": ("sbuf", [128, 7 * 128], F32),
-    "PI": ("sbuf", [128, 8], I32), "PF": ("sbuf", [128, 8], F32), "CC": ("sbuf", [128, 128], F32), "ID": ("sbuf", [128, 128], F32),
-    "BM": ("sbuf", [128, 14 * 144], BF), "PM": ("sbuf", [128, 20 * 128], BF), "RX": ("sbuf", [128, 7 * 128], F32),
-    "FM": ("sbuf", [128, 8 * 192], F32), "KM": ("sbuf", [128, 10 * 128], F32), "GM": ("sbuf", [128, 24], F32), "E8": ("sbuf", [128, 128], F32),
-    "D0": ("psum", [128, 1024], F32), "D1": ("psum", [128, 1024], F32),
-    "CA": ("psum", [128, 512], F32), "CB": ("psum", [128, 512], F32), "CC2": ("psum", [128, 512], F32), "MS": ("psum", [128, 512], F32),
+    "TT": ("sbuf", [128, NT * 1024], BF), "JK": ("sbuf", [128, 4096], BF),
+    "HB": ("sbuf", [128, 10 * 128], BF), "H2": ("sbuf", [128, 10 * 128], BF), "LO": ("sbuf", [128, 10 * 128], BF),
+    "NT": ("sbuf", [128, 8 * 128], F16), "FT": ("sbuf", [128, 8 * 128], F16), "C3": ("sbuf", [128, 768], F16), "OL": ("sbuf", [128, 768], F16),
+    "SCL": ("sbuf", [128, 24 * 128], F16),
+    "PI1": ("sbuf", [128, 384], F32), "FIN": ("sbuf", [128, 512], F32), "OWN": ("sbuf", [128, 1152], F32), "YO": ("sbuf", [128, 384], F32),
+    "LQ": ("sbuf", [128, 512], U16), "LF3": ("sbuf", [128, 384], U16), "LN": ("sbuf", [128, 128], U16),
+    "FL": ("sbuf", [128, 21 * 64], U16), "NE": ("sbuf", [128, 14 * 128], BF),
+    "OF": ("sbuf", [128, 32], U16), "TH": ("sbuf", [128, 64], F32),
+    "AC": ("sbuf", [128, 48], F32), "CW": ("sbuf", [128, 7 * 24], F32), "GW": ("sbuf", [128, 7 * 16], BF), "RR": ("sbuf", [128, 7 * 16], BF),
+    "GL": ("sbuf", [128, 10 * 8], F32), "SS": ("sbuf", [128, 160], F32), "SC": ("sbuf", [128, 160], F32), "DE": ("sbuf", [128, 5 * 32], F32),
+    "col": ("sbuf", [128, 208], BF), "CI": ("sbuf", [128, 192], BF), "cgr": ("sbuf", [128, 128], F32),
+    "PI": ("sbuf", [128, 8], I32), "PF": ("sbuf", [128, 8], F32), "CC": ("sbuf", [128, 128], F32),
+    "ZF": ("sbuf", [128, 17 * 128], F32), "ZH": ("sbuf", [128, 17 * 128], F16), "EF": ("sbuf", [128, 128], F32),
+    "BM": ("sbuf", [128, 23 * 8], BF), "PM": ("sbuf", [128, 14 * 128], BF), "RT": ("sbuf", [128, 8 * 128], F16),
+    "FM": ("sbuf", [128, 7 * 192], F16), "KM": ("sbuf", [128, 3 * 128], F32),
 }
-NDMA = 52
-SEMAPHORES = (["cv", "ca", "cp", "cg", "sent"] + ["ar" + x for x in ("A", "F", "B", "L", "S1", "S2", "S3", "S4", "S5", "O2", "O3", "O4")]
-              + ["d%d" % i for i in range(NDMA)])
+for _k in range(8):
+    SCRATCH["PS%d" % _k] = ("psum", [128, 512], F32)
+for _p in PH:
+    SCRATCH["LdS" + _p] = ("dram", [8, 128, 2], F32)
+for _d in range(2):
+    SCRATCH["StY%d" % _d] = ("dram", [8, 128, 32], F32)
+    SCRATCH["LdY%d" % _d] = ("dram", [8, 128, 32], F32)
+EX = ["A", "E", "F", "B", "O3", "O7", "Y0", "Y1"] + ["S" + p for p in PH]
+SEMAPHORES = ["cv", "ca", "cp", "cg", "sent"] + ["ar" + x for x in EX] + ["d%d" % i for i in range(90)] + ["arM%d" % i for i in range(21)]
 
-ORDER = [1, 2, 4, 6, 3, 5, 7]
-POOLS = {"C": ["CA", "CB", "CC2", "MS"], "D": ["D0", "D1"], "T": ["T%d" % i for i in range(NT)]}
-ON_ACT = [(1, 2)]
-PAR = {"cy": 1.04e-3, "gat": 1.56, "pe": 0.55e-3, "dma": 1.9, "bw": 250e3, "sem": 0.08, "lk": 1.0}
+POOLS = {"C": ["PS%d" % k for k in range(8)], "D": []}
+GREATER = [[1, 3, 5, 7], [6, 3, 2, 7], [6, 4, 5, 7]]
+POS = {1: 0, 2: 1, 3: 2, 4: 3, 5: 4, 6: 5, 7: 6, "id": 7, "A": 8, "B": 9}
+PAR = {"cy": 0.92e-3, "gat": 1.56, "pe": 0.46e-3, "dma": 1.62, "bw": 360e3, "sem": 0.065, "mix": 0.3, "turns": 3, "small": 0.0, "flow": 0, "look": 0.25, "ahead": 0.5, "spare": 0.3,
+       "A": 8.3, "E": 8.3, "F": 10.3, "B": 6.8, "aided": [], "S": 1.1, "room": 300e3, "Y": 3.2, "O3": 3.2, "O7": 2.3, "fin": 0, "wide": [2, 5, 8, 9, 10, 11, 13, 15],
+       "moves": 90000, "cut": [11, 12, 21, 41, 61, 72, 71, 52], "mean": 1.5, "seed": 4, "heat": 0.4, "far": 8, "cases": [(1.0, 1.0, 1.0), (1.2, 1.25, 1.4)]}
+STEPS = ("Ba Bb g10 g12 g11 s10 s12 s11 g20 F2a F2b g40 F4a s20 F4b g60 F6a s40 F6b s60 Na Nb g22 g21 g30 s22 s21 g42 g41 s30 g50 s42 s41 g62 g61 s50 g70 s62 s61 "
+         "F3a F3b s70 g31 g32 F5a F5b s31 s32 F7a F7b g51 g52 s51 s52 g71 g72 s71 s72").split()
+ACT_G, VEC_X = "g12 g20 g30 g50 g70".split(), "Bb Na F4b F6b F3a F7a s71".split()
+LONG = {"v": [x for x in STEPS if x in VEC_X or (x[0] == "g" and x not in ACT_G)], "f": []}
+LONG["a"] = [x for x in STEPS if x not in LONG["v"]]
 PLAN = {}
-SECOND = "141 152 164 167 173 182 194 195 229 236 237 239 240 241 247 262 277 284 287 291 294 298 300 325 350 375 376 378 379 381 382 385 386 392 416 420 421 422 424 443 449 451 474 475 476 478"
-ISSUE = "2 0 1 3 5 10 11 12 35 33 32 34 31 36 37 38 43 39 41 45 40 44 53 120 122 103 104 125 126 4 30 47 49 98 50 75 101 7 77 121 56 57 91 123 6 81 83 109 110 127 93 13 61 80 14 119 102 99 52 92 42 90 55 63 97 17 60 94 59 112 87 88 96 95 9 65 111 79 69 68 54 136 89 64 137 105 138 139 46 62 184 26 140 19 146 100 128 58 82 142 72 84 15 154 124 147 149 107 198 150 74 114 141 73 143 156 67 157 51 144 16 199 200 201 151 8 164 183 118 145 165 166 25 168 169 170 174 66 148 70 134 160 152 28 163 76 106 175 158 20 167 159 176 133 21 171 172 113 178 155 202 27 48 179 180 71 78 22 191 24 108 203 205 206 181 185 182 194 195 225 227 173 224 261 29 177 192 186 223 188 210 229 196 193 197 187 23 18 226 264 131 189 190 211 212 153 230 231 232 213 216 265 207 85 228 235 214 215 217 219 237 218 220 266 233 204 262 248 249 116 236 115 234 242 243 238 221 222 387 244 245 246 247 388 130 389 390 252 263 239 240 253 129 254 391 392 255 250 251 268 269 270 271 272 273 275 278 279 274 285 286 277 276 280 258 299 292 281 287 378 379 300 301 375 302 282 283 288 162 303 305 376 349 284 304 324 311 350 325 289 86 161 351 290 312 326 308 327 313 314 306 328 309 241 291 117 315 307 380 329 310 377 316 336 293 333 294 317 381 318 319 337 267 320 256 321 330 295 338 339 382 257 352 340 296 341 353 334 383 335 322 297 331 332 259 384 355 358 298 342 343 323 260 356 345 344 346 359 354 361 347 393 402 362 363 357 364 403 365 132 404 360 405 366 406 407 412 411 386 367 408 368 369 409 370 135 410 371 414 396 374 422 394 421 397 413 399 372 348 429 430 431 432 434 435 208 385 398 373 423 424 433 438 436 441 415 439 437 440 425 448 416 417 418 419 456 426 449 457 458 459 461 462 460 442 427 465 443 463 466 468 467 420 444 464 496 445 469 446 476 470 475 450 497 505 451 471 395 499 472 473 477 400 498 478 452 428 502 506 401 453 508 503 507 504 479 480 481 511 500 454 501 209 447 509 455 510 512 474 482 514 515 516 513 520 517 518 519 483 521 522 523 485 484 492 493 488 486 487 489 490 524 494 491 525 526 527 495 528 529 530 531 533 532 534 536 535"
 
 
-def u_of(j):
-    return j - 4 if j >= 4 else 3 - j
-
-
-def lam_of(q):
-    return q if q >= 4 else 3 - q
-
-
-def r_of(d, u):
-    return [r for r in range(8) if r < (r ^ d) and u_of(r ^ d) == u][0]
+def top(d):
+    return d.bit_length() - 1
 
 
 def runs(x):
     out = []
-    i = 0
-    while i < len(x):
-        n, s = 1, 1
-        if i + 1 < len(x) and x[i + 1] > x[i]:
-            s = x[i + 1] - x[i]
-            while i + n < len(x) and x[i + n] - x[i + n - 1] == s:
-                n += 1
-        out.append((i, n, x[i], s))
-        i += n
+    for i, v in enumerate(x):
+        if out and v > x[i - 1] and (out[-1][1] == 1 or v - x[i - 1] == out[-1][3]):
+            out[-1][1] += 1
+            out[-1][3] = v - x[i - 1]
+        else:
+            out.append([i, 1, v, 1])
     return out
 
 
-def pieces(vals, at):
-    n = len(vals)
-    if n == 1:
-        return [(at, n, vals[0], [])]
-    steps = []
-    k = n // 2
-    while k >= 1:
-        steps.append(vals[k] - vals[0])
-        k //= 2
-    ok = True
-    for a in range(n):
-        v = vals[0]
-        for b in range(len(steps)):
-            if a >> (len(steps) - 1 - b) & 1:
-                v += steps[b]
-        ok = ok and v == vals[a]
-    if ok and n <= 4:
-        return [(at, n, vals[0], steps)]
-    return pieces(vals[:n // 2], at) + pieces(vals[n // 2:], at + n // 2)
+def bits(m):
+    return bin(m).count("1")
 
 
-def deal(T, topo, me, halves):
-    src = T.cores[me]
+def helper(T, topo, r):
+    c = T.cores[r]
+    ok = [k for k in topo.cores_of(c) if topo.die(k) != topo.die(c) and all(topo.may_write(k, x) for x in T.cores)]
+    return ok[[x for x in T.cores if topo.chip(x) == topo.chip(c)].index(c)]
+
+
+def deal(T, topo, me, name):
+    src, aid = T.cores[me], helper(T, topo, me)
     far = [me ^ x for x in range(1, 8) if topo.chip(T.cores[me ^ x]) != topo.chip(src)]
     near = [me ^ x for x in range(1, 8) if topo.chip(T.cores[me ^ x]) == topo.chip(src)]
     eo = topo.engines(src, T.cores[far[0]])
-    ei = [e for e in topo.engines(src, T.cores[near[0]]) if e not in eo]
-    if not halves:
-        order = eo[0::2] + eo[1::4] + eo[3::4]
-        return [[(a, 0, 1 << order[k]) for k, a in enumerate(far)] + [(a, 0, 1 << ei[2 * k]) for k, a in enumerate(near)]]
-    ps = [(a, h) for h in range(2) for a in far]
-    one = [(a, h, 1 << eo[k]) for k, (a, h) in enumerate(ps[:len(eo)])]
-    one += [(a, h, 1 << ei[4 * k + 2 * h]) for k, a in enumerate(near) for h in range(2)]
-    two = [(a, h, (1 << eo[2 * k]) | (1 << eo[2 * k + 1])) for k, (a, h) in enumerate(ps[len(eo):])]
-    return [one, two]
+    ei = [e for e in topo.engines(src, aid) if e not in eo]
+    eo = eo[0::2] + eo[1::4] + eo[3::4]
+    n = 2 if name == "F" else 1
+    ld = T["Ld" + name]
+    st = (lambda a, h: ld[me]) if name[0] == "S" else (lambda a, h: T["St" + name][n * a + h])
+    own = [(T.cores[a], st(a, h), ld[n * me + h], 1 << ei[-1 - h - n * k]) for k, a in enumerate(near) for h in range(n)]
+    aids = []
+    for h in range(n):
+        if (name, h) in PAR["aided"]:
+            own += [(aid, st(a, h), T["Via" + name][k], 1 << ei[k]) for k, a in enumerate(far)]
+            aids += [(T.cores[a], T["Via" + name][k], ld[n * me + h], 1 << eo[k]) for k, a in enumerate(far)]
+        elif h == 0:
+            own += [(T.cores[a], st(a, h), ld[n * me + h], 1 << eo[k]) for k, a in enumerate(far)]
+        else:
+            k = len(eo) - len(far)
+            own += [(T.cores[a], st(a, h), ld[n * me + h], 1 << eo[-1 - i]) for i, a in enumerate(far[:k])]
+            two = sorted(eo)
+            own += [(T.cores[a], st(a, h), ld[n * me + h], (1 << two[2 * i]) | (1 << two[2 * i + 1])) for i, a in enumerate(far[k:])]
+    return own, aids
+
+
+def send(g, T, topo, part, name):
+    calls = []
+    for t in part:
+        free = [c for c in calls if not any(t[3] & u[3] for u in c)]
+        if not free:
+            calls.append([])
+        (free + calls[-1:])[0].append(t)
+    for c in calls:
+        g.remote_dma_fused([RemoteDMATransfer(dst_ids=[DstId(rid=topo.addr(k)[0], pnc=topo.addr(k)[1])], dma_engine_mask=m, remote_sem=T.sem["ar" + name], src=a, dst=b)
+                            for k, a, b, m in c], local_sem=T.sem.sent)
+    return sum(bits(t[3]) for t in part)
 
 
 def schedule(nodes):
-    order = [int(x) for x in ISSUE.split()]
-    if sorted(order) != list(range(len(nodes))):
-        order = list(range(len(nodes)))
-    second = set(int(x) for x in SECOND.split())
-    left = {}
-    for nd in nodes:
-        for s in nd["slots"]:
-            left[s] = left.get(s, 0) + 1
-    pool = {p: list(vs) for p, vs in POOLS.items()}
-    val = {}
-    for i in order:
-        for s in nodes[i]["slots"]:
-            if s not in val:
-                val[s] = pool[s[0]].pop(0)
-        for s in nodes[i]["slots"]:
-            left[s] -= 1
-            if left[s] == 0:
-                pool[s[0]].append(val[s])
-    return [(i, list(nodes[i]["cost"])[-1 if i in second else 0]) for i in order], val
+    n = len(nodes)
+    pre = [set() for _ in nodes]
+    lastw, readers = {}, {}
+    for i, nd in enumerate(nodes):
+        for k in nd["r"] + nd["x"] + nd["w"]:
+            pre[i].update(lastw.get(k, []))
+        for k in nd["w"]:
+            pre[i].update(readers.get(k, []))
+        for k in nd["r"] + nd["x"]:
+            readers.setdefault(k, []).append(i)
+        for k in nd["w"]:
+            lastw[k] = [i]
+            readers[k] = []
+        pre[i].discard(i)
+    soft = [set(j for j in pre[i] if all(k[0] == "~" for k in set(nodes[j]["w"]) & set(nodes[i]["r"] + nodes[i]["w"])) and set(nodes[j]["w"]) & set(nodes[i]["r"]))
+            for i in range(n)]
+    true = [set(p) for p in pre]
+    named = {nd["name"]: i for i, nd in enumerate(nodes)}
+    for line in (LONG["v"], LONG["a"]):
+        for a, b in zip(line, line[1:]):
+            if named[a] not in pre[named[b]]:
+                pre[named[b]].add(named[a])
+                soft[named[b]].add(named[a])
+    end = {}
+    post = [[] for _ in nodes]
+    for i in range(n):
+        for j in pre[i]:
+            post[j].append(i)
+    way, due = [0.0] * n, [0.0] * n
+    left = [len(p) for p in post]
+    line = [i for i in range(n) if not left[i]]
+    for i in line:
+        for j in pre[i]:
+            left[j] -= 1
+            if not left[j]:
+                line.append(j)
+    for i in line:
+        nd = nodes[i]
+        way[i] = min(nd["cost"].values()) + max([way[j] + (0.0 if i in soft[j] else nd["lat"] + nd["bytes"] / PAR["bw"] + PAR["sem"]) for j in post[i]] + [nd["lat"]])
+        due[i] = min([nd["rank"][0]] + [due[j] for j in post[i]])
+    units = {}
+    unit = [nd["slots"][0] if nd["slots"] else i for i, nd in enumerate(nodes)]
+    for i in range(n):
+        if unit[i] == i and not nodes[i]["name"]:
+            both = set(unit[j] for j in pre[i]) & set(unit[j] for j in post[i])
+            unit[i] = ([u for u in both if isinstance(u, tuple)] + [i])[0]
+    for i in range(n):
+        units.setdefault(unit[i], []).append(i)
+    outer = {u: set(unit[j] for i in m for j in pre[i]) - {u} for u, m in units.items()}
+    after = {u: [] for u in units}
+    for u in units:
+        for v in outer[u]:
+            after[v].append(u)
+    rank = {u: min(PAR["mix"] * due[i] - way[i] for i in m) - (0 if any(nodes[i]["name"] or nodes[i]["bytes"] for i in m) else PAR["small"]) for u, m in units.items()}
+    sem = PAR["sem"]
+
+    def sweep(rank, back):
+        before, behind = (after, outer) if back else (outer, after)
+        wait = {u: len(before[u]) for u in units}
+        ready = [u for u in units if not wait[u]]
+        busy, val, fin, start = {}, {}, {}, {}
+
+        def gap(q, t, d):
+            for a, b in busy.get(q, []):
+                if b > t:
+                    if a >= t + d:
+                        break
+                    t = b
+            return t
+
+        def take(q, a, b):
+            busy.setdefault(q, []).append((a, b))
+            busy[q].sort()
+
+        while ready:
+            u = min(ready, key=lambda u: (rank[u], units[u][0]))
+            ready.remove(u)
+            t0 = 0.0
+            while True:
+                last, got = (t0, t0, None), []
+                for i in units[u][::-1 if back else 1]:
+                    nd = nodes[i]
+                    d = nd["bytes"] / PAR["bw"]
+                    if back:
+                        t = max([end[j] + sem for j in post[i] if i not in soft[j]] + [0.0])
+                        if d:
+                            t = gap("bus", t, d)
+                            take("bus", t, t + d)
+                        t = max([t + d + nd["lat"], t0] + [end[j] for j in post[i]])
+                    else:
+                        t = max([end[j] if j in soft[i] else fin[j] + sem for j in pre[i]] + [t0])
+                        if d:
+                            lead = nd["lat"] + max(nd["cost"].values())
+                            t = gap("bus", t + lead, d) - lead
+                    t, q = min(((gap(q, max(t, last[0] if q == last[2] else last[1]), c), q) for q, c in nd["cost"].items()),
+                               key=lambda x: x[0] + nd["cost"][x[1]] + (x[1] == "v") * PAR["spare"])
+                    end[i] = t + nd["cost"][q]
+                    fin[i] = end[i] + (0.0 if back else nd["lat"])
+                    got.append((i, q, t))
+                    last = (end[i], end[i] + sem, q)
+                if not isinstance(u, tuple):
+                    break
+                a, b = got[0][2], last[1]
+                t1, v = min((gap(v, a, b - a), v) for v in POOLS[u[0]])
+                if t1 <= a:
+                    val[u] = v
+                    take(v, a, b)
+                    break
+                t0 = t1
+            for i, q, t in got:
+                take(q, t, end[i])
+                start[i] = (t, i, q)
+                if nodes[i]["bytes"] and not back:
+                    d = nodes[i]["bytes"] / PAR["bw"]
+                    t = gap("bus", fin[i], d)
+                    take("bus", t, t + d)
+                    fin[i] = t + d
+            for v in behind[u]:
+                wait[v] -= 1
+                if not wait[v]:
+                    ready.append(v)
+        PLAN["fin"] = {str(nodes[i]["w"][0]): round(fin[i], 1) for i in fin}
+        return max(fin[i] for i in range(n)), [(i, q) for t, i, q in sorted(start.values())], val, {u: -max(fin[i] for i in m) for u, m in units.items()}
+
+    def flow():
+        wait = [len(p) for p in pre]
+        shut = {u: sum(len(units[v]) for v in outer[u]) for u in units}
+        pool = {p: {v: 0.0 for v in vs} for p, vs in POOLS.items()}
+        left = {u: len(m) for u, m in units.items()}
+        val, fin, free, bank, order, at = {}, {}, {}, {}, [], {}
+        ready = [i for i in range(n) if not wait[i]]
+        bus = 0.0
+        prev = {}
+        for line in (LONG["v"], LONG["a"]):
+            us = [unit[named[x]] for x in line if x[0] == "s"]
+            prev.update(zip(us[1:], us))
+        while ready:
+            cand = []
+            for i in ready:
+                nd, u = nodes[i], unit[i]
+                if i not in at:
+                    at[i] = max([end[j] if j in soft[i] else fin[j] + sem for j in pre[i]] + [0.0])
+                t = at[i]
+                if isinstance(u, tuple):
+                    if u not in val:
+                        if (prev.get(u, u) not in val and prev.get(u, u) != u if u[0] == "D" else shut[u]) or not pool[u[0]]:
+                            continue
+                        t = max(t, min(pool[u[0]].values()))
+                if nd["bytes"]:
+                    t = max(t, bus - nd["lat"] - PAR["ahead"])
+                t, q = min(((max(t, free.get(q, 0.0), bank.get(u, (0.0, q))[0] + (sem if bank.get(u, (0.0, q))[1] != q else 0.0) if nd["slots"] else 0.0), q) for q in nd["cost"]),
+                           key=lambda x: x[0] + (x[1] == "v") * PAR["spare"])
+                cand.append((t, i, q))
+            t0, _, q0 = min(cand)
+            t, i, q = min([c for c in cand if c[2] == q0 and c[0] <= t0 + PAR["look"]],
+                          key=lambda c: (PAR["mix"] * due[c[1]] - way[c[1]] + (PAR["small"] if nodes[c[1]]["name"] or unit[c[1]] in val and unit[c[1]][0] == "D" else 0.0), c[1]))
+            nd, u = nodes[i], unit[i]
+            free[q] = end[i] = t + nd["cost"][q]
+            fin[i] = end[i] + nd["lat"]
+            if nd["bytes"]:
+                bus = fin[i] = max(bus, fin[i]) + nd["bytes"] / PAR["bw"]
+            if isinstance(u, tuple):
+                if u not in val:
+                    val[u] = min(pool[u[0]], key=pool[u[0]].get)
+                    pool[u[0]].pop(val[u])
+                if nd["slots"]:
+                    bank[u] = (end[i], q)
+                left[u] -= 1
+                if not left[u]:
+                    pool[u[0]][val[u]] = bank[u][0] + sem
+            for v in after[u]:
+                shut[v] -= 1
+            order.append((i, q))
+            PLAN.setdefault("log", []).append((round(t, 1), q, nd["name"] or str(nd["w"][0])))
+            ready.remove(i)
+            for j in post[i]:
+                wait[j] -= 1
+                if not wait[j]:
+                    ready.append(j)
+        PLAN["fin"] = {str(nodes[i]["w"][0]): round(fin[i], 1) for i in fin}
+        PLAN["end"] = max(fin[i] for i in range(n))
+        return order, val
+
+    def polish(order):
+        hard = [sorted(true[i]) for i in range(n)]
+        succ = [[j for j in post[i] if i in true[j]] for i in range(n)]
+        qs = {q: k for k, q in enumerate("gvaps")}
+        seq, on = [i for i, q in order], [0] * n
+        for i, q in order:
+            on[i] = qs[q]
+        alt = [[qs[q] for q in nd["cost"]] for nd in nodes]
+        slots = sorted(set(s for nd in nodes for s in nd["slots"]))
+        sl = [slots.index(nd["slots"][0]) if nd["slots"] else -1 for nd in nodes]
+        count = [sl.count(k) for k in range(len(slots))]
+        kind = [s[0] == "D" for s in slots]
+        sets = []
+        for fc, fl, fb in PAR["cases"]:
+            sets.append(([{qs[q]: c * (fc if q in "vap" else 1.0) for q, c in nd["cost"].items()} for nd in nodes], [nd["lat"] * fl for nd in nodes],
+                         [nd["bytes"] / PAR["bw"] * fb for nd in nodes], [[(j, j in soft[i]) for j in hard[i]] for i in range(n)]))
+
+        m = len(count)
+        marks = [{0: ([0.0] * 5, 0.0, [(0.0, v) for v in POOLS["C"]], list(count), [0.0] * m, [-1] * m, [None] * m), "t": ([0.0] * n, [0.0] * n)} for _ in sets]
+        fresh = []
+
+        def run(keep=None, first=0):
+            total, first = 0.0, first - first % 48
+            fresh[:] = []
+            for (cost, lat, byt, pr), mark in zip(sets, marks):
+                free, bus, p, left, last, lq, got = mark[first]
+                free, p, left, last, lq, got = list(free), list(p), list(left), list(last), list(lq), list(got)
+                fin, end = list(mark["t"][0]), list(mark["t"][1])
+                new = {"t": (fin, end)}
+                fresh.append(new)
+                for a in range(first, n):
+                    if not a % 48:
+                        new[a] = (list(free), bus, list(p), list(left), list(last), list(lq), list(got))
+                    i = seq[a]
+                    q = on[i]
+                    t = free[q]
+                    for j, s in pr[i]:
+                        u = end[j] if s else fin[j]
+                        if u > t:
+                            t = u
+                    k = sl[i]
+                    if k >= 0:
+                        if got[k] is None:
+                            if not p:
+                                return 1e9
+                            u, got[k] = p.pop(0)
+                            if u > t:
+                                t = u
+                        elif lq[k] != q and last[k] > t:
+                            t = last[k]
+                    t += cost[i][q]
+                    free[q] = end[i] = t
+                    u = t + lat[i]
+                    if byt[i]:
+                        if bus > u:
+                            u = bus
+                        bus = u = u + byt[i]
+                    fin[i] = u + sem
+                    if k >= 0:
+                        last[k], lq[k] = t + sem, q
+                        left[k] -= 1
+                        if not left[k]:
+                            p.append((t + sem, got[k]))
+                total += max(fin) + (PAR["mean"] * sum(fin) / n if keep is None else 0.0)
+            if keep is not None:
+                keep.update(zip(slots, got))
+            return total / len(sets)
+
+        def accept():
+            for mark, new in zip(marks, fresh):
+                mark.update(new)
+
+        x, cur = PAR["seed"], run()
+        accept()
+        best = (cur, list(seq), list(on))
+        for k in range(PAR["moves"]):
+            x = (x * 6364136223846793005 + 1442695040888963407) % 2 ** 64
+            a = (x >> 40) % n
+            i = seq[a]
+            room = PAR["heat"] * (1.0 - k / PAR["moves"]) * ((x >> 8) % 1000) ** 3 / 1e9
+            if len(alt[i]) > 1 and (x >> 20) % 3 == 0:
+                old = on[i]
+                on[i] = alt[i][1] if old == alt[i][0] else alt[i][0]
+                e = run(None, a)
+                if e > cur + room:
+                    on[i] = old
+                    continue
+            else:
+                far, b, d = 1 + ((x >> 24) % 1000) ** 2 * PAR["far"] // 10 ** 6, a, 1 - 2 * ((x >> 21) % 2)
+                go, stay = [i], []
+                need = set(true[i] if d < 0 else succ[i])
+                while far and 0 <= b + d < n:
+                    b += d
+                    j = seq[b]
+                    if j in need:
+                        go.append(j)
+                        need.update(true[j] if d < 0 else succ[j])
+                    else:
+                        stay.append(j)
+                        far -= on[j] == on[i]
+                if not stay:
+                    continue
+                lo, hi = min(a, b), max(a, b) + 1
+                old = seq[lo:hi]
+                seq[lo:hi] = go[::-1] + stay[::-1] if d < 0 else stay + go
+                e = run(None, lo)
+                if e > cur + room:
+                    seq[lo:hi] = old
+                    continue
+            accept()
+            cur = e
+            if e < best[0]:
+                best = (e, list(seq), list(on))
+        seq[:], on[:] = best[1], best[2]
+        val = {}
+        PLAN["end"] = run(val)
+        return [(i, "gvaps"[on[i]]) for i in seq], val
+
+    if PAR["flow"]:
+        return flow()
+    best = None
+    for k in range(PAR["turns"]):
+        got = sweep(rank, False)
+        if best is None or got[0] < best[0]:
+            best = got
+        if k + 1 < PAR["turns"]:
+            rank = sweep(got[3], True)[3]
+    PLAN["end"] = best[0]
+    if PAR["moves"]:
+        for nd in nodes:
+            nd["cost"] = nd["any"]
+        return polish(best[1])
+    return best[1], best[2]
 
 
 def rank_program(g, core, T, topo):
     me = T.rank_of(core)
     if me is None:
+        for r in range(8):
+            if helper(T, topo, r) == core and PAR["aided"]:
+                n = 0
+                for name, h in PAR["aided"]:
+                    own, aids = deal(T, topo, r, name)
+                    g.wait_ge(T.sem["ar" + name], sum(bits(t[3]) for t in own if t[0] == core))
+                    n += send(g, T, topo, aids, name)
+                g.wait_ge(T.sem.sent, n)
         return
     Q = {"g": g, "v": g.vector, "a": g.scalar, "p": g.tensor, "s": g.sync}
     CS = {"g": "cg", "v": "cv", "a": "ca", "p": "cp"}
     nodes = []
     val = {}
-    total = {}
-    nd_ = [0]
     ns = [0]
+    lvl = [99]
+
+    def stage(x):
+        lvl[0] = PAR.get(x, 99)
+
     CY = PAR["cy"]
+    V = g.vector
 
     def slot(p):
         ns[0] += 1
@@ -160,567 +479,619 @@ def rank_program(g, core, T, topo):
             return x[1](val[x[2]])
         return x
 
-    def ps(s, p0, p1, a, b, step=1):
-        return ("lazy", lambda v: T[v][p0:p1, a:b:step], s)
+    def ps(s, a, b, p1=128, step=1):
+        return ("lazy", lambda v: T[v][0:p1, a:b:step], s)
 
     def tb(s, a, b):
-        return ("lazy", lambda v: T.TT[:, 1024 * int(v[1:]) + a:1024 * int(v[1:]) + b], s)
+        return T.TT[:, 1024 * int(s[1:]) + a:1024 * int(s[1:]) + b]
 
-    def node(kind, cost, f, r, w, lat=0.0, nbytes=0, also=()):
-        slots = sorted(set(k for k in list(r) + list(w) if isinstance(k, tuple)))
-        nodes.append({"kind": kind, "cost": cost, "f": f, "r": list(r), "w": list(w), "lat": lat, "bytes": nbytes, "also": list(also), "slots": slots})
+    def node(kind, cost, f, r, w, lat=0.0, nbytes=0, push=0.0):
+        x = [k for k in r if isinstance(k, tuple)]
+        r = [k for k in r if k not in x]
+        slots = sorted(set(k for k in r + x + list(w) if isinstance(k, tuple)))
+        nodes.append({"kind": kind, "cost": cost, "f": f, "r": r, "x": x, "w": list(w), "lat": lat, "bytes": nbytes, "slots": slots, "push": push,
+                      "rank": (lvl[0], len(nodes)), "name": "", "any": cost})
+
+    def on(name):
+        return "v" if name in LONG["v"] else "a"
+
+    def call(name):
+        nodes[-1]["name"] = name
+        if name[0] != "g":
+            nodes[-1]["any"] = {q: min(nodes[-1]["cost"].values()) for q in "va"}
 
     def cyc(n):
         return max(64, n) * CY
 
-    def gop(f, n, w):
-        node("op", {"g": 0.13 + 2 * n * CY}, lambda q: f(), [], w)
+    def vop(f, r, w, n=64):
+        node("op", {"v": cyc(n)}, lambda q: f(), r, w)
 
-    def memset(ap, v, n, w):
-        node("op", {"v": cyc(n)}, lambda q: g.vector.memset(ap, v), [], w)
+    def gop(f, n, r, w):
+        node("op", {"g": 0.14 + 2 * n * CY}, lambda q: f(), r, w)
+
+    def memset(ap, v, w, n=64):
+        vop(lambda: V.memset(ap, v), [], w, n)
 
     def pe(mms, r, w):
-        node("pe", {"p": sum(m[5] for m in mms) * PAR["pe"]}, mms, r, w)
+        out = []
+        for i, m in enumerate(mms):
+            if m is not None:
+                out.append((m[0], m[1], m[2], i == 0 or mms[i - 1] is None, i == len(mms) - 1 or mms[i + 1] is None, m[3]))
+        node("pe", {"p": sum(m[5] + 8 for m in out) * PAR["pe"]}, out, r, w)
 
-    def dma(qs, moves, r, w, nbytes):
-        node("dma", {q: 0.1 * len(moves) for q in qs}, moves, r, w, PAR["dma"], nbytes)
+    def dma(qs, moves, r, w, nbytes, push=0.0):
+        node("dma", {q: 0.07 * len(moves) for q in qs}, moves, r, w, PAR["dma"], nbytes, push)
 
-    def exchange(name, src, dst, r, w, lat, halves=False):
-        node("ex", {"g": 0.6 if not halves else 1.2}, (name, src, dst, halves, w), r, [], lat * PAR["lk"], 0, [w])
+    def exchange(name, r, lat):
+        node("ex", {"g": 0.7}, name, r, ["ar" + name], lat, PAR["room"] if name[0] == "S" else 0)
 
     def ts(out, in0, s1, s2, o0, o1, r, w, n=64):
         if o1 is None:
-            node("op", {"v": cyc(n)}, lambda q: g.vector.tensor_scalar(z(out), z(in0), s1, None, o0), r, w)
+            vop(lambda: V.tensor_scalar(z(out), z(in0), z(s1), None, o0), r, w, n)
         else:
-            node("op", {"v": cyc(n)}, lambda q: g.vector.tensor_scalar(z(out), z(in0), s1, s2, o0, o1), r, w)
+            vop(lambda: V.tensor_scalar(z(out), z(in0), z(s1), z(s2), o0, o1), r, w, n)
 
     def tt(out, a, b, o, r, w, n=64):
-        node("op", {"v": cyc(n)}, lambda q: g.vector.tensor_tensor(z(out), z(a), z(b), o), r, w)
+        vop(lambda: V.tensor_tensor(z(out), z(a), z(b), o), r, w, n)
 
     def cp(qs, out, in_, r, w, n=64):
         def f(q):
             if q == "v":
-                return g.vector.tensor_copy(z(out), z(in_))
+                return V.tensor_copy(z(out), z(in_))
             return g.scalar.activation(z(out), z(in_), ACT.Copy)
         node("op", {q: cyc(n) for q in qs}, f, r, w)
 
     def addc(qs, out, in_, c, r, w, n, half):
         def f(q):
             if q == "v":
-                return g.vector.tensor_scalar(out, in_, c, None, ALU.add)
-            return g.scalar.activation(out, in_, ACT.Identity, bias=c)
+                return V.tensor_scalar(z(out), z(in_), c, None, ALU.add)
+            return g.scalar.activation(z(out), z(in_), ACT.Identity, bias=c)
         node("op", {q: cyc(n // 2 if half and q == "v" else n) for q in qs}, f, r, w)
 
     def blk(t, k, n=128, m=1):
         return t[:, k * n:(k + m) * n]
 
-    def rows(t, a=me):
-        return t[a * 128:(a + 1) * 128, :]
-
     def c1(t, k):
         return t[:, k:k + 1]
 
-    gop(lambda: g.iota(T.PI[:, 0:1], [[0, 1]], 0, 1), 1, ["PI0", "~g0"])
-    gop(lambda: g.iota(T.col[:], [[1, 192]], 0, 0, allow_small_or_imprecise_dtypes=True), 192, ["col", "~g0"])
+    EQ, MUL, ADD, SUB, GT = ALU.is_equal, ALU.mult, ALU.add, ALU.subtract, ALU.is_gt
     mine = slice(16 * me, 16 * me + 16)
-    dma("s", [(T.StA[:], T.mp[:, 0:384])], [], ["StA", "~s0"], 196e3)
-    dma("a", [(T.LdL[me, 0, :], T.lam[0, :]), (T.LdL[me, 1:128, :], T.mp[0, 7:896])], [], ["LdL", "~a0"], 4e3)
-    dma("a", [(rows(T.LdA), T.mp[mine, 0:384])], [], ["LdA", "~a0"], 24e3)
-    dma("s", [(T.StF[h::2], T.ft[:, 1024 * h:1024 * h + 1024]) for h in range(2)], [], ["StF", "~s0"], 524e3)
-    dma("s", [(T.StB[:], T.mp[:, 384:896])], [], ["StB", "~s0"], 262e3)
-    dma("a", [(T.LdF[2 * lam_of(me) + h], T.ft[mine, 1024 * h:1024 * h + 1024]) for h in range(2)], [], ["LdF", "~a0"], 65e3)
-    dma("a", [(rows(T.LdB), T.mp[mine, 384:896])], [], ["LdB", "~a0"], 32e3)
-    dma("s", [(blk(T.MP3, m), blk(T.mp, 2 * m + 2)) for m in range(3)], [], ["MP3", "~s0"], 196e3)
-    exchange("A", lambda a, h: rows(T.StA, a), lambda h: rows(T.LdA), ["StA", "~g0"], "LdA", 6.5)
-    exchange("L", lambda a, h: T.LdL[me], lambda h: T.LdL[me], ["LdL", "~exA"], "LdL", 7.0)
-    exchange("F", lambda a, h: T.StF[2 * a + h], lambda h: T.LdF[2 * lam_of(me) + h], ["StF", "~exL"], "LdF", 11.0, True)
-    exchange("B", lambda a, h: rows(T.StB, a), lambda h: rows(T.LdB), ["StB", "~exF"], "LdB", 14.0)
-    node("nop", {"g": 0.0}, None, ["~exB"], ["~g1"])
 
-    def table(o, pat, base, n, w):
-        node("op", {"g": 0.13 + 2 * n * CY}, lambda q: g.iota(o, pat, base, 0, allow_small_or_imprecise_dtypes=True), ["~g1"], w)
+    gop(lambda: g.iota(T.PI[:, 0:1], [[0, 1]], 0, 1), 1, [], ["PI0", "~g0"])
+    gop(lambda: g.iota(T.col[:], [[1, 208]], -16, 0, allow_small_or_imprecise_dtypes=True), 208, ["~g0"], ["col", "~g1"])
+    gop(lambda: g.iota(T.cgr[:], [[1, 8], [0, 16]], 0, 0, allow_small_or_imprecise_dtypes=True), 128, ["~g1"], ["cgr", "~g2"])
+    dma("s", [(T.StA[:, 64 * k:64 * k + 64, :], blk(T.mp, 1 + k)) for k in range(2)], [], ["StA", "~s0"], 131e3)
+    dma("a", [(T.StE[:], blk(T.mp, 0))], [], ["StE"], 0)
+    dma("s", [(T.StF[h::2], T.ft[:, 1024 * h:1024 * h + 1024]) for h in range(2)], ["~s0"], ["StF", "~s1"], 524e3)
+    dma("s", [(T.MPB[:], T.mp[:, 256:896])], ["~s1"], ["MPB", "~s2"], 328e3)
+    dma("s", [(T.LdA[me, 64 * k:64 * k + 64, :], T.mp[mine, 128 + 128 * k:256 + 128 * k]) for k in range(2)] + [(T.LdE[me], T.mp[mine, 0:128])], ["~s2"], ["LdA", "~s3"], 24e3)
+    dma("s", [(T.LdF[2 * me + h], T.ft[mine, 1024 * h:1024 * h + 1024]) for h in range(2)], ["~s3"], ["LdF"], 65e3)
+    dma("a", [(T.LM[0:1, 0:7], T.lam[0:1, :])], [], ["LM"], 0)
+    exchange("A", ["StA", "~g2"], PAR["A"])
+    exchange("E", ["StE", "~arA"], PAR["E"])
+    exchange("F", ["StF", "~arE"], PAR["F"])
+    gop(lambda: g.partition_broadcast(T.LB[:, 0:7], T.LM[0:1, 0:7], 128), 14, ["LM", "~arF"], ["LB", "~g3"])
+    gop(lambda: g.iota(T.WI[:], [[0, 2048]], 0, 0), 2048, ["~g3"], ["WI"])
+    ts(T.BT[:, 512:528], T.col[:, 0:16], 0.0, None, MUL, None, ["col"], ["BTw"])
+    cp("v", T.BT[:, 0:512], T.MPB[:, 128:640], ["MPB"], ["BT"], 512)
+    cp("v", T.BT[:, 512:519], T.LB[:, 0:7], ["LB"], ["BTw"])
+    dma("s", [(T.StB[:], T.BT[:]), (T.LdB[me], T.BT[mine, :])], ["BT", "BTw"], ["StB"], 160e3)
+    exchange("B", ["StB", "~arF"], PAR["B"])
 
-    table(T.cgr[:], [[1, 8], [0, 16]], 0, 128, ["cgr"])
-    utk = []
-    for n, (d, x) in enumerate(((1, 0), (2, 0), (2, 1), (4, 0), (4, 1), (6, 0), (6, 1))):
-        vals = [u_of(max(a ^ x, a ^ x ^ d)) for a in range(8)]
-        for at, cnt, base, steps in pieces(vals, 0):
-            utk.append("UT%d_%d" % (n, at))
-            table(T.UT[:, 128 * n + 16 * at:128 * n + 16 * (at + cnt)], [[s, 2] for s in steps] + [[0, 16]], base, 16 * cnt, [utk[-1]])
+    stage(2)
+    CC, PF = T.CC, T.PF
+    TG, TB, RM, FK, BT6, SB, TP, I3, UB, ONE, KH3, KK = 0, 8, 16, 24, 28, 36, 66, 74, 82, 90, 91, 92
 
-    memset(T.WM1[:], 0.0, 1024, ["WM1"])
+    def col(a, n):
+        return T.col[:, 16 + a:16 + a + n]
+
     for k in range(3):
         ts(c1(T.PI, 1 + k), c1(T.PI, 0), 4 + k, 1, ALU.logical_shift_right, ALU.bitwise_and, ["PI0"], ["PI%d" % (1 + k)])
     ts(c1(T.PI, 4), c1(T.PI, 0), 15, None, ALU.bitwise_and, None, ["PI0"], ["PI4"])
     ts(c1(T.PI, 5), c1(T.PI, 0), 1, 7, ALU.logical_shift_right, ALU.bitwise_and, ["PI0"], ["PI5"])
-    ts(c1(T.PI, 6), c1(T.PI, 0), 4, 3, ALU.logical_shift_right, ALU.bitwise_and, ["PI0"], ["PI6"])
-    cp("v", T.PF[:, 0:7], T.PI[:, 0:7], ["PI%d" % k for k in range(7)], ["PF"])
-    P0, B0, KM16, KH = c1(T.PF, 0), c1(T.PF, 1), c1(T.PF, 4), c1(T.PF, 5)
-    CC = T.CC
-    TG, TB, T64, RM, FK, NB, SO, AL, BE, UU, KHM, WE, RX1 = 0, 8, 16, 24, 32, 36, 40, 44, 68, 92, 96, 104, 108
+    ts(c1(T.PI, 6), c1(T.PI, 0), 7, None, ALU.bitwise_and, None, ["PI0"], ["PI6"])
+    ts(c1(T.PI, 7), c1(T.PI, 0), 1, None, ALU.bitwise_and, None, ["PI0"], ["PI7"])
+    cp("v", PF[:], T.PI[:], ["PI%d" % k for k in range(8)], ["PF"])
+    P0, I16, KH, K7, K1 = c1(PF, 0), c1(PF, 4), c1(PF, 5), c1(PF, 6), c1(PF, 7)
+    ts(CC[:, FK:FK + 3], PF[:, 1:4], -2.0, 1.0, MUL, ADD, ["PF"], ["FK"])
+    cp("v", c1(CC, TG), P0, ["PF"], ["TG0"])
     for k in range(3):
-        ts(c1(CC, FK + k), c1(T.PF, 1 + k), -32.0 * 2 ** k, 16.0 * 2 ** k, ALU.mult, ALU.add, ["PF"], ["FK%d" % k])
-    cp("v", c1(CC, TG), P0, ["PF"], ["TGa"])
-    ts(CC[:, RM:RM + 8], T.col[:, 0:8], KH, None, ALU.is_equal, None, ["col", "PF"], ["RM"])
-    ts(c1(CC, TG + 1), P0, c1(CC, FK), None, ALU.add, None, ["PF", "FK0"], ["TGb"])
-    ts(CC[:, NB:NB + 3], T.PF[:, 1:4], -1.0, 1.0, ALU.mult, ALU.add, ["PF"], ["NB"])
-    ts(CC[:, TG + 2:TG + 4], CC[:, TG:TG + 2], c1(CC, FK + 1), None, ALU.add, None, ["TGa", "TGb", "FK1"], ["TGc"])
-    ts(CC[:, SO:SO + 2], T.PF[:, 1:3], -2048.0, 2048.0, ALU.mult, ALU.add, ["PF"], ["SO"])
-    ts(CC[:, TG + 4:TG + 8], CC[:, TG:TG + 4], c1(CC, FK + 2), None, ALU.add, None, ["TGa", "TGb", "TGc", "FK2"], ["TG"])
-    ts(T.ID[:], T.col[:, 0:128], 16.0, KM16, ALU.mult, ALU.add, ["col", "PF"], ["ID"], 128)
-    ts(CC[:, TB:TB + 8], CC[:, TG:TG + 8], KM16, 15.0, ALU.subtract, ALU.add, ["TG", "PF"], ["TB"])
-    ts(CC[:, T64:T64 + 8], CC[:, TG:TG + 8], 64.0, None, ALU.add, None, ["TG"], ["T64"])
-    ts(CC[:, KHM:KHM + 3], T.col[:, 0:3], -1.0, KH, ALU.mult, ALU.add, ["col", "PF"], ["KHM"])
-    for n, (src, wt) in enumerate(((c1(CC, NB), 1.0 / 16), (c1(CC, NB), 128.0), (B0, 1.0 / 16), (B0, 128.0))):
-        ts(c1(CC, WE + n), src, wt, None, ALU.mult, None, ["NB", "PF"], ["WE%d" % n])
-    ts(c1(CC, RX1), c1(CC, NB), KH, None, ALU.is_equal, None, ["NB", "PF"], ["RX1"])
-    ts(c1(CC, RX1 + 1), B0, KH, None, ALU.is_equal, None, ["PF"], ["RX2"])
+        ts(c1(CC, TP + k), c1(CC, FK + k), 16.0 * 2 ** k, None, MUL, None, ["FK"], ["TP%d" % k])
+        ts(CC[:, TG + 2 ** k:TG + 2 ** (k + 1)], CC[:, TG:TG + 2 ** k], c1(CC, TP + k), None, ADD, None, ["TG%d" % i for i in range(k + 1)] + ["TP%d" % k], ["TG%d" % (k + 1)])
+    TGK = ["TG0", "TG1", "TG2", "TG3"]
+    ts(CC[:, TB:TB + 8], CC[:, TG:TG + 8], I16, 15.0, SUB, ADD, TGK + ["PF"], ["TB"])
+    ts(CC[:, RM:RM + 8], col(0, 8), KH, None, EQ, None, ["col", "PF"], ["RM"])
 
-    def onehot(out, x, wt, key, w, n=128):
-        ts(out, T.col[:, 0:128], c1(CC, TG + x), wt, ALU.is_equal, ALU.mult, ["col", "TG"] + key, w, n)
-
-    pm = {}
-    for x, par in ((2, 0), (3, 0), (2, 1), (3, 1), (1, 2), (5, 2), (7, 2)):
-        n = 2 * len(pm)
-        pm[x, par] = n
-        for k in range(2):
-            wt = (1.0 / 16, 128.0)[k] if par == 2 else c1(CC, WE + 2 * par + k)
-            onehot(blk(T.PM, n + k), x, wt, [] if par == 2 else ["WE%d" % (2 * par + k)], ["PM%d" % (n + k)])
-    for n, (x, wt) in enumerate(((0, 1.0), (0, -1.0), (4, -1.0))):
-        onehot(blk(T.PM, 14 + n), x, wt, [], ["PMd%d" % n])
-    EYE, NEG, SWP = blk(T.PM, 14), blk(T.PM, 15), blk(T.PM, 16)
-    if ON_ACT:
-        onehot(blk(T.PM, 17 + 2), 4, 1.0, [], ["PMd3"])
-    for n, (x, wt) in enumerate(((0, c1(CC, NB)), (0, B0), (1, B0), (1, c1(CC, NB)))):
-        onehot(blk(T.RX, 3 + n), x, wt, ["NB", "PF"], ["RX%d" % (3 + n)])
-    for m in range(3):
-        onehot(blk(T.RX, m), 2 * m + 3, 1.0, [], ["RX%d" % m])
+    def onehot(out, x, wt, w):
+        ts(out, col(0, 128), c1(CC, TG + x), wt, EQ, MUL, ["col"] + TGK, w)
 
     def mk_b(n, x, mask, key):
-        ts(blk(T.BM, n, 144), T.col[:, 0:144], c1(CC, TB + x), mask, ALU.is_equal, ALU.mult, ["col", "TB", key], ["BM%d" % n], 144)
+        ts(blk(T.BM, n, 8), T.col[:, 31:144:16], c1(CC, TB + x), mask, EQ, MUL, ["col", "TB", key], ["BM%d" % n])
 
-    mk_b(0, 2, c1(CC, RX1), "RX1")
-    mk_b(1, 2, c1(CC, RX1 + 1), "RX2")
+    for k in ("WM2", "WM3"):
+        memset(T[k][:], 0.0, [k], 1024)
+    memset(T.W[:, 2048:4096], 0.0, ["Wy"], 1024)
+    pm = {2: 0, 3: 2, 1: 4, 5: 6, 7: 8}
+    for x in pm:
+        onehot(blk(T.PM, pm[x]), x, 1.0 / 16, ["PM%d" % pm[x]])
+        onehot(blk(T.PM, pm[x] + 1), x, 128.0, ["PM%d" % (pm[x] + 1)])
+    ts(c1(CC, 96), I16, 0.0, None, EQ, None, ["PF"], ["R0"])
+    ts(T.BH[:], T.col[:, 31:144:16], c1(CC, TB + 2), c1(CC, 96), EQ, MUL, ["col", "TB", "R0"], ["BM0"])
+    mk_b(1, 3, c1(CC, RM + 0), "RM")
+    EYE, NEG, SWQ, SWP = [blk(T.PM, 10 + k) for k in range(4)]
+    for k, name in enumerate(("EYE", "NEG", "SWQ", "SWP")):
+        onehot(blk(T.PM, 10 + k), 4 * (k // 2), 1.0 - 2 * (k % 2), [name])
+    for x in (0, 2, 3, 4, 5, 6, 7):
+        onehot(blk(T.RT, x), x, 1.0, ["RT%d" % x])
+    MASKS, SCALES = [1, 2, 4, 3, 6, 5], [1, 2, 4, 16, 32, 2048]
+    BS = T.BS
+    cp("v", BS[:, 0:3], PF[:, 1:4], ["PF"], ["B6a"])
+    tt(BS[:, 3:5], PF[:, 1:3], PF[:, 2:4], ALU.not_equal, ["PF"], ["B6b"])
+    tt(BS[:, 5:6], PF[:, 1:2], PF[:, 3:4], ALU.not_equal, ["PF"], ["B6c"])
+    ts(BS[:, 6:12], BS[:, 0:6], -1.0, 1.0, MUL, ADD, ["B6a", "B6b", "B6c"], ["SB1"])
+    for n, s in enumerate(SCALES[1:]):
+        ts(blk(BS, n + 1, 12), BS[:, 0:12], float(s), None, MUL, None, ["SB1"], ["SB%d" % s])
+
+    def bit(s, f, on=range(8)):
+        for k in range(12):
+            if all((bin(a & MASKS[k % 6]).count("1") + k // 6) % 2 == f(a) for a in on):
+                return c1(BS, 12 * SCALES.index(s) + k)
+
+    SBK = ["SB%d" % s for s in SCALES]
+    ts(T.CI[:], col(0, 192), I16, -64.0, SUB, ADD, ["col", "PF"], ["CI"], 96)
+    for d in range(1, 8):
+        t = top(d)
+        lo, hi = [k for k in range(3) if k != t]
+        less = [a for a in range(8) if not a >> t & 1]
+        ts(c1(CC, UB + d), bit(1, lambda a: a >> t & 1), 1000.0, bit(32, lambda a: GREATER[t].index(a ^ d) >> 1, less), MUL, ADD, SBK, ["UB%d" % d])
+        ts(blk(T.FM, d - 1, 192), T.CI[:], bit(16, lambda a: GREATER[t].index(a ^ d) & 1, less), c1(CC, UB + d), SUB, EQ, ["CI", "UB%d" % d] + SBK, ["FM%d" % d], 96)
+        ts(blk(T.GL, d - 1, 8), col(0, 8), bit(2 ** lo, lambda a: (GREATER[t][a & 3] ^ d) >> lo & 1), bit(2 ** hi, lambda a: (GREATER[t][a & 3] ^ d) >> hi & 1),
+           SUB, EQ, ["col"] + SBK, ["GL%d" % d])
+        ts(T.RR[:, 16 * d - 16:16 * d - 8], T.col[:, 31:144:16], c1(CC, TB), None, EQ, None, ["col", "TB"], ["RRa%d" % d])
+        ts(T.RR[:, 16 * d - 8:16 * d], T.col[:, 31:144:16], c1(CC, TB + d), None, EQ, None, ["col", "TB"], ["RRb%d" % d])
+    for t in range(3):
+        lo, hi = [k for k in range(3) if k != t]
+        ts(blk(T.GL, 7 + t, 8), col(-2 ** t, 8), bit(2 ** lo, lambda a: GREATER[t][a & 3] >> lo & 1), bit(2 ** hi, lambda a: GREATER[t][a & 3] >> hi & 1),
+           SUB, EQ, ["col"] + SBK, ["GG%d" % t])
+    if LONG["f"]:
+        for d in range(1, 8):
+            cp("a", T.GB[:, 16 * d - 16:16 * d - 8], blk(T.GL, d - 1, 8), ["GL%d" % d], ["GBa%d" % d])
+            cp("a", T.GB[:, 16 * d - 8:16 * d], blk(T.GL, 7 + top(d), 8), ["GG%d" % top(d)], ["GBb%d" % d])
+        ts(blk(T.GB, 1, 112), blk(T.GB, 0, 112), 2.0, None, MUL, None, ["GB%s%d" % (x, d) for x in "ab" for d in range(1, 8)], ["GB2"])
+        ts(blk(T.GB, 2, 112), blk(T.GB, 1, 112), -1.0, None, MUL, None, ["GB2"], ["GB"])
+    onehot(T.EF[:], 0, 1.0, ["EF"])
+    for n, e in enumerate((2, 4, 6, 3, 5, 7)):
+        mk_b(2 + n, 1, c1(CC, RM + (e ^ 1) - 2), "RM")
     for m in range(3):
-        mk_b(2 + m, 1, c1(CC, RM + m), "RM")
-        mk_b(8 + m, 2 * m + 3, c1(CC, RM + 3), "RM")
-
-    def mk_fm(n, lo, hi, mask):
-        o = n * 192
-        if lo is None:
-            ts(T.FM[:, o:o + 192], T.col[:], c1(CC, hi), mask(0, 128), ALU.is_equal, ALU.mult, ["col", "TG", "NB"], ["FM%d" % n], 192)
-        else:
-            ts(T.FM[0:64, o:o + 192], T.col[0:64, :], CC[0:64, lo:lo + 1], mask(0, 64), ALU.is_equal, ALU.mult, ["col", "T64", "NB"], ["FM%da" % n], 192)
-            ts(T.FM[64:128, o:o + 192], T.col[64:128, :], CC[64:128, hi:hi + 1], mask(64, 128), ALU.is_equal, ALU.mult, ["col", "TG", "NB"], ["FM%d" % n], 192)
-
-    def notbit(k):
-        return lambda a, b: CC[a:b, NB + k:NB + k + 1]
-
-    for n, d in enumerate(ORDER):
-        mk_fm(n, None if d >= 4 else T64 + (d ^ 3), TG + d, notbit(d.bit_length() - 1))
-    mk_fm(7, T64 + 3, TG, lambda a, b: T.PF[a:b, 1:2])
-    memset(T.WM2[:], 0.0, 1024, ["WM2"])
-    memset(T.WM3[:], 0.0, 1024, ["WM3"])
-    memset(T.SS[:], 0.0, 80, ["SS%d" % k for k in range(5)])
-    ts(c1(CC, UU), c1(T.PF, 6), 8.0, None, ALU.add, None, ["PF"], ["UU"])
-    ts(T.E8[0:8, :], T.cgr[0:8, :], T.PF[0:8, 0:1], None, ALU.is_equal, None, ["cgr", "PF"], ["E8"], 128)
-    ts(T.GM[:], T.col[:, 0:24], c1(CC, UU), None, ALU.is_equal, None, ["col", "UU"], ["GM"])
-    alk = {0: [], 1: [], 2: [], 4: []}
-    alk[3] = alk[2]
-    wd = 128.0
-    for ph, m, k in ((0, 0, 0), (1, 0, 1), (1, 1, 1), (2, 0, 2), (2, 1, 2)):
-        a = AL + 4 * ph + 2 * m
-        alk[ph] += ["AL%d" % a, "AL%d" % (a + 1)]
-        ts(c1(CC, a), c1(T.PF, 1 + k), wd, wd, ALU.mult, ALU.add, ["PF"], ["AL%d" % a])
-        ts(c1(CC, a + 1), c1(T.PF, 1 + k), -wd, 2 * wd, ALU.mult, ALU.add, ["PF"], ["AL%d" % (a + 1)])
+        for n, (x, v) in enumerate(((2 * m + 2, -4.0), (2 * m + 3, -5.0))):
+            mk_b(17 + 2 * m + n, x, c1(CC, RM + 7 - n), "RM")
+            ts(blk(T.BM, 17 + 2 * m + n, 8), blk(T.BM, 17 + 2 * m + n, 8), v, 5.0, MUL, ADD, [], ["BM%d" % (17 + 2 * m + n)])
+    memset(T.SS[:], 0.0, ["SS" + p for p in PH], 160)
+    memset(c1(CC, ONE), 1.0, ["ONE"])
+    ts(c1(CC, KH3), KH, -3.0, None, ADD, None, ["PF"], ["KH3"])
+    ts(c1(CC, KK), K1, -2.0, K7, MUL, ADD, ["PF"], ["KKa"])
+    ts(c1(CC, KK + 1), K7, float(me), None, EQ, None, ["PF"], ["KKb"])
+    ts(c1(CC, KK + 2), I16, 3.0, 1.0, MUL, ADD, ["PF"], ["KKc"])
+    ts(T.KM[0:64, 0:128], T.cgr[0:64, :], PF[0:64, 6:7], None, EQ, None, ["cgr", "PF"], ["KM0"], 128)
+    ts(T.KM[0:64, 128:256], T.cgr[0:64, :], -1.0, CC[0:64, KK:KK + 1], ADD, EQ, ["cgr", "KKa"], ["KM1"], 128)
+    ts(T.KM[0:64, 256:384], T.cgr[0:64, :], 0.0, CC[0:64, KK + 1:KK + 2], MUL, ADD, ["cgr", "KKb"], ["KM2"], 128)
+    ts(CC[:, I3:I3 + 8], col(0, 8), 48.0, c1(CC, KK + 2), MUL, ADD, ["col", "KKc"], ["I3"])
+    memset(T.TH[:], 0.0, ["TH"])
+    memset(T.TH[:, 4:54:6], -0.5, ["TH"])
+    memset(T.TH[:, 5:54:6], -0.5, ["TH"])
+    for t in range(3):
+        for v in range(2):
+            f = t == 0 and v == 1
+            ts(c1(T.TH, 12 * t + 6 * v + 1), bit(1, lambda a: (a >> t & 1) == f), -0.5, None, MUL, None, SBK, ["TH"])
+            ts(c1(T.TH, 12 * t + 6 * v + 3), bit(1, lambda a: (a >> t & 1) != f), -0.5, None, MUL, None, SBK, ["TH"])
     for m in range(3):
-        lesser = me < (me ^ (2 * m + 3))
-        a = AL + 32 + 2 * m
-        memset(c1(CC, a), 384.0 if lesser else 768.0, 1, ["AL%d" % a])
-        memset(c1(CC, a + 1), 768.0 if lesser else 384.0, 1, ["AL%d" % (a + 1)])
-        alk[4] += ["AL%d" % a, "AL%d" % (a + 1)]
-    memset(T.TH[:], 0.0, 24, ["TH"])
-    memset(T.TH[:, 1::4], -0.5, 6, ["TH"])
-    ts(blk(T.H2, 7), T.col[:, 0:128], 16.0, None, ALU.mult, None, ["col"], ["H7"], 128)
-    ts(blk(T.LO, 7), T.col[:, 0:128], 0.0, KM16, ALU.mult, ALU.add, ["col", "PF"], ["L7"], 128)
-    ts(T.KM[:, 0:128], T.UT[:, 0:128], KM16, None, ALU.is_equal, None, utk + ["PF"], ["KM0"], 128)
-    for h in range(3):
-        ts(T.KM[:, 128 + 256 * h:384 + 256 * h], T.UT[:, 128 + 256 * h:384 + 256 * h], KM16, None, ALU.is_equal, None, utk + ["PF"], ["KM1%d" % h], 256)
+        memset(c1(T.TH, 36 + 6 * m + (1 if me < (me ^ (2 * m + 3)) else 3)), -0.5, ["TH"])
+    ts(blk(T.H2, 7), col(0, 128), 16.0, None, MUL, None, ["col"], ["Hid"])
+    ts(blk(T.LO, 7), col(0, 128), 0.0, I16, MUL, ADD, ["col", "PF"], ["Lid"])
     for m in range(3):
-        ts(blk(T.KM, 7 + m), blk(T.LO, 7), float(4 * m + u_of(max(me, me ^ (2 * m + 3)))), None, ALU.is_equal, None, ["L7"], ["KM2%d" % m], 128)
-    cp("v", T.OWN[:, 0:384], T.MP3[:], ["MP3"], ["OWNa"], 384)
+        cp("v", T.OWN[:, 384 * m:384 * m + 384:3], blk(T.MPB, 2 * m), ["MPB"], ["OW0%d" % m], 128)
 
-    def split(qs, src, key, k, n):
-        hk = ["H%d" % (k + i) for i in range(n)]
-        lk = ["L%d" % (k + i) for i in range(n)]
-        hb, h2 = blk(T.HB, k, 128, n), blk(T.H2, k, 128, n)
-        addc(qs, hb, src, 2056.5, key, ["HB%d" % k], 128 * n, False)
-        addc(qs, h2, hb, -2064.0, ["HB%d" % k], hk, 128 * n, True)
-        tt(blk(T.LO, k, 128, n), src, h2, ALU.subtract, key + hk, lk, 256 * n)
+    def X(d):
+        return blk(T.XA, d - 1) if d < 4 else blk(T.IB, d - 4)
 
-    def wrows(win, items, qs="s"):
-        mv = []
-        r = []
+    def xk(d):
+        return "XA%d" % (d > 1) if d < 4 else "IB"
+
+    def wrows(win, items, key, qs="s", r=()):
+        mv, r = [], list(r)
         for k, row in items:
-            mv += [(T[win][2 * row::16, :], blk(T.H2, k)), (T[win][2 * row + 1::16, :], blk(T.LO, k))]
-            r += ["H%d" % k, "L%d" % k]
-        dma(qs, mv, r, [win], 5e4)
+            mv += [(T[win][2 * row::16, :], blk(T.H2, POS[k])), (T[win][2 * row + 1::16, :], blk(T.LO, POS[k]))]
+            r += ["H%s" % k, "L%s" % k]
+        dma(qs, mv, r, key, 90e3 * len(mv))
 
-    def places(items, qs, dst, key):
-        s = slot("C")
-        for n, terms in enumerate(items):
-            mms = []
-            r = []
-            for k, x, par in terms:
-                j = pm[x, par]
-                mms += [(blk(T.PM, j), blk(T.H2, k)), (blk(T.PM, j + 1), blk(T.LO, k))]
-                r += ["PM%d" % j, "PM%d" % (j + 1), "H%d" % k, "L%d" % k]
-            pe([(ps(s, 0, 128, 128 * n, 128 * n + 128), a, b, i == 0, i == len(mms) - 1, 128) for i, (a, b) in enumerate(mms)], r, [s])
-        cp(qs, dst, ps(s, 0, 128, 0, 128 * len(items)), [], [s, key], 128 * len(items))
+    def places(s, n, k, x):
+        j = pm[x]
+        o = ps(s, 128 * n, 128 * n + 128)
+        pe([(o, blk(T.PM, j), blk(T.H2, POS[k]), 128), (o, blk(T.PM, j + 1), blk(T.LO, POS[k]), 128)], ["PM%d" % j, "PM%d" % (j + 1), "H%s" % k, "L%s" % k], [s])
 
-    def gather(qs, out, a, n, win, wk, lst, lk, wkey):
-        src = T[win][:, :].indirect(lst[:, a:a + n])
-        cp(qs, T[out][:, 16 * (a % 128):16 * (a % 128 + n)], src, wk + lk, wkey, int(16 * n * PAR["gat"]) + 60)
-
-    def gather2(out, a, win, wk, lst, lk, qs="va"):
+    def gather2(out, win, wk, lst, a, lk, name):
         for h in range(2):
-            gather(qs, out, a + 64 * h, 64, win, wk, lst, lk, ["%s_%d" % (out, h)])
+            cp(on(name + "ab"[h]), T[out][:, 1024 * h:1024 * h + 1024], T[win][:, :].indirect(lst[:, a + 64 * h:a + 64 * h + 64]), wk + [lk], ["%s_%d" % (out, h)],
+               int(1024 * PAR["gat"]) + 60)
+            call(name + "ab"[h])
 
-    def to_tile(rb, b, dst, key, more=(), mk=()):
+    def turn(rb, b, n):
         s = slot("C")
-        o = ps(s, 0, 128, 0, 128)
-        mms = [(T.BM[:, 144 * b + 15 - i:144 * b + 143 - i], T[rb][:, i::16]) for i in range(16)] + list(more)
-        pe([(o, a, c, i == 0, i == len(mms) - 1, 128) for i, (a, c) in enumerate(mms)], [rb + "_0", rb + "_1", "BM%d" % b] + list(mk), [s])
-        cp("va", dst, o, [], [s, key], 128)
+        mms = []
+        for i in range(16):
+            mms += [(ps(s, i, 128 * n, 128, 16), T[rb][:, i::16], blk(T.BM, b, 8, n) if b else T.BH[:], 64), None]
+        pe(mms[:-1], [rb + "_0", rb + "_1"] + ["BM%d" % (b + k) for k in range(n)], [s])
+        wide = b in PAR["wide"]
+        cp("a" if wide else "v", blk(T.ZF if wide else T.ZH, b, 128, n), ps(s, 0, 128 * n), [s], ["Z%d" % (b + k) for k in range(n)], 128 * n)
+        for k in range(n):
+            zt[b + k] = wide
+
+    zt = {}
+
+    def to_tile(b, more=(), mk=()):
+        s = slot("C")
+        o = ps(s, 0, 128)
+        pe([(o, blk(T.ZF, b), T.EF[:], 512) if zt[b] else (o, blk(T.ZH, b), blk(T.RT, 0), 128)] + [(o, a, c, 128) for a, c in more], ["Z%d" % b, "RT0", "EF"] + list(mk), [s])
+        return s, o
 
     def fcol(d, c):
-        n = ORDER.index(d)
-        return 64 * c if d == 1 else 192 + 576 * ((n - 1) // 3) + 192 * c + 64 * ((n - 1) % 3)
-
-    have = {d: [] for d in ORDER}
+        return 64 * (7 * c + d - 1)
 
     def lists(c, items):
         s = slot("C")
-        for n, it in enumerate(items):
-            d, tile, k, key = it[:4]
-            f = it[4] if len(it) > 4 else ORDER.index(d)
-            out = ps(s, 0, 128, 64 * n, 64 * n + 64)
-            pe([(out, T.FM[:, 192 * f + 64:192 * f + 192], tile[:, 128 * k:128 * k + 64], True, False, 256),
-                (out, T.FM[:, 192 * f:192 * f + 128], tile[:, 128 * k + 64:128 * k + 128], False, True, 256)], ["FM%d" % f, "FM%da" % f, key], [s])
-        ds = [it[0] for it in items]
-        n = 0
-        while n < len(ds):
-            m = 1 if ds[n] < 4 else len(ds) - n
-            a = fcol(ds[n], c)
-            so = c1(CC, SO + 1) if ds[n] in (2, 3) else 0.0
-            ts(T.FLu[:, a:a + 64 * m], ps(s, 0, 128, 64 * n, 64 * (n + m)), so, None, ALU.add, None, ["SO"],
-               [s] + ["FLu%d%d" % (d, c) for d in ds[n:n + m]], 64 * m)
-            n += m
-        for o in range(3):
-            n = 0
-            while n < len(ds):
-                m = 0
-                while n + m < len(ds) and o in have[ds[n + m]]:
-                    m += 1
-                if m:
-                    a, b = fcol(ds[n], o), fcol(ds[n], 3 - c - o)
-                    tt(T.NE[:, b:b + 64 * m], ps(s, 0, 128, 64 * n, 64 * (n + m)), T.FLf[:, a:a + 64 * m], ALU.not_equal,
-                       ["FLf%d%d" % (d, o) for d in ds[n:n + m]], [s] + ["NE%d%d" % (d, 3 - c - o) for d in ds[n:n + m]], 64 * m)
-                n += max(m, 1)
-        keep = [n for n, d in enumerate(ds) if len(have[d]) < 2]
-        if keep:
-            n, m = keep[0], keep[-1] - keep[0] + 1
-            a = fcol(ds[n], c)
-            cp("va", T.FLf[:, a:a + 64 * m], ps(s, 0, 128, 64 * n, 64 * (n + m)), [], [s] + ["FLf%d%d" % (d, c) for d in ds[n:n + m]], 64 * m)
-        for d in ds:
-            have[d].append(c)
+        for n, (d, tile, key) in enumerate(items):
+            o = ps(s, 64 * n, 64 * n + 64)
+            f = 192 * (d - 1)
+            pe([(o, T.FM[:, f + 64:f + 192], tile(0), 64), (o, T.FM[:, f:f + 128], tile(64), 64)], ["FM%d" % d, key], [s])
+        a = fcol(items[0][0], c)
+        t = top(items[0][0])
+        ts(T.FL[:, a:a + 64 * len(items)], ps(s, 0, 64 * len(items)), bit(2048, lambda g: 1 - GREATER[t][g & 3] % 2) if t else 0.0, None, ADD, None,
+           [s] + SBK, ["FL%d%d" % (it[0], c) for it in items], 64 * len(items))
 
-    def acol(d, c):
-        return 3 * ORDER.index(d) + c
+    def half(t, k):
+        return lambda a: t[:, 128 * k + a:128 * k + a + 64]
+
+    def xhalf(d):
+        return half(T.XA, d - 1) if d < 4 else half(T.IB, d - 4)
 
     def judge(d, c):
-        t, s = slot("T"), slot("D")
+        t = "T%d" % (3 * d + c - 3)
         a = fcol(d, c)
-        wn = "W1" if d == 1 else "W"
-        src = T[wn][:, :].indirect(T.FLu[:, a:a + 64])
-        n = ORDER.index(d)
-        cost = int(1024 * PAR["gat"]) + 60
-        act = (d, c) in ON_ACT
-        if act:
-            cp("a", tb(t, 0, 1024), src, [wn, "FLu%d%d" % (d, c)], [t], cost)
-        else:
-            tt(tb(t, 0, 1024), src, blk(T.FR, n, 1024), ALU.subtract, [wn, "FLu%d%d" % (d, c), "FR%d" % d], [t], cost)
-        mms = []
-        for o, k in ((0, 512), (512, 511), (1023, 1)):
-            out = ps(s, 0, 128, o, o + k)
-            nx = o + 1 if k > 1 else 0
-            terms = [(EYE, tb(t, o, o + k)), (NEG if k > 1 else SWP, tb(t, nx, nx + k))]
+        wn = "W%d" % (d > 1)
+        act = on("g%d%d" % (d, c)) == "a"
+        f = 1024 * d - 1024
+        for x, y, w in ((0, 34, "a"), (34, 64, "b")) if 10 * d + c in PAR["cut"] else ((0, 64, "ab"),):
+            src, cost, w = T.W[:, 0:4096 if d > 1 else 2048].indirect(T.FL[:, a + x:a + y]), int(16 * (y - x) * PAR["gat"]) + 60, [t + k for k in w]
             if act:
-                f = 1024 * n
-                terms += [(NEG, T.FR[:, f + o:f + o + k]), (EYE if k > 1 else blk(T.PM, 19), T.FR[:, f + nx:f + nx + k])]
-            mms += [(out, x, y, i == 0, i == len(terms) - 1, max(k, 64)) for i, (x, y) in enumerate(terms)]
-        pe(mms, [t, "PMd0", "PMd1", "PMd2"] + (["PMd3", "FR%d" % d] if act else []), [s])
-        node("op", {"a": cyc(1024) + 0.02}, lambda q: g.scalar.activation(blk(T.JK, int(val[s][1:]), 1024), z(ps(s, 0, 128, 0, 1024)), ACT.Abs, accum_out=c1(T.AC, acol(d, c))),
-             [], [s, "AC%d%d" % (d, c)])
+                cp("a", tb(t, 16 * x, 16 * y), src, [wn, "FL%d%d" % (d, c)], w, cost)
+            else:
+                tt(tb(t, 16 * x, 16 * y), src, T.FR[:, f + 16 * x:f + 16 * y], SUB, [wn, "FL%d%d" % (d, c), "FR%d" % d], w, cost)
+            if x == 0:
+                call("g%d%d" % (d, c))
+        for h, parts in enumerate((((0, 512),), ((512, 511), (1023, 1)))):
+            s, mms = slot("C"), []
+            for o, k in parts:
+                nx, out, n = o + 1 if k > 1 else 0, ps(s, o - 512 * h, o - 512 * h + k), max(k, 64)
+                if act:
+                    mms += [(out, NEG, T.FR[:, f + o:f + o + k], n), (out, EYE if k > 1 else SWQ, T.FR[:, f + nx:f + nx + k], n)]
+                mms += [(out, EYE, tb(t, o, o + k), n), (out, NEG if k > 1 else SWP, tb(t, nx, nx + k), n), None]
+            pe(mms[:-1], [t + "a", "EYE", "NEG", "SWP", "SWQ", "FR%d" % d] + [t + "b"] * h, [s])
+            size(s, c1(T.AC, 6 * d + 2 * c + h - 6), "s%d%d" % (d, c), "AC%d%d%d" % (d, c, h))
+            call("st"[h] + "%d%d" % (d, c))
 
-    def counts(ph, ds):
+    def size(s, acc, name, key):
+        def f(q):
+            if q == "v":
+                return V.tensor_reduce(acc, z(ps(s, 0, 512)), AxisListType.X, ADD, apply_absolute_value=True)
+            return g.scalar.activation(blk(T.JK, POOLS["C"].index(val[s]), 512), z(ps(s, 0, 512)), ACT.Abs, accum_out=acc)
+        node("op", {on(name): cyc(512) + 0.02}, f, [s], [key])
+
+    def tile_out(s, o, d, c, dst, key, other, okey):
+        cp("v", blk(*dst), o, [s], [key], 128)
+        tt(blk(T.NE, 2 * d + c - 3), o, other, ALU.not_equal, [s, okey], ["NE%d%d" % (d, c)], 128)
+        lists(c, [(d, half(*dst), key)])
+
+    def counts(d):
         s = slot("C")
-        for c in range(3):
-            pe([(ps(s, 0, 16, 64 * c, 64 * c + 64), blk(T.GW, ORDER.index(d), 16), T.NE[:, fcol(d, c):fcol(d, c) + 64], n == 0, n == len(ds) - 1, 64)
-                for n, d in enumerate(ds)], ["GW%d" % d for d in ds] + ["NE%d%d" % (d, c) for d in ds], [s])
-        for c in range(3):
-            red(T.WQ[0:16, 4 * ph + c:4 * ph + c + 1], ps(s, 0, 16, 64 * c, 64 * c + 64), s, "WQ%d%d" % (ph, c))
-
-    def red(o, i, s, key):
-        node("op", {"v": cyc(64)}, lambda q: g.vector.tensor_reduce(o, z(i), AxisListType.X, ALU.add), [], [s, key])
+        a = 16 * d - 16
+        pe([(ps(s, 0, 8), blk(T.NE, 2 * d - 1), T.GW[:, a:a + 8], 64), None, (ps(s, 8, 24), blk(T.NE, 2 * d - 2), T.GW[:, a:a + 16], 64)],
+           ["NE%d1" % d, "NE%d2" % d, "GW%d" % d], [s])
+        cp("va", blk(T.CW, d - 1, 24), ps(s, 0, 24), [s], ["CW%d" % d])
 
     def scores(ph, ds):
+        a = 32 * PH.index(ph)
+        k = "SS" + ph
+        for m, d in enumerate(ds):
+            s = slot("C")
+            gl, gg = blk(T.GL, d - 1, 8), blk(T.GL, 7 + top(d), 8)
+            mms = []
+            for c, (x, y, w) in enumerate(((0, 0, 0), (1, 2, 16), (2, 1, 8))):
+                o = ps(s, 3 * m + c, 3 * m + c + 1, 8)
+                mms += [(o, T.CW[:, 24 * d - 24 + w:24 * d - 16 + w], c1(CC, ONE), 32)]
+                mms += [(o, a, c1(T.AC, 6 * d - 6 + 2 * u + h), 32) for a, u in ((gl, x), (gg, y)) for h in range(2)] + [None]
+            pe(mms[:-1], ["CW%d" % d, "ONE", "GL%d" % d, "GG%d" % top(d)] + ["AC%d%d%d" % (d, c, h) for c in range(3) for h in range(2)], [s])
+            b = 3 * m
+            for n, (i0, i1, st, sc) in enumerate(((b, b + 3, 2, b + 1), (b, b + 2, 1, b + 2), (b + 1, b + 3, 1, b))):
+                ts(T.SS[0:8, a + 6 * m + 2 * n:a + 6 * m + 2 * n + 2], ps(s, i0, i1, 8, st), ps(s, sc, sc + 1, 8), None, SUB, None, [s, k], [k + "%d%d" % (m, n)])
+        ld = "LdS" + ph
+        dma("s", [(T[ld][me], T.SS[0:8, a:a + 32])], [k] + [k + "%d%d" % (m, n) for m in range(len(ds)) for n in range(3)], [ld], 1e3)
+        exchange("S" + ph, [ld], PAR["S"])
+        dma("s", [(T.SC[0:64, a:a + 32], T[ld][:])], [ld, "arS" + ph], ["SC" + ph], 8e3)
+
+    def decide(ph, views, th):
         s = slot("C")
-        o = ps(s, 0, 16, 0, 3)
-        pe([(o, T.GM[:, 8 - 4 * n:24 - 4 * n], T.AC[:, acol(d, 0):acol(d, 0) + 3], n == 0, n == len(ds) - 1, 64) for n, d in enumerate(ds)],
-           ["GM"] + ["AC%d%d" % (d, c) for d in ds for c in range(3)], [s])
-        a = 16 * ph
-        k = "SS%d" % ph
-        S = T.SS
-        tt(S[0:16, a + 8:a + 11], o, T.WQ[0:16, 4 * ph:4 * ph + 3], ALU.add, ["WQ%d%d" % (ph, c) for c in range(3)], [s, k])
-        ts(S[0:16, a:a + 2], S[0:16, a + 8:a + 11:2], S[0:16, a + 9:a + 10], None, ALU.subtract, None, [k], [k + "a"])
-        ts(S[0:16, a + 2:a + 4], S[0:16, a + 8:a + 10], S[0:16, a + 10:a + 11], None, ALU.subtract, None, [k], [k + "b"])
-        ld = "LdS%d" % (ph + 1)
-        dma("s", [(rows(T[ld]), S[0:16, a:a + 16])], [k, k + "a", k + "b"], [ld], 1e3)
-        exchange("S%d" % (ph + 1), lambda a, h: rows(T[ld]), lambda h: rows(T[ld]), [ld], ld, 2.5)
-        dma("s", [(T.SC[:, 16 * ph:16 * ph + 16], T[ld][:])], [ld], ["SC%d" % ph], 8e3)
+        a = 32 * PH.index(ph)
+        mms, n = [], 0
+        for km, w in views:
+            mms += [(ps(s, n, n + w), T.KM[0:64, 128 * km:128 * km + 128], T.SC[0:64, a:a + w], 256), None]
+            n += w
+        pe(mms[:-1], ["SC" + ph, "KM0", "KM1", "KM2"], [s])
+        tt(T.DE[:, a:a + n], ps(s, 0, n), T.TH[:, th:th + n], GT, [s, "TH"], ["x" + ph])
+        tt(T.DE[:, a + 20:a + 20 + n // 2], T.DE[:, a:a + n:2], T.DE[:, a + 1:a + n:2], MUL, ["x" + ph], ["y" + ph])
+        return (lambda i: c1(T.DE, a + 20 + i)), "y" + ph
 
-    def decide(ph):
-        n = (1, 2, 2, 2, 3)[ph]
-        k0 = (0, 1, 3, 5, 7)[ph]
-        al = AL + (0, 4, 8, 8, 32)[ph]
-        kk = (["KM0"], ["KM10"], ["KM11"], ["KM12"], ["KM20", "KM21", "KM22"])[ph]
+    def pick(out, win, m, ind, i, key, r, w):
+        ts(blk(T.OF, m, 8), CC[:, I3:I3 + 8], ind(i + 1), ind(i + 2), ADD, SUB, ["I3", key], ["OF%d" % m])
+        cp("va" if m else "v", out, win.indirect(blk(T.OF, m, 8)), r + ["OF%d" % m], w, int(128 * PAR["gat"]) + 60)
+
+    nsc = [0]
+
+    def scaled(tile, tk, ind, key):
+        n = nsc[0]
+        nsc[0] += 1
+        ts(blk(T.SCL, n), tile, ind, None, MUL, None, [tk, key], ["SCL%d" % n])
+        return blk(T.SCL, n), "SCL%d" % n
+
+    def final(d, n, terms):
         s = slot("C")
-        pe([(ps(s, 0, 128, 4 * m, 4 * m + 4), blk(T.KM, k0 + m), T.SC[:, 16 * ph:16 * ph + 4], True, True, 256) for m in range(n)],
-           ["SC%d" % ph] + kk, [s])
-        b = 96 * ph
-        DE = T.DE
-        k = ["x%d%d" % (ph, i) for i in range(4)]
-        tt(DE[:, b:b + 4 * n], ps(s, 0, 128, 0, 4 * n), T.TH[:, 0:4 * n], ALU.is_gt, ["TH"], [s, k[0]])
-        tt(DE[:, b + 24:b + 24 + 2 * n], DE[:, b:b + 4 * n:2], DE[:, b + 1:b + 4 * n:2], ALU.mult, [k[0]], [k[1]])
-        tt(DE[:, b + 48:b + 48 + 2 * n], DE[:, b + 24:b + 24 + 2 * n], CC[:, al:al + 2 * n], ALU.mult, [k[1]] + alk[ph], [k[2]])
-        if ph < 4:
-            tt(DE[:, b + 72:b + 72 + n], DE[:, b + 48:b + 48 + 2 * n:2], DE[:, b + 49:b + 48 + 2 * n:2], ALU.add, [k[2]], [k[3]])
-            n = 1
-        for m in range(n):
-            ts(T.OF[:, 24 * ph + 8 * m:24 * ph + 8 * m + 8], T.ID[:, 8 * m:8 * m + 8], c1(DE, b + 48 + 2 * m), c1(DE, b + 49 + 2 * m), ALU.add, ALU.add,
-               ["ID", k[2]], ["OF%d%d" % (ph, m)])
-        return T.OF[:, 24 * ph:24 * ph + 8 * n], ["OF%d%d" % (ph, m) for m in range(n)], b + 72, k[3]
+        pe([(ps(s, 0, 128), blk(T.RT, 0), t, 128) for t, k in terms], ["RT0"] + [k for t, k in terms], [s])
+        cp("va", blk(T.FIN, n), ps(s, 0, 128), [s], ["FIN%d" % d], 128)
+        y, k = "Y%d" % (n // 2), 64 * (n % 2)
+        st, ld = T["St" + y], T["Ld" + y]
+        dma("s", [(st[:, k:k + 64, :], blk(T.FIN, n)), (ld[me, k:k + 64, :], T.FIN[mine, 128 * n:128 * n + 128])], ["FIN%d" % d], ["StY%d" % d], 70e3)
+        if k:
+            ds = (d - 2 + (d == 2), d)
+            exchange(y, ["StY%d" % e for e in ds], PAR["Y"])
+            dma("s", [(blk(T.ym, e - 1), ld[:, 64 * i:64 * i + 64, :]) for i, e in enumerate(ds)], ["StY%d" % e for e in ds] + ["ar" + y], ["ym%d" % d], 131e3)
 
-    def fr_fill(d):
-        n = ORDER.index(d)
-        mv = []
-        for h in range(2):
-            for u, cnt, v, s in runs([lam_of(r_of(d, u)) for u in range(4)]):
-                mv.append((T.FR[64 * h + 16 * u:64 * h + 16 * (u + cnt), 1024 * n:1024 * n + 1024],
-                           T.LdF[2 * v + h:2 * (v + s * (cnt - 1)) + h + 1:2 * s]))
-        dma("s", mv, ["LdF"], ["FR%d" % d], 262e3)
+    def home(name, a, b):
+        st, ld = T["St" + name], T["Ld" + name]
+        ks = ["%s%d" % (x, 2 * m + 3) for m in range(a, b) for x in "AB"]
+        dma("s", [(st[:], T.C3[:, 256 * a:256 * b]), (ld[me], T.C3[mine, 256 * a:256 * b])], ks, ["St" + name], 70e3 * (b - a))
+        exchange(name, ["St" + name], PAR[name])
+        dma("s", [(T.OL[:, 256 * a:256 * b], ld[:])], ["St" + name, "ar" + name], ["OL" + name], 65e3 * (b - a))
+        for m in range(a, b):
+            for c in range(2):
+                cp("v", T.OWN[:, 384 * m + 1 + c:384 * m + 384:3], blk(T.OL, 2 * m + c), ["OL" + name], ["OW%d%d" % (c + 1, m)], 128)
 
-    def pick(out, win, off, n, r, w):
-        cp("v", out, win.indirect(off), r, w, int(n * PAR["gat"]) + 60)
+    def feats(dst, o, ranks, hs):
+        return [(dst[64 * b + 16 * u:64 * b + 16 * (u + cnt), o + 1024 * i:o + 1024 * i + 1024], T.LdF[2 * v + h:2 * (v + s * (cnt - 1)) + h + 1:2 * s])
+                for b in range(2) for i, h in enumerate(hs(b)) for u, cnt, v, s in runs(ranks)]
 
-    def home(name, src, r, lat, dst, key, nbytes):
-        st, ld = "St" + name, "Ld" + name
-        dma("s", [(T[st][:], src)], r, [st], nbytes)
-        dma("s", [(rows(T[ld]), rows(T[st]))], [st], [ld], nbytes / 8)
-        exchange(name, lambda a, h: rows(T[st], a), lambda h: rows(T[ld]), [st], ld, lat)
-        dma("s", [(dst, T[ld][:])], [ld], [key], nbytes)
-
-    dma("s", [(T.IA[:], T.LdA[:])], ["LdA"], ["IA"], 196e3)
-    split("v", T.IA[:, 128:384], ["IA"], 1, 2)
-    wrows("WM1", [(1, 0), (2, 1)], "sa")
-    places([[(1, 2, 0), (2, 3, 0)]], "v", blk(T.LQ, 0), "LQ0")
-    places([[(1, 2, 1), (2, 3, 1)]], "v", blk(T.LQ, 1), "LQ1")
-    split("v", T.IA[:, 0:128], ["IA"], 0, 1)
-    cp("v", blk(T.CAT1, 0), blk(T.IA, 0), ["IA"], ["I1"], 128)
-    lists(0, [(1, T.CAT1, 0, "I1")])
-    cp("v", blk(T.CAT2, 0), blk(T.IA, 1), ["IA"], ["I2"], 128)
-    cp("v", blk(T.CAT3, 0), blk(T.IA, 2), ["IA"], ["I3"], 128)
-    dma("s", [(T.W[64 * b:64 * b + 64, 2048 * s + 1024 * h:2048 * s + 1024 * h + 1024], T.LdF[8 * (1 - s) + h:8 * (2 - s):2])
-              for s in range(2) for h in range(2) for b in range(2)], ["LdF"], ["W"], 1048e3)
-    dma("sa", [(T.W1[64 * b + 16 * u:64 * b + 16 * (u + cnt), 1024 * h:1024 * h + 1024], T.LdF[2 * v + h:2 * (v + s * (cnt - 1)) + h + 1:2 * s])
-               for h in range(2) for b in range(2) for u, cnt, v, s in runs([lam_of(r_of(1, u) ^ 1) for u in range(4)])], ["LdF"], ["W1"], 524e3)
-    for d in ORDER:
-        fr_fill(d)
-    gather2("RA", 0, "WM1", ["WM1"], T.LQ, ["LQ0"])
-    gather2("RB", 128, "WM1", ["WM1"], T.LQ, ["LQ1"])
-    to_tile("RA", 0, blk(T.X12, 0), "X1")
-    lists(1, [(1, T.X12, 0, "X1")])
-    lists(2, [(1, T.X12, 0, "X1", 7)])
-    to_tile("RB", 1, blk(T.X12, 1), "X2")
+    stage(1)
+    dma("s", [(blk(T.IA, 1 + k), T.LdA[:, 64 * k:64 * k + 64, :]) for k in range(2)], ["LdA", "arA"], ["IA1"], 131e3)
+    dma("a", [(T.WI[0::16, :], T.LdA[:, 64:128, :])], ["LdA", "arA"], ["WI"], 65e3)
+    dma("s", [(blk(T.IA, 0), T.LdE[:])], ["LdA", "arE"], ["IA0"], 65e3)
+    for a, n, ds in ((1, 2, (2, 3)), (0, 1, (1,))):
+        addc("v", blk(T.HB, a, 128, n), blk(T.IA, a, 128, n), 2056.5, ["IA%d" % a], ["HB%d" % a], 128 * n, False)
+        ts(blk(T.AN, a, 128, n), blk(T.IA, a, 128, n), 15, None, ALU.bitwise_and, None, ["IA%d" % a], ["AN%d" % a], 128 * n)
+        cp("v", blk(T.XA, a, 128, n), blk(T.IA, a, 128, n), ["IA%d" % a], ["XA%d" % a], 128 * n)
+        addc("va", blk(T.H2, a, 128, n), blk(T.HB, a, 128, n), -2064.0, ["HB%d" % a], ["H%d" % d for d in ds], 128 * n, True)
+        cp("v", blk(T.LO, a, 128, n), blk(T.AN, a, 128, n), ["AN%d" % a], ["L%d" % d for d in ds], 128 * n)
+    wrows("WM2", [("id", 6)], ["WM2c"], "s", ["WM2"])
+    wrows("WM2", [(2, 0)], ["WM1a", "~wm"], "s", ["WM2"])
+    wrows("WM2", [(3, 1)], ["WM1b"], "a", ["WM2"])
     s = slot("C")
-    for n in range(2):
-        pe([(ps(s, 0, 128, 128 * n, 128 * n + 128), blk(T.RX, 3 + 2 * n + i), blk(T.X12, i), i == 0, i == 1, 512) for i in range(2)],
-           ["X1", "X2", "RX%d" % (3 + 2 * n), "RX%d" % (4 + 2 * n)], [s])
-    cp("va", T.CAT1[:, 128:384], ps(s, 0, 128, 0, 256), [], [s, "QAB"], 256)
-    dma("s", [(T.IB[:], T.LdB[:])], ["LdB"], ["IB"], 262e3)
-    dma("s", [(T.L8[0:8, 0:7], T.LdL[:, 0, :])], ["LdL"], ["L8"], 1e3)
-    for c in range(3):
+    places(s, 0, 2, 2)
+    places(s, 1, 3, 3)
+    cp("v", T.LQ[:, 0:256], ps(s, 0, 256), [s], ["LQ23"], 256)
+    dma("s", [(T.IB[:], T.LdB[:])], ["StB", "arB"], ["IB"], 135e3)
+    stage("w0")
+    dma("s", feats(T.W, 0, GREATER[0], lambda b: (0, 1)), ["LdF", "arF", "~wm"], ["W0"], 524e3)
+    stage("w1")
+    dma("s", feats(T.W, 2048, [7 - j for j in GREATER[0][:3]], lambda b: (0, 1)), ["LdF", "arF", "~wm"], ["Wy"], 393e3)
+    node("nop", {"g": 0.0}, None, ["W0", "Wy"], ["W1"])
+    for d in range(1, 8):
+        stage("f%d" % d)
+        dma("s", feats(T.FR, 1024 * d - 1024, [j ^ d for j in GREATER[top(d)]], lambda b: (b,)), ["LdF", "arF", "~wm"], ["FR%d" % d], 262e3)
+    stage(10)
+    for h in range(2):
+        cp("v", blk(T.RA, h, 1024), T.WI[:, :].indirect(blk(T.LQ, h, 64)), ["WI", "LQ23"], ["RA_%d" % h], int(1024 * PAR["gat"]) + 60)
+    gather2("RB", "WM2", ["WM1a", "WM1b", "WM2c", "WM2b"], T.LQ, 128, "LQ23", "B")
+    for c, (rb, k, dst) in enumerate((("RA", "A", (T.NT, 1)), ("RB", "B", (T.FT, 1)))):
+        turn(rb, c, 1)
+        s, o = to_tile(c)
+        tile_out(s, o, 1, c + 1, dst, "NF"[c] + "1", (X(1), blk(T.NT, 1))[c], ("XA0", "N1")[c])
+        addc("va", blk(T.HB, POS[k]), o, 2056.5, [s], ["HB" + k], 128, False)
+        addc("va", blk(T.H2, POS[k]), blk(T.HB, POS[k]), -2064.0, ["HB" + k], ["H" + k], 128, True)
+        tt(blk(T.LO, POS[k]), o, blk(T.H2, POS[k]), SUB, [s, "H" + k], ["L" + k], 128)
+    lists(0, [(1, xhalf(1), "XA0")])
+    lists(0, [(d, xhalf(d), "XA1") for d in (2, 3)])
+    lists(0, [(d, xhalf(d), "IB") for d in (4, 5, 6, 7)])
+    ts(T.WF[:, 0:7], T.IB[:, 512:519], -1.0, None, MUL, None, ["IB"], ["WF"])
+
+    def weigh(d):
+        def f(q):
+            if q == "v":
+                return V.tensor_scalar(blk(T.GW, d - 1, 16), blk(T.RR, d - 1, 16), c1(T.WF, d - 1), None, MUL)
+            return g.scalar.activation(blk(T.GW, d - 1, 16), blk(T.RR, d - 1, 16), ACT.Copy, scale=c1(T.WF, d - 1))
+        node("op", {"v": cyc(1), "a": cyc(1)}, f, ["RRa%d" % d, "RRb%d" % d, "WF"], ["GW%d" % d])
+
+    for d in range(1, 8):
+        weigh(d)
+    addc("v", blk(T.HB, 3, 128, 4), T.IB[:, 0:512], 2056.5, ["IB"], ["HB3"], 512, True)
+    addc("va", blk(T.H2, 3, 128, 4), blk(T.HB, 3, 128, 4), -2064.0, ["HB3"], ["H4", "H5", "H6", "H7"], 512, True)
+    s = slot("C")
+    pe([(ps(s, 0, 512), blk(T.RT, 0), T.IB[:, 0:512], 512), (ps(s, 0, 512), NEG, blk(T.H2, 3, 128, 4), 512)], ["RT0", "NEG", "IB", "H4", "H5", "H6", "H7"], [s])
+    cp("va", blk(T.LO, 3, 128, 4), ps(s, 0, 512), [s], ["L4", "L5", "L6", "L7"], 512)
+    stage("r1")
+    for c in (1, 2, 0):
         judge(1, c)
-    split("va", T.CAT1[:, 128:384], ["QAB"], 3, 2)
-    wrows("WM1", [(0, 2), (3, 3), (4, 4)])
-    cp("v", T.L8f[0:8, 0:7], T.L8[0:8, 0:7], ["L8"], ["L8f"])
-    s = slot("C")
-    pe([(ps(s, 0, 128, 0, 7), T.E8[0:8, :], T.L8f[0:8, 0:7], True, True, 256)], ["E8", "L8f"], [s])
-    cp("va", T.Wp[:, 0:7], ps(s, 0, 128, 0, 7), [], [s, "Wp"])
-    s = slot("C")
-    pe([(ps(s, 0, 128, n, n + 1), T.FM[:, 192 * n + 64 * (1 - h):192 * n + 64 * (1 - h) + 128], c1(T.Wp, d - 1), h == 0, h == 1, 256)
-        for n, d in enumerate(ORDER) for h in range(2)], ["Wp"] + ["FM%d%s" % (n, x) for n in range(7) for x in ("", "a")], [s])
-    cp("va", T.Wf[:, 0:7], ps(s, 0, 128, 0, 7), [], [s, "Wf"])
-    for n, d in enumerate(ORDER):
-        o = 8 - 4 * max(n - 4, 0)
-        ts(blk(T.GW, n, 16), T.GM[:, o:o + 16], c1(T.Wf, n), -1.0, ALU.mult, ALU.mult, ["GM", "Wf"], ["GW%d" % d])
-    counts(0, [1])
-    scores(0, [1])
+    counts(1)
+    scores("1", [1])
 
-    for m in range(2):
-        cp("v", blk(T.CAT3, 1 + m), blk(T.IB, 1 + 2 * m), ["IB"], ["I%d" % (5 + 2 * m)], 128)
-        cp("v", blk(T.CAT2, 3 + 3 * m), blk(T.IB, 2 * m), ["IB"], ["I%d" % (4 + 2 * m)], 128)
-    places([[(2, 3, 0), (2, 3, 1)]], "v", blk(T.LF2, 0), "LF20")
-    split("va", T.CAT3[:, 128:384], ["I5", "I7"], 5, 2)
-    places([[(5, 5, 2)], [(6, 7, 2)]], "v", T.LF2[:, 128:384], "LF21")
-    wrows("WM2", [(2, 0), (5, 1), (6, 2), (7, 3)])
+    stage(10)
+    wrows("WM3", [(1, 2)], ["WM3a"], "s", ["WM3"])
+    wrows("WM3", [("A", 3), ("B", 4)], ["WM3b"], "s", ["WM3"])
+    stage("wm")
+    wrows("WM2", [(4, 2), (5, 3), (6, 4), (7, 5)], ["WM2b"], "s", ["WM2"])
+    stage(10)
+    s = slot("C")
+    places(s, 0, 5, 5)
+    places(s, 1, 7, 7)
+    cp("v", T.LQ[:, 256:512], ps(s, 0, 256), [s], ["LQ57"], 256)
+    stage(13)
+    s = slot("C")
+    for c, k in enumerate((1, "A", "B")):
+        places(s, c, k, 1)
+    for c in range(3):
+        cp("a", T.PI1[:, c:384:3], ps(s, 128 * c, 128 * c + 128), [s], ["PI1%d" % c], 128)
     for m in range(3):
-        gather2("RF%d" % m, 128 * m, "WM1", ["WM1"], T.LF2, ["LF2%d" % min(m, 1)])
-    lists(0, [(2 * m + 2, T.CAT2, 3 * m, "I%d" % (2 * m + 2)) for m in range(3)])
-    places([[(0, 1, 2)], [(4, 1, 2)], [(3, 1, 2)]], "va", T.PI1[:], "PI1t")
-    for d in (2, 4, 6):
+        stage("rf%d" % m)
+        gather2("RF%d" % m, "WM3", ["WM3a", "WM3b"], T.LQ, 128 + 128 * m, "LQ57" if m else "LQ23", "F%d" % (2 * m + 2))
+    for d in (2, 4, 6, 3, 5, 7):
+        stage("c%d" % d)
         judge(d, 0)
-    split("va", blk(T.CAT2, 3), ["I4"], 8, 1)
-    split("va", blk(T.CAT2, 6), ["I6"], 9, 1)
-    wrows("WM3", [(1, 0), (8, 1), (9, 2)])
 
-    off, ok, oc, okey = decide(0)
-    pick(T.LN[:], T.PI1[:, :], off, 128, ["PI1t"] + ok, ["LN"])
-    ts(c1(T.DE, 88), c1(T.DE, oc), 1.0 / 128, c1(CC, KHM + 2), ALU.mult, ALU.is_equal, [okey, "KHM"], ["sel"])
-    gather2("RN", 0, "WM2", ["WM2"], T.LN, ["LN"])
-    for m in range(3):
-        mk_b(11 + m, 2 * m + 3, c1(T.DE, 88), "sel")
-        to_tile("RF%d" % m, 11 + m, blk(T.CAT2, 3 * m + 2), "F%d" % (2 * m + 2))
-        lists(2, [(2 * m + 2, T.CAT2, 3 * m + 2, "F%d" % (2 * m + 2))])
+    stage("rn")
+    ind, key = decide("1", [(0, 6), (1, 6)], 0)
+    pick(T.LN[:], T.PI1[:, :], 0, ind, 3, key, ["PI10", "PI11", "PI12"], ["LN"])
+    gather2("RN", "WM2", ["WM1a", "WM1b", "WM2b", "WM2c"], T.LN, 0, "LN", "N")
+    ts(c1(T.DE, 28), ind(1), ind(2), c1(CC, KH3), SUB, EQ, [key, "KH3"], ["sel"])
+    dma("s", [(T.RB[12 + i::16, :], T.RN[12 + i::16, :]) for i in range(2)]
+        + [(T.RB[16 * (1 - b) + 14 + i::32, :], T.RN[16 * b + 12 + i::32, :]) for b in range(2) for i in range(2)], ["RN_0", "RN_1"], ["RB_0", "RB_1"], 131e3)
+    turn("RN", 2, 3)
     for m in range(3):
         d = 2 * m + 2
-        to_tile("RN", 2 + m, blk(T.CAT2, 3 * m + 1), "N%d" % d)
-        lists(1, [(d, T.CAT2, 3 * m + 1, "N%d" % d)])
+        stage("t%d" % d)
+        mk_b(8 + m, d + 1, c1(T.DE, 28), "sel")
+        turn("RF%d" % m, 8 + m, 1)
+        s, o = to_tile(8 + m)
+        cp("v", blk(T.FT, d), o, [s], ["F%d" % d], 128)
+        lists(2, [(d, half(T.FT, d), "F%d" % d)])
+        s, o = to_tile(2 + m)
+        tile_out(s, o, d, 1, (T.NT, d), "N%d" % d, X(d), xk(d))
+        tt(blk(T.NE, 2 * d - 1), o, blk(T.FT, d), ALU.not_equal, [s, "F%d" % d], ["NE%d2" % d], 128)
+        counts(d)
+        stage("j%d" % d)
         judge(d, 2)
         judge(d, 1)
-        counts(1 + m, [d])
-        scores(1 + m, [d])
-    pick(blk(T.FIN, 0), T.CAT1[:, :], off, 128, ["I1", "QAB"] + ok, ["FIN0"])
-
-    for m in range(3):
-        split("va", blk(T.CAT2, 3 * m + 2), ["F%d" % (2 * m + 2)], 10 + m, 1)
-    wrows("WM3", [(10, 3), (11, 4), (12, 5)])
-    gather2("RA", 0, "WM3", ["WM3"], T.LN, ["LN"])
-    lists(0, [(2 * m + 3, T.CAT3, m, "I%d" % (2 * m + 3)) for m in range(3)])
+        stage("s%d" % d)
+        scores(str(d), [d])
+    stage("fin")
+    final(1, 0, [scaled(X(1), "XA0", ind(2), key), scaled(blk(T.NT, 1), "N1", ind(0), key), scaled(blk(T.FT, 1), "F1", ind(1), key)])
+    stage("n3")
+    turn("RN", 5, 3)
     for d in (3, 5, 7):
-        judge(d, 0)
+        stage("n%d" % d)
+        s, o = to_tile(4 + d // 2)
+        cp("v", blk(T.NT, d), o, [s], ["N%d" % d], 128)
 
     for m in range(3):
-        d = 2 * m + 3
-        off, ok, oc, okey = decide(1 + m)
-        pick(blk(T.FIN, 1 + m), blk(T.CAT2, m, 384), off, 128, ["%s%d" % (x, d - 1) for x in "INF"] + ok, ["FIN%d" % (1 + m)])
+        d, e = 2 * m + 3, 2 * m + 2
+        stage("t%d" % d)
+        ind, key = decide(str(e), [(0, 6), (1, 6)], 12 * top(e))
+        xz, nn, nf = scaled(X(e), xk(e), ind(2), key), scaled(blk(T.NT, e), "N%d" % e, ind(0), key), scaled(blk(T.NT, e), "N%d" % e, ind(4), key)
         s = slot("C")
-        pe([(ps(s, 0, 128, 0, 128), blk(T.RX, m), blk(T.FIN, 1 + m), True, True, 512)], ["RX%d" % m, "FIN%d" % (1 + m)], [s])
-        cp("v", blk(T.LF3, m), ps(s, 0, 128, 0, 128), [], [s, "LF3%d" % m], 128)
-        ts(c1(T.DE, oc + 4), c1(T.DE, oc + 1), 128.0, None, ALU.is_equal, None, [okey], ["seln%d" % m])
-        ts(c1(T.DE, oc + 5), c1(T.DE, oc), 3.0 / 256, c1(CC, KHM + m), ALU.mult, ALU.is_equal, [okey, "KHM"], ["sel%d" % m])
-        mk_b(5 + m, 1, c1(T.DE, oc + 5), "sel%d" % m)
-        dg = blk(T.HB, m)
-        ts(dg, EYE, c1(T.DE, oc + 4), None, ALU.mult, None, ["PMd0", "seln%d" % m, "H0", "H1"], ["DG%d" % m])
-        k = (2, 5, 6)[m]
-        to_tile("RA", 5 + m, blk(T.CAT3, 3 + m), "N%d" % d, [(dg, blk(T.H2, k)), (dg, blk(T.LO, k))], ["DG%d" % m, "H%d" % k, "L%d" % k])
-        lists(1, [(d, T.CAT3, 3 + m, "N%d" % d)])
-        gather2("RF%d" % m, 128 * m, "RN", ["RN_0", "RN_1"], T.LF3, ["LF3%d" % m])
-        to_tile("RF%d" % m, 8 + m, blk(T.CAT3, 6 + m), "F%d" % d)
-        lists(2, [(d, T.CAT3, 6 + m, "F%d" % d)])
-    home("O2", T.FIN[:], ["FIN%d" % k for k in range(4)], 6.0, T.OW2[:], "OW2", 262e3)
-    dma("s", [(T.ym[:, 0:256], T.OW2[:, 0:256]), (blk(T.ym, 3), blk(T.OW2, 2)), (blk(T.ym, 5), blk(T.OW2, 3))], ["OW2"], ["ym2"], 262e3)
-    home("O3", T.CAT3[:, 384:1024], ["N3", "N5", "N7", "F3", "F5"], 7.0, T.OWN[:, 384:1024], "OWNb", 328e3)
-    home("O4", T.CAT3[:, 1024:1152], ["F7"], 3.5, T.OWN[:, 1024:1152], "OWNc", 66e3)
-    for c in (1, 2):
-        for d in (3, 5, 7):
-            judge(d, c)
-    counts(4, [3, 5, 7])
-    scores(4, [3, 5, 7])
-    off, ok, oc, okey = decide(4)
-    pick(T.YO[:], T.OWN[:, :], off, 384, ["OWNa", "OWNb", "OWNc"] + ok, ["YO"])
-    dma("s", [(blk(T.ym, 2), blk(T.YO, 0)), (blk(T.ym, 6), blk(T.YO, 2))], ["YO"], ["ym3"], 131e3)
-    dma("a", [(blk(T.ym, 4), blk(T.YO, 1))], ["YO"], ["ym4"], 66e3)
+        pe([(ps(s, 0, 128), blk(T.RT, x), t[0], 128) for x, t in ((d, xz), (d, nn), (e, nf))], ["RT%d" % d, "RT%d" % e, xz[1], nn[1], nf[1]], [s])
+        cp("v", blk(T.LF3, m), ps(s, 0, 128), [s], ["LF3%d" % m], 128)
+        gather2("RF%d" % m, "RB", ["RB_0", "RB_1"], T.LF3, 128 * m, "LF3%d" % m, "F%d" % d)
+        b = 11 + 2 * m
+        ts(blk(T.BM, b, 8, 2), blk(T.BM, b + 6, 8, 2), ind(3), None, EQ, None, ["BM%d" % (b + 6), "BM%d" % (b + 7), key], ["BM%d" % b, "BM%d" % (b + 1)])
+        turn("RF%d" % m, b, 2)
+        a1, a2, b1 = scaled(blk(T.NT, d), "N%d" % d, ind(5), key), scaled(X(d), xk(d), ind(3), key), scaled(X(d), xk(d), ind(1), key)
+        s, o = to_tile(b, [(blk(T.RT, 0), a1[0]), (blk(T.RT, 0), a2[0])], ["RT0", a1[1], a2[1]])
+        tile_out(s, o, d, 1, (T.C3, 2 * m), "A%d" % d, X(d), xk(d))
+        s, o = to_tile(b + 1, [(blk(T.RT, 0), b1[0])], ["RT0", b1[1]])
+        tile_out(s, o, d, 2, (T.C3, 2 * m + 1), "B%d" % d, blk(T.C3, 2 * m), "A%d" % d)
+        counts(d)
+        stage("j%d" % d)
+        judge(d, 1)
+        judge(d, 2)
+        stage("fin")
+        final(e, m + 1, [xz, nn, scaled(blk(T.FT, e), "F%d" % e, ind(1), key)])
+    stage(60)
+    home("O3", 0, 2)
+    home("O7", 2, 3)
+    scores("7", [3, 5, 7])
+    ind, key = decide("7", [(2, 18)], 36)
+    for m in range(3):
+        pick(blk(T.YO, m), blk(T.OWN, m, 384), 1 + m, ind, 3 * m, key, ["OW%d%d" % (c, m) for c in range(3)], ["YO%d" % m])
+        dma("as", [(blk(T.ym, 2 * m + 2), blk(T.YO, m))], ["YO%d" % m], ["ym%d" % (2 * m + 3)], 65e3)
 
     for nd in nodes:
         if nd["kind"] == "ex":
-            nd["w"] = ["~ex" + nd["f"][0]]
+            nd["w"] = nd["w"] + ["~" + nd["w"][0]]
     if "order" not in PLAN:
-        PLAN["order"], PLAN["val"] = schedule(nodes)
-        PLAN["nodes"] = nodes
+        tied = []
+        for i, nd in enumerate(nodes):
+            tied.append(dict(nd))
+        PLAN["order"], PLAN["val"] = schedule(tied)
+    if "dry" in PAR:
+        return
     val.update(PLAN["val"])
     waited = {q: {} for q in Q}
-    lastw = {}
-    readers = {}
+    lastw, readers, total = {}, {}, {}
+    ndma = [0]
 
     def need(q, toks):
         best = {}
         for s, n in toks:
-            if q == "p" and s == "cp":
-                continue
-            best[s] = max(best.get(s, 0), n)
+            if not (q == "p" and s == "cp"):
+                best[s] = max(best.get(s, 0), n)
         for s, n in best.items():
             if waited[q].get(s, 0) < n:
                 Q[q].wait_ge(T.sem[s], n)
                 waited[q][s] = n
 
-    def bits(m):
-        return bin(m).count("1")
-
     for i, q in PLAN["order"]:
         nd = nodes[i]
-        if nd["kind"] == "nop":
-            continue
-        r = [val.get(k, k) for k in nd["r"] if k[0] != "~"]
-        w = [val.get(k, k) for k in nd["w"] if k[0] != "~"]
+        r, x, w = [[val.get(k, k) for k in nd[y] if k[0] != "~"] for y in "rxw"]
         toks = []
-        for k in r + w:
+        for k in r + x + w:
             toks += lastw.get(k, [])
         for k in w:
             toks += readers.get(k, [])
+        for k in x:
+            toks += [tk for tk in readers.get(k, []) if tk[0] != CS[q]]
+        if nd["kind"] == "nop":
+            lastw[w[0]] = [tk for k in r for tk in lastw[k]]
+            continue
         need(q, toks)
         if nd["kind"] == "ex":
-            name, src, dst, halves, ld = nd["f"]
-            for call in deal(T, topo, me, halves):
-                ts_ = []
-                for a, h, m in call:
-                    rid, pid, _se = topo.addr(T.cores[a])
-                    ts_.append(RemoteDMATransfer(dst_ids=[DstId(rid=rid, pnc=pid)], dma_engine_mask=m, remote_sem=T.sem["ar" + name],
-                                                 src=src(a, h), dst=dst(h)))
-                    total["sent"] = total.get("sent", 0) + bits(m)
-                g.remote_dma_fused(ts_, local_sem=T.sem.sent)
-            n = sum(bits(m) for b in range(8) if b != me for call in deal(T, topo, b, halves) for a, h, m in call if a == me)
-            total["ar" + name] = n
-            lastw[ld] = lastw.get(ld, []) + [("ar" + name, n)]
+            name = nd["f"]
+            total["sent"] = total.get("sent", 0) + send(g, T, topo, deal(T, topo, me, name)[0], name)
+            s = "ar" + name
+            total[s] = sum(bits(t[3]) for b in range(8) for part in deal(T, topo, b, name) for t in part if t[0] == core)
+            lastw[s] = [(s, total[s])]
+            continue
+        if nd["kind"] == "fold":
+            n, s = nd["f"], w[0]
+            sib = T.cores[me ^ 1]
+            m = sum(1 << e for e in topo.engines(core, sib)[-PAR["Me"]:])
+            g.remote_dma_fused([RemoteDMATransfer(dst_ids=[DstId(rid=topo.addr(sib)[0], pnc=topo.addr(sib)[1])], dma_engine_mask=m, remote_sem=T.sem[s], alu_op=2,
+                                                  srcs=[T.TT[:, 1024 * n + k:1024 * n + k + 1023] for k in range(2)], dsts=[T.MM[:, 1024 * n:1024 * n + 1023]])],
+                               local_sem=T.sem.sent)
+            total["sent"] += bits(m)
+            total[s] = bits(m)
+            lastw[s] = [(s, total[s])]
             continue
         if nd["kind"] == "dma":
-            s = "d%d" % nd_[0]
-            nd_[0] += 1
-            for o, x in nd["f"]:
-                Q[q].dma_start(o, x).then_inc(T.sem[s], 16)
+            s = "d%d" % ndma[0]
+            ndma[0] += 1
+            for o, y in nd["f"]:
+                Q[q].dma_start(o, y).then_inc(T.sem[s], 16)
             total[s] = 16 * len(nd["f"])
         else:
             s = CS[q]
             total[s] = total.get(s, 0) + 1
             if nd["kind"] == "pe":
-                for m in nd["f"][:-1]:
-                    g.tensor.matmul(z(m[0]), z(m[1]), z(m[2]), m[3], m[4])
-                m = nd["f"][-1]
-                g.tensor.matmul(z(m[0]), z(m[1]), z(m[2]), m[3], m[4]).then_inc(T.sem.cp, 1)
+                for m in nd["f"]:
+                    last = g.tensor.matmul(z(m[0]), z(m[1]), z(m[2]), m[3], m[4])
+                last.then_inc(T.sem.cp, 1)
             else:
                 nd["f"](q).then_inc(T.sem[s], 1)
-        for k in r:
+        for k in r + x:
             readers.setdefault(k, []).append((s, total[s]))
         for k in w:
             lastw[k] = [(s, total[s])]

@@ -5,37 +5,39 @@ ALU = AluOpType
 ACT = ActivationFunctionType
 F32, BF, I32, U16, F16 = "float32", "bfloat16", "int32", "uint16", "float16"
 NT = 21
-PH = ["1", "2", "4", "6", "7"]
+PH = ["1", "2", "4", "6", "5", "7"]
 
 SCRATCH = {
-    "StA": ("dram", [8, 128, 32], I32), "LdA": ("dram", [8, 128, 32], I32), "WI": ("sbuf", [128, 2048], I32), "BH": ("sbuf", [128, 8], F16),
-    "StB": ("dram", [8, 128, 66], F16), "LdB": ("dram", [8, 128, 66], F16),
+    "StA": ("dram", [8, 128, 32], I32), "LdA": ("dram", [8, 128, 32], I32), "WI": ("sbuf", [128, 2048], I32), "BH": ("sbuf", [128, 24], F16),
+    "StB": ("dram", [8, 128, 64], F16), "LdB": ("dram", [8, 128, 64], F16),
     "StF": ("dram", [16, 128, 128], BF), "LdF": ("dram", [16, 128, 128], BF), "ViaF": ("dram", [6, 128, 128], BF),
-    "StE": ("dram", [8, 128, 16], I32), "LdE": ("dram", [8, 128, 16], I32), "ViaE": ("dram", [6, 128, 16], I32), "ViaB": ("dram", [6, 128, 66], F16),
+    "StE": ("dram", [8, 128, 18], F16), "LdE": ("dram", [8, 128, 18], F16), "ViaE": ("dram", [6, 128, 16], I32), "ViaB": ("dram", [6, 128, 66], F16),
     "ViaY0": ("dram", [6, 128, 32], F32), "ViaY1": ("dram", [6, 128, 32], F32),
     "StO3": ("dram", [8, 128, 64], F16), "LdO3": ("dram", [8, 128, 64], F16),
     "StO7": ("dram", [8, 128, 32], F16), "LdO7": ("dram", [8, 128, 32], F16),
     "IA": ("sbuf", [128, 384], I32), "AN": ("sbuf", [128, 384], I32), "XA": ("sbuf", [128, 384], F16),
-    "MPB": ("sbuf", [128, 640], I32), "BT": ("sbuf", [128, 528], F16), "IB": ("sbuf", [128, 528], F16),
+    "MPB": ("sbuf", [128, 640], I32), "BT": ("sbuf", [128, 512], F16), "IB": ("sbuf", [128, 512], F16), "ET": ("sbuf", [128, 144], F16), "IE": ("sbuf", [128, 144], F16),
     "LM": ("sbuf", [128, 8], I32), "LB": ("sbuf", [128, 8], I32), "WF": ("sbuf", [128, 8], F32),
-    "W": ("sbuf", [128, 4096], BF), "FR": ("sbuf", [128, 7 * 1024], BF), "BS": ("sbuf", [128, 72], F32),
-    "WM2": ("sbuf", [128, 2048], BF), "WM3": ("sbuf", [128, 2048], BF),
+    "W": ("sbuf", [128, 4096], BF), "FR": ("sbuf", [128, 7 * 1040], BF), "MM": ("sbuf", [128, NT * 1040], BF), "K256": ("sbuf", [128, 128], BF), "CO": ("sbuf", [128, 24], F32), "GF": ("sbuf", [128, 168], F32),
+    "GB": ("sbuf", [128, 3 * 168], BF), "CF": ("sbuf", [128, 7 * 16], F32), "PH": ("sbuf", [128, 14 * 128], F16), "BS": ("sbuf", [128, 72], F32),
+    "WM1": ("sbuf", [128, 2048], BF), "WM3": ("sbuf", [128, 2048], BF),
     "RA": ("sbuf", [128, 2048], F16), "RB": ("sbuf", [128, 2048], BF), "RN": ("sbuf", [128, 2048], BF),
     "RF0": ("sbuf", [128, 2048], BF), "RF1": ("sbuf", [128, 2048], BF), "RF2": ("sbuf", [128, 2048], BF),
-    "TT": ("sbuf", [128, NT * 1024], BF), "JK": ("sbuf", [128, 4096], BF),
+    "TT": ("sbuf", [128, NT * 1040], BF),
     "HB": ("sbuf", [128, 10 * 128], BF), "H2": ("sbuf", [128, 10 * 128], BF), "LO": ("sbuf", [128, 10 * 128], BF),
     "NT": ("sbuf", [128, 8 * 128], F16), "FT": ("sbuf", [128, 8 * 128], F16), "C3": ("sbuf", [128, 768], F16), "OL": ("sbuf", [128, 768], F16),
     "SCL": ("sbuf", [128, 24 * 128], F16),
     "PI1": ("sbuf", [128, 384], F32), "FIN": ("sbuf", [128, 512], F32), "OWN": ("sbuf", [128, 1152], F32), "YO": ("sbuf", [128, 384], F32),
-    "LQ": ("sbuf", [128, 512], U16), "LF3": ("sbuf", [128, 384], U16), "LN": ("sbuf", [128, 128], U16),
-    "FL": ("sbuf", [128, 21 * 64], U16), "NE": ("sbuf", [128, 14 * 128], BF),
+    "LQ": ("sbuf", [128, 640], U16), "LF3": ("sbuf", [128, 384], U16), "LN": ("sbuf", [128, 128], U16),
+    "FL": ("sbuf", [128, 21 * 66], U16), "NE": ("sbuf", [128, 14 * 128], BF),
     "OF": ("sbuf", [128, 32], U16), "TH": ("sbuf", [128, 64], F32),
     "AC": ("sbuf", [128, 48], F32), "CW": ("sbuf", [128, 7 * 24], F32), "GW": ("sbuf", [128, 7 * 16], BF), "RR": ("sbuf", [128, 7 * 16], BF),
-    "GL": ("sbuf", [128, 10 * 8], F32), "SS": ("sbuf", [128, 160], F32), "SC": ("sbuf", [128, 160], F32), "DE": ("sbuf", [128, 5 * 32], F32),
+    "GL": ("sbuf", [128, 10 * 8], F32), "SS": ("sbuf", [128, 192], F32), "SC": ("sbuf", [128, 192], F32), "DE": ("sbuf", [128, 6 * 32], F32),
     "col": ("sbuf", [128, 208], BF), "CI": ("sbuf", [128, 192], BF), "cgr": ("sbuf", [128, 128], F32),
     "PI": ("sbuf", [128, 8], I32), "PF": ("sbuf", [128, 8], F32), "CC": ("sbuf", [128, 128], F32),
-    "ZF": ("sbuf", [128, 17 * 128], F32), "ZH": ("sbuf", [128, 17 * 128], F16), "EF": ("sbuf", [128, 128], F32),
-    "BM": ("sbuf", [128, 23 * 8], BF), "PM": ("sbuf", [128, 14 * 128], BF), "RT": ("sbuf", [128, 8 * 128], F16),
+    "ZF": ("sbuf", [128, 17 * 128], F32), "ZH": ("sbuf", [128, 17 * 128], F16), "EF": ("sbuf", [128, 130], F32),
+    "BX": ("sbuf", [128, 228], BF), "UC": ("sbuf", [128, 24], F32), "CH": ("sbuf", [128, 14 * 64], F16), "CZ": ("sbuf", [128, 14 * 64], F32),
+    "BM": ("sbuf", [128, 23 * 8], BF), "PM": ("sbuf", [128, 3 * 128], BF), "RT": ("sbuf", [128, 8 * 128], F16),
     "FM": ("sbuf", [128, 7 * 192], F16), "KM": ("sbuf", [128, 3 * 128], F32),
 }
 for _k in range(8):
@@ -51,15 +53,26 @@ SEMAPHORES = ["cv", "ca", "cp", "cg", "sent"] + ["ar" + x for x in EX] + ["d%d" 
 POOLS = {"C": ["PS%d" % k for k in range(8)], "D": []}
 GREATER = [[1, 3, 5, 7], [6, 3, 2, 7], [6, 4, 5, 7]]
 POS = {1: 0, 2: 1, 3: 2, 4: 3, 5: 4, 6: 5, 7: 6, "id": 7, "A": 8, "B": 9}
-PAR = {"cy": 0.92e-3, "gat": 1.56, "pe": 0.46e-3, "dma": 1.62, "bw": 360e3, "sem": 0.065, "mix": 0.3, "turns": 3, "small": 0.0, "flow": 0, "look": 0.25, "ahead": 0.5, "spare": 0.3,
-       "A": 8.3, "E": 8.3, "F": 10.3, "B": 6.8, "aided": [], "S": 1.1, "room": 300e3, "Y": 3.2, "O3": 3.2, "O7": 2.3, "fin": 0, "wide": [2, 5, 8, 9, 10, 11, 13, 15],
-       "moves": 90000, "cut": [11, 12, 21, 41, 61, 72, 71, 52], "mean": 1.5, "seed": 4, "heat": 0.4, "far": 8, "cases": [(1.0, 1.0, 1.0), (1.2, 1.25, 1.4)]}
-STEPS = ("Ba Bb g10 g12 g11 s10 s12 s11 g20 F2a F2b g40 F4a s20 F4b g60 F6a s40 F6b s60 Na Nb g22 g21 g30 s22 s21 g42 g41 s30 g50 s42 s41 g62 g61 s50 g70 s62 s61 "
-         "F3a F3b s70 g31 g32 F5a F5b s31 s32 F7a F7b g51 g52 s51 s52 g71 g72 s71 s72").split()
-ACT_G, VEC_X = "g12 g20 g30 g50 g70".split(), "Bb Na F4b F6b F3a F7a s71".split()
-LONG = {"v": [x for x in STEPS if x in VEC_X or (x[0] == "g" and x not in ACT_G)], "f": []}
-LONG["a"] = [x for x in STEPS if x not in LONG["v"]]
+PAR = {"cy": 0.92e-3, "gat": 1.56, "pe": 0.46e-3, "dma": 1.62, "bw": 360e3, "sem": 0.065, "mix": 0.3, "turns": 3, "small": 5.0, "flow": 0, "look": 0.3, "ahead": 0.5, "spare": 0.3,
+       "A": 7.4, "E": 7.0, "F": 6.0, "B": 1.5, "bA": 330e3, "bE": 110e3, "bF": 550e3, "bB": 500e3, "Bafter": ["W0"], "aided": [], "S": 1.1, "room": 300e3, "Y": 2.0, "O3": 2.0, "O7": 1.7, "bY": 450e3, "bO": 450e3, "gdma": 1.0, "fin": 0, "wide": [0, 2, 5, 8, 9, 10, 11, 13, 15], "widec": [],
+       "moves": 85000, "cut": [11, 12, 21, 41, 61, 72, 71, 52], "mean": 0.3, "seed": 4, "heat": 0.5, "far": 4, "aim": 10, "step": 64, "quit": 0.6, "mile": 0.02, "hold": 0.5, "cutS": 2, "tries": 0, "heat2": 0.5, "reach": 120, "case": (1.0, 1.0, 1.0, 1.0, 1.0), "cases": [(1.0, 1.0, 1.0, 1.0, 1.0), (1.15, 1.22, 1.1, 1.1, 1.1), (1.0, 0.78, 1.25, 1.5, 1.3)]}
+STEPS = "Ra Rb Ba Bb g11 g10 g12 g20 g30 F2b F2a g40 F4b F4a g60 F6a F6b Nb Na g22 g21 g42 g41 g62 g61 g50 g70 F3a F3b g32 g31 F5b F5a g52 g51 F7a F7b g72 g71".split()
+ACT_G, VEC_X = "g12 g22 g42 g62 g32 g52 g72 g30 g50 g70".split(), "Na F7b F3b F4b pg30 pg50 pg70 pg22 pg42 pg52".split()
+LONG = {}
+LOADS = "WM1 W0 XA1 FR1 Wy FR2 FR3 WM3a WM2c IB WM3b FR4 FR6 WM2b FR5 FR7".split()
+
+
+def share(act, vec):
+    LONG["v"] = [x for x in STEPS if x in vec or (x[0] == "g" and x not in act) or x[0] in "suR"]
+    LONG["a"] = [x for x in STEPS if x not in LONG["v"]]
+    LONG["s"] = LOADS
+    LONG["p"] = [x[1:] for x in vec if x[0] == "p" and x[1:] in act]
+    LONG["d"] = [x[1:] for x in vec if x[0] == "d" and x[1:] in act and x[1:] not in LONG["p"]]
+
+
+share(ACT_G, VEC_X)
 PLAN = {}
+PAIRED = [(1, 1), (1, 2), (2, 1), (4, 1), (6, 1), (2, 2), (4, 2), (6, 2)] + [(d, c) for d in (3, 5, 7) for c in (1, 2)]
 
 
 def top(d):
@@ -113,17 +126,18 @@ def deal(T, topo, me, name):
     return own, aids
 
 
-def send(g, T, topo, part, name):
+def send(g, T, topo, part, name, one=None):
     calls = []
     for t in part:
         free = [c for c in calls if not any(t[3] & u[3] for u in c)]
         if not free:
             calls.append([])
         (free + calls[-1:])[0].append(t)
+    calls = calls if one is None else calls[one:one + 1]
     for c in calls:
         g.remote_dma_fused([RemoteDMATransfer(dst_ids=[DstId(rid=topo.addr(k)[0], pnc=topo.addr(k)[1])], dma_engine_mask=m, remote_sem=T.sem["ar" + name], src=a, dst=b)
                             for k, a, b, m in c], local_sem=T.sem.sent)
-    return sum(bits(t[3]) for t in part)
+    return sum(bits(t[3]) for c in calls for t in c)
 
 
 def schedule(nodes):
@@ -445,6 +459,475 @@ def schedule(nodes):
     return best[1], best[2]
 
 
+def plan(nodes):
+    n, sem, bw = len(nodes), PAR["sem"], PAR["bw"]
+    pre = [set() for _ in nodes]
+    lastw, readers = {}, {}
+    for i, nd in enumerate(nodes):
+        for k in nd["r"] + nd["x"] + nd["w"]:
+            pre[i].update(lastw.get(k, []))
+        for k in nd["w"]:
+            pre[i].update(readers.get(k, []))
+        for k in nd["r"] + nd["x"]:
+            readers.setdefault(k, []).append(i)
+        for k in nd["w"]:
+            lastw[k] = [i]
+            readers[k] = []
+        pre[i].discard(i)
+    soft = [set(j for j in pre[i] if list(nodes[i]["cost"]) == list(nodes[j]["cost"]) == ["p"]
+                or all(k[0] == "~" for k in set(nodes[j]["w"]) & set(nodes[i]["r"] + nodes[i]["w"])) and set(nodes[j]["w"]) & set(nodes[i]["r"])) for i in range(n)]
+    unit = [nd["slots"][0] if nd["slots"] else i for i, nd in enumerate(nodes)]
+    post = [[] for _ in nodes]
+    for i in range(n):
+        for j in pre[i]:
+            post[j].append(i)
+    for i in range(n):
+        if unit[i] == i:
+            both = set(unit[j] for j in pre[i]) & set(unit[j] for j in post[i])
+            unit[i] = ([u for u in both if isinstance(u, tuple)] + [i])[0]
+    named = {nd["name"]: i for i, nd in enumerate(nodes)}
+    true = [set(p) for p in pre]
+    for line in (LONG["v"], LONG["a"], LONG["s"]):
+        line = [x for x in line if x in named]
+        for a, b in zip(line, line[1:]):
+            if named[a] not in pre[named[b]]:
+                pre[named[b]].add(named[a])
+                soft[named[b]].add(named[a])
+                post[named[a]].append(named[b])
+    outer = {}
+    for i in range(n):
+        if isinstance(unit[i], tuple):
+            outer.setdefault(unit[i], set()).update(j for j in pre[i] if unit[j] != unit[i])
+    opens = [[] for _ in nodes]
+    for u in outer:
+        for j in outer[u]:
+            opens[j].append(u)
+    way = [0.0] * n
+    left = [len(p) for p in post]
+    line = [i for i in range(n) if not left[i]]
+    for i in line:
+        nd = nodes[i]
+        way[i] = min(nd["cost"].values()) + max([way[j] + (0.0 if i in soft[j] else nd["lat"] + nd["bytes"] / bw + sem) for j in post[i]] + [nd["lat"]])
+        for j in pre[i]:
+            left[j] -= 1
+            if not left[j]:
+                line.append(j)
+    wait = [len(p) for p in pre]
+    shut = {u: len(outer[u]) for u in outer}
+    left = {u: unit.count(u) for u in outer}
+    pool = [(0.0, v) for v in POOLS["C"]]
+    val, bank, at, free, order = {}, {}, {}, {q: 0.0 for q in "gvaps"}, []
+    end, fin = [0.0] * n, [0.0] * n
+    ready = [i for i in range(n) if not wait[i]]
+    bus = 0.0
+    PLAN["log"] = []
+    while ready:
+        cand = []
+        for i in ready:
+            nd, u = nodes[i], unit[i]
+            if i not in at:
+                at[i] = max([end[j] if j in soft[i] else fin[j] + sem for j in pre[i]] + [0.0])
+            t = at[i]
+            if nd["slots"] and u not in val:
+                if shut[u] or not pool:
+                    continue
+                t = max(t, pool[0][0])
+            if nd["bytes"]:
+                t = max(t, bus - nd["lat"] - PAR["ahead"])
+            best = None
+            for q, c in nd["cost"].items():
+                s = max(t, free[q])
+                if nd["slots"] and u in bank and bank[u][1] != q:
+                    s = max(s, bank[u][0])
+                if best is None or s + c + (q == "v") * PAR["spare"] < best[0]:
+                    best = (s + c + (q == "v") * PAR["spare"], s, q, c)
+            cand.append((best[1] + best[3], best[1], i, best[2]))
+        e0, _, i0, q0 = min(cand)
+        both = [c for c in cand if c[3] == q0 and (c[1] < e0 or c[2] == i0)]
+        t0 = min(c[1] for c in both) + PAR["look"]
+        e, t, i, q = min(both, key=lambda c: (-way[c[2]] - (PAR["small"] if 9.0 < c[1] <= t0 and c[0] - c[1] < 0.4 else 0.0), c[2]))
+        nd, u = nodes[i], unit[i]
+        free[q] = end[i] = e
+        fin[i] = e + nd["lat"]
+        if nd["bytes"]:
+            bus = fin[i] = max(bus, fin[i]) + nd["bytes"] / bw
+        if nd["slots"]:
+            if u not in val:
+                val[u] = pool.pop(0)[1]
+            bank[u] = (e + sem, q)
+        if u in left:
+            left[u] -= 1
+            if not left[u]:
+                pool.append((bank[u][0], val[u]))
+                pool.sort()
+        for v in opens[i]:
+            shut[v] -= 1
+        order.append((i, q))
+        PLAN["log"].append((round(t, 1), q, nd["name"] or str(nd["w"][0]), round(fin[i], 1)))
+        ready.remove(i)
+        for j in post[i]:
+            wait[j] -= 1
+            if not wait[j]:
+                ready.append(j)
+    PLAN["end"] = max(fin) if len(order) == n else 1e9
+    PLAN["way"] = max(way)
+    PLAN["busy"] = {q: round(sum(nodes[i]["cost"][q] for i, x in order if x == q and end[i] > 13.2), 1) for q in free}
+    if "path" in PAR:
+        i = way.index(max(way))
+        PLAN["path"] = []
+        while post[i]:
+            PLAN["path"].append((nodes[i]["name"] or str(nodes[i]["w"][0]), round(max(way) - way[i], 1)))
+            i = max(post[i], key=lambda j: way[j] + (0.0 if i in soft[j] else nodes[i]["lat"] + nodes[i]["bytes"] / bw + sem))
+    if PAR["tries"] and len(order) == n:
+        order = place(nodes, true, soft, order)
+    if PAR["moves"] and len(order) == n:
+        return polish(nodes, true, soft, order)
+    return order, val
+
+
+def place(nodes, pre, soft, order):
+    n, sem, bw = len(nodes), PAR["sem"], PAR["bw"]
+    pre = [set(p) for p in pre]
+    last = {}
+    for i, nd in enumerate(nodes):
+        for s in nd["slots"]:
+            if s in last:
+                pre[i].add(last[s][1])
+            last[s] = (last.get(s, (i, i))[0], i)
+    above = [0] * n
+    for i in range(n):
+        for j in pre[i]:
+            above[i] |= above[j] | 1 << j
+    late = [[] for _ in nodes]
+    lead = {}
+    for i, nd in enumerate(nodes):
+        for s in nd["slots"]:
+            a = last[s][0]
+            late[a] += [(j, lead.get(s, 0.0) + PAR["hold"]) for j in pre[i] if j != a and not above[j] >> a & 1 and j not in pre[a]]
+            lead[s] = lead.get(s, 0.0) + min(nd["any"].values()) + sem
+    true = [set(p) for p in pre]
+    for i in range(n):
+        pre[i].update(j for j, t in late[i])
+    post = [[] for _ in nodes]
+    for i in range(n):
+        for j in pre[i]:
+            post[j].append(i)
+    fc, fg, fl, fe, fb = PAR["case"]
+    qs = {q: k for k, q in enumerate("gvaps")}
+    cost = [[(qs[q], c * (fc * (fg if c > 0.7 else 1.0) if q in "va" else fc if q == "p" else 1.0)) for q, c in nd["any"].items()] for nd in nodes]
+    lat = [nd["lat"] * (fl if nd["kind"] == "dma" else fe) for nd in nodes]
+    byt = [nd["bytes"] / bw * fb for nd in nodes]
+    pr = [[(j, j in soft[i]) for j in sorted(true[i])] for i in range(n)]
+    miles = [i for i, nd in enumerate(nodes) if nd["kind"] == "ex"]
+    seq, done = [], set()
+
+    def put(i):
+        if i not in done:
+            done.add(i)
+            for j in sorted(pre[i]):
+                put(j)
+            seq.append(i)
+
+    for i, q in order:
+        put(i)
+    pick = [0] * n
+    spans = list(last.values())
+
+    def room(a, b, t, d):
+        lo, hi = 0, len(b)
+        while lo < hi:
+            m = (lo + hi) // 2
+            if b[m] <= t:
+                lo = m + 1
+            else:
+                hi = m
+        while lo < len(a) and a[lo] < t + d - 1e-9:
+            t = b[lo]
+            lo += 1
+        return t, lo
+
+    skip = [0, None]
+
+    def run():
+        if skip[1]:
+            a, b, end, fin, on, why = [[list(x) for x in y] for y in skip[1][:2]] + [list(y) for y in skip[1][2:]]
+        else:
+            a, b = [[] for _ in range(6)], [[] for _ in range(6)]
+            end, fin, on, why = [0.0] * n, [0.0] * n, [0] * n, [-1] * n
+        for i in seq[skip[0]:]:
+            t, y = 0.0, -1
+            for j, s in pr[i]:
+                u = end[j] if s else fin[j]
+                if u > t:
+                    t, y = u, j
+            for j, s in late[i]:
+                if fin[j] - s > t:
+                    t = fin[j] - s
+            c = cost[i]
+            if byt[i]:
+                lead = lat[i] + c[0][1]
+                t = room(a[5], b[5], t + lead, byt[i])[0] - lead
+            q, d = c[pick[i] - 1] if pick[i] else c[0]
+            u, k = room(a[q], b[q], t, d)
+            if len(c) > 1 and not pick[i]:
+                q2, d2 = c[1]
+                u2, k2 = room(a[q2], b[q2], t, d2)
+                if u2 + d2 <= u + d + PAR["spare"]:
+                    q, d, u, k = q2, d2, u2, k2
+            a[q].insert(k, u)
+            b[q].insert(k, u + d)
+            end[i] = u = u + d
+            u += lat[i]
+            if byt[i]:
+                u, k = room(a[5], b[5], u, byt[i])
+                a[5].insert(k, u)
+                u += byt[i]
+                b[5].insert(k, u)
+            fin[i], on[i], why[i] = u + sem, q, y
+        ev = sorted([(end[i] - cost[i][0][1], 1) for i, j in spans] + [(fin[j], -1) for i, j in spans])
+        over = use = 0
+        for t, k in ev:
+            use += k
+            if use > 8:
+                over += 1
+        return max(fin) + PAR["mean"] * sum(fin) / n + PAR["mile"] * sum(fin[i] for i in miles) + over, end, fin, on, (a, b, end, fin, on, why)
+
+    got = run()
+    early = [i for i in seq if got[1][i] < 9.0]
+    seq[:] = early + [i for i in seq if got[1][i] >= 9.0]
+    full, seq[:] = list(seq), early
+    skip[1] = run()[4]
+    seq[:], skip[0] = full, len(early)
+    got = run()
+    cur, best, x = got[0], (got, list(seq)), PAR["seed"]
+    big = [i for i in full[skip[0]:] if cost[i][0][1] > 0.4 or byt[i]]
+    for k in range(PAR["tries"]):
+        x = (x * 6364136223846793005 + 1442695040888963407) % 2 ** 64
+        heat = PAR["heat2"] * (1.0 - k / PAR["tries"]) * ((x >> 8) % 1000) ** 3 / 1e9
+        kind = (x >> 20) % 8
+        i = big[(x >> 40) % len(big)] if kind < 5 else full[skip[0] + (x >> 40) % (n - skip[0])]
+        if kind == 0 and len(cost[i]) > 1:
+            old = pick[i]
+            pick[i] = (old + 1 + (x >> 30) % 2) % 3
+            new = run()
+            if new[0] > cur + heat:
+                pick[i] = old
+                continue
+        else:
+            a = seq.index(i)
+            d = 1 - 2 * ((x >> 35) % 2)
+            b = min(n - 1, max(skip[0], a + d * (1 + ((x >> 24) % 1000) ** 2 * PAR["reach"] // 10 ** 6)))
+            if a == b:
+                continue
+            link = post if d > 0 else pre
+            go, stay, need = [i], [], set(link[i])
+            for c in range(a + d, b + d, d):
+                j = seq[c]
+                if j in need:
+                    go.append(j)
+                    need.update(link[j])
+                else:
+                    stay.append(j)
+            lo, hi = min(a, b), max(a, b) + 1
+            old = seq[lo:hi]
+            seq[lo:hi] = go[::-1] + stay[::-1] if d < 0 else stay + go
+            new = run()
+            if new[0] > cur + heat:
+                seq[lo:hi] = old
+                continue
+        cur = new[0]
+        if cur < best[0][0]:
+            best = (new, list(seq))
+    got, seq = best
+    PLAN["placed"] = (round(max(got[2]), 1), round(got[0], 1))
+    rank = {i: k for k, i in enumerate(seq)}
+    start = {i: got[1][i] - dict(cost[i])[got[3][i]] for i in seq}
+    return [(i, "gvaps"[got[3][i]]) for i in sorted(seq, key=lambda i: (round(start[i], 6), rank[i]))]
+
+
+def polish(nodes, pre, soft, order):
+    n, sem, step = len(nodes), PAR["sem"], PAR["step"]
+    post = [[] for _ in nodes]
+    for i in range(n):
+        for j in pre[i]:
+            post[j].append(i)
+    qs = {q: k for k, q in enumerate("gvaps")}
+    seq, on = [i for i, q in order], [0] * n
+    for i, q in order:
+        on[i] = qs[q]
+    alt = [[qs[q] for q in nd["any"]] for nd in nodes]
+    slots = sorted(set(s for nd in nodes for s in nd["slots"]))
+    sl = [slots.index(nd["slots"][0]) if nd["slots"] else -1 for nd in nodes]
+    count = [sl.count(k) for k in range(len(slots))]
+    pr = [[(j, j in soft[i]) for j in sorted(pre[i])] for i in range(n)]
+    sets = [([{qs[q]: c * (fc * (fg if c > 0.7 else 1.0) if q in "va" else fc if q == "p" else 1.0) for q, c in nd["any"].items()} for nd in nodes],
+             [nd["lat"] * (fl if nd["kind"] == "dma" else fe) for nd in nodes], [nd["bytes"] / PAR["bw"] * fb for nd in nodes]) for fc, fg, fl, fe, fb in PAR["cases"]]
+    m = len(count)
+    marks = [{0: ([0.0] * 5, [-1] * 5, 0.0, -1, [(0.0, 0, -1) for v in POOLS["C"]], list(count), [0.0] * m, [-1] * m, [None] * m), "t": ([0.0] * n, [0.0] * n, [-1] * n)} for _ in sets]
+    fresh = []
+    miles = [i for i, nd in enumerate(nodes) if nd["kind"] == "ex"]
+
+    at = [0] * n
+    for a, i in enumerate(seq):
+        at[i] = a
+
+    def run(first, upto=n):
+        total, first = 0.0, first - first % step
+        fresh[:] = []
+        for (cost, lat, byt), mark in zip(sets, marks):
+            free, who, bus, bw, p, left, last, lq, got = mark[first]
+            free, who, p, left, last, lq, got = list(free), list(who), list(p), list(left), list(last), list(lq), list(got)
+            fin, end, why = list(mark["t"][0]), list(mark["t"][1]), list(mark["t"][2])
+            new = {"t": (fin, end, why), "got": got}
+            fresh.append(new)
+            reach = upto
+            for a in range(first, n):
+                if not a % step:
+                    new[a] = (list(free), list(who), bus, bw, list(p), list(left), list(last), list(lq), list(got))
+                    if a > reach and new[a] == mark[a]:
+                        new["got"] = mark["got"]
+                        break
+                i = seq[a]
+                q = on[i]
+                t, y = free[q], who[q]
+                for j, s in pr[i]:
+                    u = end[j] if s else fin[j]
+                    if u > t:
+                        t, y = u, j
+                k = sl[i]
+                if k >= 0:
+                    if got[k] is None:
+                        if not p:
+                            return 1e9
+                        u, got[k], j = p.pop(0)
+                        if u > t:
+                            t, y = u, j
+                    elif on[lq[k]] != q and last[k] > t:
+                        t, y = last[k], lq[k]
+                t += cost[i][q]
+                free[q] = t
+                who[q] = i
+                u = t + lat[i]
+                if byt[i]:
+                    if bus > u:
+                        u, y = bus, bw
+                    bus = u = u + byt[i]
+                    bw = i
+                u += sem
+                if u != fin[i] or t != end[i]:
+                    end[i], fin[i] = t, u
+                    for j in post[i]:
+                        if at[j] > reach:
+                            reach = at[j]
+                why[i] = y
+                if k >= 0:
+                    last[k], lq[k] = t + sem, i
+                    left[k] -= 1
+                    if not left[k]:
+                        p.append((t + sem, got[k], i))
+                        last[k] = lq[k] = 0
+            new["sum"] = max(fin) + PAR["mean"] * sum(fin) / n + PAR["mile"] * sum(fin[i] for i in miles)
+            if new["sum"] > mark.get("sum", 1e9) + PAR["quit"]:
+                return 1e9
+            total += new["sum"]
+        return total / len(sets)
+
+    def accept():
+        for mark, new in zip(marks, fresh):
+            mark.update(new)
+
+    def held():
+        out = []
+        for mark in marks:
+            fin, end, why = mark["t"]
+            i = fin.index(max(fin))
+            while why[i] >= 0:
+                out.append((i, why[i]))
+                i = why[i]
+        return [x for x in out if x[1] not in pre[x[0]]], [x[0] for x in out if len(alt[x[0]]) > 1]
+
+    def shift(a, b):
+        d = 1 if b > a else -1
+        link = post if d > 0 else pre
+        go, stay, need = [seq[a]], [], set(link[seq[a]])
+        for c in range(a + d, b + d, d):
+            j = seq[c]
+            if j in need:
+                go.append(j)
+                need.update(link[j])
+            else:
+                stay.append(j)
+        return go[::-1] + stay[::-1] if d < 0 else stay + go
+
+    x, cur = PAR["seed"], run(0)
+    accept()
+    best = (cur, list(seq), list(on))
+    arcs, flex = held()
+    skip = sum(t < 9.0 for t in marks[0]["t"][1])
+    for k in range(PAR["moves"]):
+        x = (x * 6364136223846793005 + 1442695040888963407) % 2 ** 64
+        room = PAR["heat"] * (1.0 - k / PAR["moves"]) * ((x >> 8) % 1000) ** 3 / 1e9
+        kind = (x >> 20) % 16
+        if kind < 3:
+            i = flex[(x >> 40) % len(flex)] if kind and flex else seq[(x >> 40) % n]
+            if len(alt[i]) < 2:
+                continue
+            old = on[i]
+            on[i] = alt[i][0] + alt[i][1] - old
+            e = run(at[i], at[i])
+            if e > cur + room:
+                on[i] = old
+                continue
+        else:
+            if kind < 3 + PAR["aim"] and arcs:
+                i, j = arcs[(x >> 40) % len(arcs)]
+                a, b = at[i], at[j]
+                if kind % 2:
+                    a, b = b, a
+            else:
+                a = skip + (x >> 40) % (n - skip)
+                b = a
+            far, d = ((x >> 24) % 1000) ** 2 * PAR["far"] * (1 if (x >> 36) % 8 else 6) // 10 ** 6 + (a == b), (1 if b > a else -1) if a != b else 1 - 2 * ((x >> 35) % 2)
+            while far and 0 <= b + d < n:
+                b += d
+                far -= on[seq[b]] == on[seq[a]]
+            if a == b:
+                continue
+            lo, hi = min(a, b), max(a, b) + 1
+            old = seq[lo:hi]
+            seq[lo:hi] = shift(a, b)
+            if seq[lo:hi] == old:
+                continue
+            e = run(lo, hi)
+            if e > cur + room:
+                seq[lo:hi] = old
+                continue
+            for a in range(lo, hi):
+                at[seq[a]] = a
+        accept()
+        if e != cur or not k % 8:
+            arcs, flex = held()
+        cur = e
+        if e < best[0]:
+            best = (e, list(seq), list(on))
+    seq[:], on[:] = best[1], best[2]
+    for mark in marks:
+        mark.pop("sum")
+        mark[0][4][:] = [(0.0, v, -1) for v in POOLS["C"]]
+    run(0)
+    accept()
+    PLAN["ends"] = [round(max(mark["t"][0]), 1) for mark in marks]
+    PLAN["end"] = sum(PLAN["ends"]) / len(sets)
+    fin, end, why = marks[0]["t"]
+    i, PLAN["path"] = fin.index(max(fin)), []
+    while i >= 0:
+        PLAN["path"].append("%s%s:%s@%.1f" % ("" if why[i] in pre[i] else "*", "gvaps"[on[i]], (nodes[i]["name"] or str(nodes[i]["w"][0])).strip("()'").replace("C', ", "#"), end[i]))
+        i = why[i]
+    PLAN["log"] = [(round(end[i] - sets[0][0][i][on[i]], 1), "gvaps"[on[i]], nodes[i]["name"] or str(nodes[i]["w"][0]), round(fin[i], 1)) for i in seq]
+    PLAN["busy"] = {q: round(sum(sets[0][0][i][on[i]] for i in seq if on[i] == qs[q] and end[i] > 13.2), 1) for q in qs}
+    return [(i, "gvaps"[on[i]]) for i in seq], dict(zip(slots, marks[0]["got"]))
+
+
 def rank_program(g, core, T, topo):
     me = T.rank_of(core)
     if me is None:
@@ -479,11 +962,11 @@ def rank_program(g, core, T, topo):
             return x[1](val[x[2]])
         return x
 
-    def ps(s, a, b, p1=128, step=1):
-        return ("lazy", lambda v: T[v][0:p1, a:b:step], s)
+    def ps(s, a, b, p1=128, step=1, p0=0):
+        return ("lazy", lambda v: T[v][p0:p1, a:b:step], s)
 
     def tb(s, a, b):
-        return T.TT[:, 1024 * int(s[1:]) + a:1024 * int(s[1:]) + b]
+        return T.TT[:, 1040 * int(s[1:]) + a:1040 * int(s[1:]) + b]
 
     def node(kind, cost, f, r, w, lat=0.0, nbytes=0, push=0.0):
         x = [k for k in r if isinstance(k, tuple)]
@@ -497,7 +980,7 @@ def rank_program(g, core, T, topo):
 
     def call(name):
         nodes[-1]["name"] = name
-        if name[0] != "g":
+        if name[0] in "BFN":
             nodes[-1]["any"] = {q: min(nodes[-1]["cost"].values()) for q in "va"}
 
     def cyc(n):
@@ -512,18 +995,29 @@ def rank_program(g, core, T, topo):
     def memset(ap, v, w, n=64):
         vop(lambda: V.memset(ap, v), [], w, n)
 
-    def pe(mms, r, w):
+    def pe(mms, r, w, start=True, stop=True):
         out = []
         for i, m in enumerate(mms):
             if m is not None:
-                out.append((m[0], m[1], m[2], i == 0 or mms[i - 1] is None, i == len(mms) - 1 or mms[i + 1] is None, m[3]))
+                out.append((m[0], m[1], m[2], mms[i - 1] is None if i else start, stop if i == len(mms) - 1 else mms[i + 1] is None, m[3]))
         node("pe", {"p": sum(m[5] + 8 for m in out) * PAR["pe"]}, out, r, w)
 
     def dma(qs, moves, r, w, nbytes, push=0.0):
         node("dma", {q: 0.07 * len(moves) for q in qs}, moves, r, w, PAR["dma"], nbytes, push)
+        nodes[-1]["name"] = w[0]
 
-    def exchange(name, r, lat):
-        node("ex", {"g": 0.7}, name, r, ["ar" + name], lat, PAR["room"] if name[0] == "S" else 0)
+    def exchange(name, r, lat, call=None):
+        node("ex", {"g": 0.7}, (name, call), r, ["ar" + name + "0" * (call == 0)], lat, PAR["room"] if name[0] == "S" else PAR.get("b" + name[0], 0) / (1 + (name == "O7")))
+
+    def aff(out, in_, a, b, r, w, n=64):
+        def f(q):
+            if q == "v":
+                return V.tensor_scalar(out, in_, a, b, ALU.mult, ALU.add)
+            return g.scalar.activation(out, in_, ACT.Identity, bias=b, scale=a)
+        node("op", {"a": cyc(n), "v": cyc(n)}, f, r, w)
+
+    def fill(out, v, w, n):
+        aff(out, T.col[:, 0:n], 0.0, v, ["col"], w, n)
 
     def ts(out, in0, s1, s2, o0, o1, r, w, n=64):
         if o1 is None:
@@ -548,6 +1042,13 @@ def rank_program(g, core, T, topo):
             return g.scalar.activation(z(out), z(in_), ACT.Identity, bias=c)
         node("op", {q: cyc(n // 2 if half and q == "v" else n) for q in qs}, f, r, w)
 
+    def mul(qs, out, in_, c, r, w):
+        def f(q):
+            if q == "v":
+                return V.tensor_scalar(out, in_, c, None, ALU.mult)
+            return g.scalar.activation(out, in_, ACT.Copy, scale=c)
+        node("op", {q: cyc(64) for q in qs}, f, r, w)
+
     def blk(t, k, n=128, m=1):
         return t[:, k * n:(k + m) * n]
 
@@ -561,22 +1062,24 @@ def rank_program(g, core, T, topo):
     gop(lambda: g.iota(T.col[:], [[1, 208]], -16, 0, allow_small_or_imprecise_dtypes=True), 208, ["~g0"], ["col", "~g1"])
     gop(lambda: g.iota(T.cgr[:], [[1, 8], [0, 16]], 0, 0, allow_small_or_imprecise_dtypes=True), 128, ["~g1"], ["cgr", "~g2"])
     dma("s", [(T.StA[:, 64 * k:64 * k + 64, :], blk(T.mp, 1 + k)) for k in range(2)], [], ["StA", "~s0"], 131e3)
-    dma("a", [(T.StE[:], blk(T.mp, 0))], [], ["StE"], 0)
+    dma("a", [(T.IA[:, 0:128], blk(T.mp, 0))], [], ["IA0", "~a0"], 65e3)
     dma("s", [(T.StF[h::2], T.ft[:, 1024 * h:1024 * h + 1024]) for h in range(2)], ["~s0"], ["StF", "~s1"], 524e3)
     dma("s", [(T.MPB[:], T.mp[:, 256:896])], ["~s1"], ["MPB", "~s2"], 328e3)
-    dma("s", [(T.LdA[me, 64 * k:64 * k + 64, :], T.mp[mine, 128 + 128 * k:256 + 128 * k]) for k in range(2)] + [(T.LdE[me], T.mp[mine, 0:128])], ["~s2"], ["LdA", "~s3"], 24e3)
+    dma("s", [(T.LdA[me, 64 * k:64 * k + 64, :], T.mp[mine, 128 + 128 * k:256 + 128 * k]) for k in range(2)], ["~s2"], ["LdA", "~s3"], 16e3)
     dma("s", [(T.LdF[2 * me + h], T.ft[mine, 1024 * h:1024 * h + 1024]) for h in range(2)], ["~s3"], ["LdF"], 65e3)
-    dma("a", [(T.LM[0:1, 0:7], T.lam[0:1, :])], [], ["LM"], 0)
+    dma("a", [(T.LM[0:1, 0:7], T.lam[0:1, :])], ["~a0"], ["LM", "~a1"], 1e3)
     exchange("A", ["StA", "~g2"], PAR["A"])
-    exchange("E", ["StE", "~arA"], PAR["E"])
-    exchange("F", ["StF", "~arE"], PAR["F"])
-    gop(lambda: g.partition_broadcast(T.LB[:, 0:7], T.LM[0:1, 0:7], 128), 14, ["LM", "~arF"], ["LB", "~g3"])
-    gop(lambda: g.iota(T.WI[:], [[0, 2048]], 0, 0), 2048, ["~g3"], ["WI"])
-    ts(T.BT[:, 512:528], T.col[:, 0:16], 0.0, None, MUL, None, ["col"], ["BTw"])
-    cp("v", T.BT[:, 0:512], T.MPB[:, 128:640], ["MPB"], ["BT"], 512)
-    cp("v", T.BT[:, 512:519], T.LB[:, 0:7], ["LB"], ["BTw"])
-    dma("s", [(T.StB[:], T.BT[:]), (T.LdB[me], T.BT[mine, :])], ["BT", "BTw"], ["StB"], 160e3)
-    exchange("B", ["StB", "~arF"], PAR["B"])
+    exchange("F", ["StF", "~arA"], PAR["F"], 0)
+    gop(lambda: g.partition_broadcast(T.LB[:, 0:7], T.LM[0:1, 0:7], 128), 14, ["LM", "~arF0"], ["LB", "~g3"])
+    gop(lambda: g.iota(T.WI[:], [[0, 2048]], 0, 0), 2048, ["~g3"], ["WI", "~g4"])
+    exchange("F", ["StF", "arA", "~g4"], PAR["B"], 1)
+    ts(T.ET[:, 128:144], T.col[:, 0:16], 0.0, None, MUL, None, ["col"], ["ETw"])
+    cp("v", T.ET[:, 0:128], T.IA[:, 0:128], ["IA0"], ["ET"], 128)
+    cp("v", T.ET[:, 128:135], T.LB[:, 0:7], ["LB"], ["ETw"])
+    dma("s", [(T.StE[:], T.ET[:]), (T.LdE[me], T.ET[mine, :])], ["ET", "ETw"], ["StE"], 60e3)
+    exchange("E", ["StE", "~arF"], PAR["B"])
+    cp("v", T.BT[:], T.MPB[:, 128:640], ["MPB"], ["BT"], 512)
+    dma("s", [(T.StB[:], T.BT[:]), (T.LdB[me], T.BT[mine, :])], ["BT"], ["StB"], 160e3)
 
     stage(2)
     CC, PF = T.CC, T.PF
@@ -608,19 +1111,12 @@ def rank_program(g, core, T, topo):
     def mk_b(n, x, mask, key):
         ts(blk(T.BM, n, 8), T.col[:, 31:144:16], c1(CC, TB + x), mask, EQ, MUL, ["col", "TB", key], ["BM%d" % n])
 
-    for k in ("WM2", "WM3"):
-        memset(T[k][:], 0.0, [k], 1024)
-    memset(T.W[:, 2048:4096], 0.0, ["Wy"], 1024)
-    pm = {2: 0, 3: 2, 1: 4, 5: 6, 7: 8}
-    for x in pm:
-        onehot(blk(T.PM, pm[x]), x, 1.0 / 16, ["PM%d" % pm[x]])
-        onehot(blk(T.PM, pm[x] + 1), x, 128.0, ["PM%d" % (pm[x] + 1)])
-    ts(c1(CC, 96), I16, 0.0, None, EQ, None, ["PF"], ["R0"])
-    ts(T.BH[:], T.col[:, 31:144:16], c1(CC, TB + 2), c1(CC, 96), EQ, MUL, ["col", "TB", "R0"], ["BM0"])
-    mk_b(1, 3, c1(CC, RM + 0), "RM")
-    EYE, NEG, SWQ, SWP = [blk(T.PM, 10 + k) for k in range(4)]
-    for k, name in enumerate(("EYE", "NEG", "SWQ", "SWP")):
-        onehot(blk(T.PM, 10 + k), 4 * (k // 2), 1.0 - 2 * (k % 2), [name])
+    memset(T.WM1[:], 0.0, ["WM1"], 1024)
+    for t, k in ((T.WM3[:], "WM3"), (T.W[:, 2048:4096], "Wy")):
+        cp("a", t, T.WM1[:], ["WM1", "~a1"], [k], 2048)
+    EYE, NEG, SWQ = [blk(T.PM, k) for k in range(3)]
+    for k, name in enumerate(("EYE", "NEG", "SWQ")):
+        onehot(blk(T.PM, k), 4 * (k // 2), 1.0 - 2 * (k % 2), [name])
     for x in (0, 2, 3, 4, 5, 6, 7):
         onehot(blk(T.RT, x), x, 1.0, ["RT%d" % x])
     MASKS, SCALES = [1, 2, 4, 3, 6, 5], [1, 2, 4, 16, 32, 2048]
@@ -638,6 +1134,22 @@ def rank_program(g, core, T, topo):
                 return c1(BS, 12 * SCALES.index(s) + k)
 
     SBK = ["SB%d" % s for s in SCALES]
+    cp("v", T.RT[:, 128:130], T.RT[:, 0:2], ["RT0"], ["RT1"])
+    pm = {(2, 0): 0, (3, 0): 2, (2, 1): 4, (3, 1): 6, 1: 8, 5: 10, 7: 12}
+    par = BS[:, 0:7:6]
+    for k, v in enumerate((1.0 / 16 - 128, 128.0)):
+        ts(CC[:, 100 + 2 * k:102 + 2 * k], par, v, None, MUL, None, SBK, ["PW%d" % k])
+        for x in pm:
+            y, wt = (x[0], c1(CC, 101 + 2 * k - x[1])) if isinstance(x, tuple) else (x, v)
+            ts(blk(T.PH, pm[x] + k), col(0, 128), c1(CC, TG + y), wt, EQ, MUL, ["col", "PW%d" % k] + TGK, ["PM%d" % (pm[x] + k)])
+    ts(c1(CC, 96), I16, 0.0, None, EQ, None, ["PF"], ["R0"])
+    ts(CC[:, 104:106], par, c1(CC, 96), None, MUL, None, SBK + ["R0"], ["R0p"])
+    for k in range(2):
+        ts(blk(T.BH, k, 8), T.col[:, 31:144:16], c1(CC, TB + 2 + k), c1(CC, 105 - k), EQ, MUL, ["col", "TB", "R0p"], ["BH%d" % k])
+        ts(c1(CC, 106 + k), c1(CC, RM + 1 - k), c1(BS, 6 * k), None, MUL, None, SBK + ["RM"], ["RMp%d" % k])
+        mk_b(k, 2 + k, c1(CC, 106 + k), "RMp%d" % k)
+    ts(c1(CC, 108), bit(1, lambda a: 1 - (a >> 1 & 1)), bit(2, lambda a: a >> 2), bit(4, lambda a: a & 1), ADD, ADD, SBK, ["BHi"])
+    ts(T.BH[:, 16:24], col(0, 8), c1(CC, 108), c1(CC, 96), EQ, MUL, ["col", "BHi", "R0"], ["BHc"])
     ts(T.CI[:], col(0, 192), I16, -64.0, SUB, ADD, ["col", "PF"], ["CI"], 96)
     for d in range(1, 8):
         t = top(d)
@@ -647,55 +1159,83 @@ def rank_program(g, core, T, topo):
         ts(blk(T.FM, d - 1, 192), T.CI[:], bit(16, lambda a: GREATER[t].index(a ^ d) & 1, less), c1(CC, UB + d), SUB, EQ, ["CI", "UB%d" % d] + SBK, ["FM%d" % d], 96)
         ts(blk(T.GL, d - 1, 8), col(0, 8), bit(2 ** lo, lambda a: (GREATER[t][a & 3] ^ d) >> lo & 1), bit(2 ** hi, lambda a: (GREATER[t][a & 3] ^ d) >> hi & 1),
            SUB, EQ, ["col"] + SBK, ["GL%d" % d])
-        ts(T.RR[:, 16 * d - 16:16 * d - 8], T.col[:, 31:144:16], c1(CC, TB), None, EQ, None, ["col", "TB"], ["RRa%d" % d])
+        if d == 1:
+            ts(T.RR[:, 0:8], T.col[:, 31:144:16], c1(CC, TB), None, EQ, None, ["col", "TB"], ["RRa1"])
+        else:
+            cp("av", T.RR[:, 16 * d - 16:16 * d - 8], T.RR[:, 0:8], ["RRa1"], ["RRa%d" % d])
         ts(T.RR[:, 16 * d - 8:16 * d], T.col[:, 31:144:16], c1(CC, TB + d), None, EQ, None, ["col", "TB"], ["RRb%d" % d])
     for t in range(3):
         lo, hi = [k for k in range(3) if k != t]
         ts(blk(T.GL, 7 + t, 8), col(-2 ** t, 8), bit(2 ** lo, lambda a: GREATER[t][a & 3] >> lo & 1), bit(2 ** hi, lambda a: GREATER[t][a & 3] >> hi & 1),
            SUB, EQ, ["col"] + SBK, ["GG%d" % t])
-    if LONG["f"]:
-        for d in range(1, 8):
-            cp("a", T.GB[:, 16 * d - 16:16 * d - 8], blk(T.GL, d - 1, 8), ["GL%d" % d], ["GBa%d" % d])
-            cp("a", T.GB[:, 16 * d - 8:16 * d], blk(T.GL, 7 + top(d), 8), ["GG%d" % top(d)], ["GBb%d" % d])
-        ts(blk(T.GB, 1, 112), blk(T.GB, 0, 112), 2.0, None, MUL, None, ["GB%s%d" % (x, d) for x in "ab" for d in range(1, 8)], ["GB2"])
-        ts(blk(T.GB, 2, 112), blk(T.GB, 1, 112), -1.0, None, MUL, None, ["GB2"], ["GB"])
-    onehot(T.EF[:], 0, 1.0, ["EF"])
+    for d in range(1, 8):
+        for n, (k, key) in enumerate(((d - 1, "GL%d" % d), (7 + top(d), "GG%d" % top(d)), (d - 1, "GL%d" % d))):
+            cp("a", blk(T.GF, 3 * d - 3 + n, 8), blk(T.GL, k, 8), [key], ["GF%d%d" % (d, n)])
+    gf = ["GF%d%d" % (d, n) for n in range(3) for d in range(1, 8)]
+    node("nop", {"g": 0.0}, None, gf, ["GF"])
+    for k, v in ((1, 2.0), (2, -2.0)):
+        node("op", {"a": cyc(168)}, lambda q, k=k, v=v: g.scalar.activation(blk(T.GB, k, 168), T.GF[:], ACT.Copy, scale=v), gf + ["GB1"] * (k - 1), [("GB1", "GB")[k - 1]])
+    fill(T.K256[:], 256.0, ["K256"], 128)
+    fill(T.CO[:], 0.0, ["CO"], 24)
+    for x, v, n in ((slice(0, 3, 2), 1.0, 2), (slice(9, 11), 1.0, 2), (slice(13, 18, 4), 1.0, 2), (slice(4, 8), -1.0, 4), (slice(14, 16), -1.0, 2)):
+        fill(T.CO[:, x], v, ["CO"], n)
+    onehot(T.EF[:, 0:128], 0, 1.0, ["EF"])
+    cp("a", T.EF[:, 128:130], T.EF[:, 0:2], ["EF"], ["EF1"])
     for n, e in enumerate((2, 4, 6, 3, 5, 7)):
         mk_b(2 + n, 1, c1(CC, RM + (e ^ 1) - 2), "RM")
+    aff(T.UC[:, 16:24], CC[:, RM:RM + 8], -2048.0, 2048.0, ["RM"], ["NM"])
+    nuc = [0]
+
+    def by_pair(a, d, x, row, w):
+        t, k = top(d), nuc[0]
+        nuc[0] += 1
+        less = [y for y in range(8) if not (y ^ x) >> t & 1]
+        ts(c1(T.UC, k), bit(2, lambda y: GREATER[t].index(y ^ x ^ d) >> 1, less), bit(2048, lambda y: (y ^ x) >> t & 1), 0.0 if row is None else c1(T.UC, 16 + row),
+           ADD, ADD, SBK + ["NM"], ["UC%d" % k])
+        ts(T.BX[:, a:a + 4], col(0, 4), bit(1, lambda y: GREATER[t].index(y ^ x ^ d) & 1, less), c1(T.UC, k), SUB, EQ, ["col", "UC%d" % k] + SBK, w)
+
+    def by_rank(a, x, mask, w):
+        ts(T.BX[:, a:a + 8], T.col[:, 31:144:16], c1(CC, TB + x), mask, EQ, MUL, ["col", "TB", "RM"], w)
+
     for m in range(3):
-        for n, (x, v) in enumerate(((2 * m + 2, -4.0), (2 * m + 3, -5.0))):
-            mk_b(17 + 2 * m + n, x, c1(CC, RM + 7 - n), "RM")
-            ts(blk(T.BM, 17 + 2 * m + n, 8), blk(T.BM, 17 + 2 * m + n, 8), v, 5.0, MUL, ADD, [], ["BM%d" % (17 + 2 * m + n)])
-    memset(T.SS[:], 0.0, ["SS" + p for p in PH], 160)
-    memset(c1(CC, ONE), 1.0, ["ONE"])
-    ts(c1(CC, KH3), KH, -3.0, None, ADD, None, ["PF"], ["KH3"])
-    ts(c1(CC, KK), K1, -2.0, K7, MUL, ADD, ["PF"], ["KKa"])
+        e = 2 * m + 2
+        by_pair(4 * m, e, 1, e - 1, ["BN%d" % m])
+        by_pair(12 + 12 * m, e, e + 1, None, ["BFa%d" % m])
+        by_rank(16 + 12 * m, e + 1, 1.0, ["BFb%d" % m])
+        for n, v in enumerate((-4.0, -5.0)):
+            a, k = 48 + 24 * m, "BO%d%d" % (m, n)
+            by_pair(a + 20 * n, e + 1, e + n, 7 - n, [k + "a"])
+            by_rank(a + 4 + 8 * n, e + n, c1(CC, RM + 7 - n), [k + "b"])
+            aff(T.BX[:, a + 12 * n:a + 12 * n + 12], T.BX[:, a + 12 * n:a + 12 * n + 12], v, 5.0, [], [k + "a", k + "b"])
+    fill(T.SS[:], 0.0, ["SS" + p for p in PH], 192)
+    aff(c1(CC, KH3), KH, 1.0, -3.0, ["PF"], ["KH3"])
+    aff(c1(CC, KK), K1, -2.0, K7, ["PF"], ["KKa"])
     ts(c1(CC, KK + 1), K7, float(me), None, EQ, None, ["PF"], ["KKb"])
-    ts(c1(CC, KK + 2), I16, 3.0, 1.0, MUL, ADD, ["PF"], ["KKc"])
+    aff(c1(CC, KK + 2), I16, 3.0, 1.0, ["PF"], ["KKc"])
     ts(T.KM[0:64, 0:128], T.cgr[0:64, :], PF[0:64, 6:7], None, EQ, None, ["cgr", "PF"], ["KM0"], 128)
     ts(T.KM[0:64, 128:256], T.cgr[0:64, :], -1.0, CC[0:64, KK:KK + 1], ADD, EQ, ["cgr", "KKa"], ["KM1"], 128)
-    ts(T.KM[0:64, 256:384], T.cgr[0:64, :], 0.0, CC[0:64, KK + 1:KK + 2], MUL, ADD, ["cgr", "KKb"], ["KM2"], 128)
-    ts(CC[:, I3:I3 + 8], col(0, 8), 48.0, c1(CC, KK + 2), MUL, ADD, ["col", "KKc"], ["I3"])
-    memset(T.TH[:], 0.0, ["TH"])
-    memset(T.TH[:, 4:54:6], -0.5, ["TH"])
-    memset(T.TH[:, 5:54:6], -0.5, ["TH"])
+    aff(T.KM[0:64, 256:384], T.cgr[0:64, :], 0.0, CC[0:64, KK + 1:KK + 2], ["cgr", "KKb"], ["KM2"], 128)
+    aff(CC[:, I3:I3 + 8], col(0, 8), 48.0, c1(CC, KK + 2), ["col", "KKc"], ["I3"])
+    fill(T.TH[:, 0:54:2], 0.0, ["TH"], 27)
+    fill(T.TH[:, 4:54:6], -0.5, ["TH"], 9)
+    fill(T.TH[:, 5:54:6], -0.5, ["TH5"], 9)
     for t in range(3):
         for v in range(2):
             f = t == 0 and v == 1
-            ts(c1(T.TH, 12 * t + 6 * v + 1), bit(1, lambda a: (a >> t & 1) == f), -0.5, None, MUL, None, SBK, ["TH"])
-            ts(c1(T.TH, 12 * t + 6 * v + 3), bit(1, lambda a: (a >> t & 1) != f), -0.5, None, MUL, None, SBK, ["TH"])
+            aff(T.TH[:, 12 * t + 6 * v + 1:12 * t + 6 * v + 4:2], BS[:, t:t + 7:6], -0.5 if f else 0.5, 0.0 if f else -0.5, SBK, ["TH%d%d" % (t, v)])
     for m in range(3):
-        memset(c1(T.TH, 36 + 6 * m + (1 if me < (me ^ (2 * m + 3)) else 3)), -0.5, ["TH"])
-    ts(blk(T.H2, 7), col(0, 128), 16.0, None, MUL, None, ["col"], ["Hid"])
-    ts(blk(T.LO, 7), col(0, 128), 0.0, I16, MUL, ADD, ["col", "PF"], ["Lid"])
+        aff(T.TH[:, 37 + 6 * m:40 + 6 * m:2], col(0, 2), *((0.5, -0.5) if me < (me ^ (2 * m + 3)) else (-0.5, 0.0)), ["col"], ["TH3%d" % m])
+    THK = ["TH", "TH5"] + ["TH%d%d" % (t, v) for t in range(4) for v in range(2 + (t == 3))]
+    aff(blk(T.H2, 7), col(0, 128), 16.0, 0.0, ["col"], ["Hid"], 128)
+    aff(blk(T.LO, 7), col(0, 128), 0.0, I16, ["col", "PF"], ["Lid"], 128)
     for m in range(3):
         cp("v", T.OWN[:, 384 * m:384 * m + 384:3], blk(T.MPB, 2 * m), ["MPB"], ["OW0%d" % m], 128)
 
     def X(d):
-        return blk(T.XA, d - 1) if d < 4 else blk(T.IB, d - 4)
+        return blk(T.IE, 0) if d == 1 else blk(T.XA, d - 1) if d < 4 else blk(T.IB, d - 4)
 
     def xk(d):
-        return "XA%d" % (d > 1) if d < 4 else "IB"
+        return "XA%d" % d if d < 4 else "IB"
 
     def wrows(win, items, key, qs="s", r=()):
         mv, r = [], list(r)
@@ -704,10 +1244,20 @@ def rank_program(g, core, T, topo):
             r += ["H%s" % k, "L%s" % k]
         dma(qs, mv, r, key, 90e3 * len(mv))
 
-    def places(s, n, k, x):
-        j = pm[x]
-        o = ps(s, 128 * n, 128 * n + 128)
-        pe([(o, blk(T.PM, j), blk(T.H2, POS[k]), 128), (o, blk(T.PM, j + 1), blk(T.LO, POS[k]), 128)], ["PM%d" % j, "PM%d" % (j + 1), "H%s" % k, "L%s" % k], [s])
+    def split(k, tile, key, n=1):
+        h, l, ks = blk(T.H2, POS[k], 128, n), blk(T.LO, POS[k], 128, n), [k] if n == 1 else range(k, k + n)
+        ts(h, tile, 8.0, None, ADD, None, [key], ["H%s" % x for x in ks], 64 * n)
+        vop(lambda: V.tensor_tensor_scan(l, tile, h, 0.0, ALU.max, SUB), [key, "H%s" % k], ["L%s" % x for x in ks], 64 * n)
+
+    SHIFT = 2064 * (128 - 1.0 / 16)
+
+    def sixteen(k, tile, key):
+        ts(blk(T.HB, POS[k]), tile, 2056.5, None, ADD, None, [key], ["HB%s" % k])
+
+    def places(s, parts):
+        o = ps(s, 0, 128)
+        pe([m for k, x, tile, key in parts for m in ((o, blk(T.PH, pm[x] + 1), tile, 128), (o, blk(T.PH, pm[x]), blk(T.HB, POS[k]), 128))],
+           [y for k, x, tile, key in parts for y in ("PM%d" % pm[x], "PM%d" % (pm[x] + 1), "HB%s" % k, key)], [s])
 
     def gather2(out, win, wk, lst, a, lk, name):
         for h in range(2):
@@ -715,87 +1265,139 @@ def rank_program(g, core, T, topo):
                int(1024 * PAR["gat"]) + 60)
             call(name + "ab"[h])
 
-    def turn(rb, b, n):
+    def turn(parts, n):
         s = slot("C")
         mms = []
         for i in range(16):
-            mms += [(ps(s, i, 128 * n, 128, 16), T[rb][:, i::16], blk(T.BM, b, 8, n) if b else T.BH[:], 64), None]
-        pe(mms[:-1], [rb + "_0", rb + "_1"] + ["BM%d" % (b + k) for k in range(n)], [s])
+            mms += [(ps(s, i, 16 * n, 128, 16), T[rb][:, i::16], m, 64) for rb, m, k in parts] + [None]
+        pe(mms[:-1], [y for rb, m, k in parts for y in [rb + "_0", rb + "_1"] + k], [s])
+        return s
+
+    def turned(s, a, b, n):
         wide = b in PAR["wide"]
-        cp("a" if wide else "v", blk(T.ZF if wide else T.ZH, b, 128, n), ps(s, 0, 128 * n), [s], ["Z%d" % (b + k) for k in range(n)], 128 * n)
+        cp("a" if wide else "v", blk(T.ZF if wide else T.ZH, b, 128, n), ps(s, a, a + 128 * n), [s], ["Z%d" % (b + k) for k in range(n)], 128 * n)
         for k in range(n):
             zt[b + k] = wide
+
+    def paired(s, a, items, more=()):
+        k = [PAIRED.index(x) for x in items]
+        wide = items[0] in PAR["widec"]
+        zb, eye, ek, f = (T.CZ, T.EF, ["EF", "EF1"], 4) if wide else (T.CH, T.RT, ["RT0", "RT1"], 1)
+        cp("a" if wide else "v", blk(zb, k[0], 64, len(k)), ps(s, a, a + 64 * len(k)), [s], ["C%d%d" % x for x in items], 64 * len(k))
+        for n, (d, c) in zip(k, items):
+            s, fm, mms = slot("C"), T.FM[:, 192 * d - 128:192 * d - 64], []
+            for b, o, x, w in ((0, 0, 0, 66), (1, 0, 64, 64), (1, 64, 0, 2)) if more else ((0, 0, 0, 66), (1, 0, 64, 66)):
+                out = ps(s, o, o + w, 64 * b + 64, 1, 64 * b)
+                mms += [(out, fm, t(x, w), 64) for t, tk in more] + [(out, blk(zb, n, 64), eye[:, x:x + w], 66 * f), None]
+            pe(mms[:-1], ["C%d%d" % (d, c), "FM%d" % d] + ek + [tk for t, tk in more], [s])
+            t = top(d)
+            ts(T.FL[:, fcol(d, c):fcol(d, c) + 66], ps(s, 0, 66), bit(2048, lambda y: 1 - GREATER[t][y & 3] % 2) if t else 0.0, None, ADD, None, [s] + SBK, ["FL%d%d" % (d, c)], 66)
 
     zt = {}
 
     def to_tile(b, more=(), mk=()):
         s = slot("C")
         o = ps(s, 0, 128)
-        pe([(o, blk(T.ZF, b), T.EF[:], 512) if zt[b] else (o, blk(T.ZH, b), blk(T.RT, 0), 128)] + [(o, a, c, 128) for a, c in more], ["Z%d" % b, "RT0", "EF"] + list(mk), [s])
+        pe([(o, blk(T.ZF, b), T.EF[:, 0:128], 512) if zt[b] else (o, blk(T.ZH, b), blk(T.RT, 0), 128)] + [(o, a, c, 128) for a, c in more], ["Z%d" % b, "RT0", "EF"] + list(mk), [s])
         return s, o
 
     def fcol(d, c):
-        return 64 * (7 * c + d - 1)
+        return 66 * (7 * c + d - 1)
 
     def lists(c, items):
         s = slot("C")
         for n, (d, tile, key) in enumerate(items):
-            o = ps(s, 64 * n, 64 * n + 64)
-            f = 192 * (d - 1)
-            pe([(o, T.FM[:, f + 64:f + 192], tile(0), 64), (o, T.FM[:, f:f + 128], tile(64), 64)], ["FM%d" % d, key], [s])
+            f, o = 192 * (d - 1), 66 * n
+            lo, hi = T.FM[:, f + 64:f + 192], T.FM[:, f:f + 128]
+            pe([(ps(s, o, o + 64), lo, tile(0, 64), 64), (ps(s, o, o + 64), hi, tile(64, 64), 64), None,
+                (ps(s, o + 64, o + 66), lo, tile(64, 2), 64), (ps(s, o + 64, o + 66), hi, tile(0, 2), 64)], ["FM%d" % d, key], [s])
         a = fcol(items[0][0], c)
         t = top(items[0][0])
-        ts(T.FL[:, a:a + 64 * len(items)], ps(s, 0, 64 * len(items)), bit(2048, lambda g: 1 - GREATER[t][g & 3] % 2) if t else 0.0, None, ADD, None,
-           [s] + SBK, ["FL%d%d" % (it[0], c) for it in items], 64 * len(items))
+        ts(T.FL[:, a:a + 66 * len(items)], ps(s, 0, 66 * len(items)), bit(2048, lambda g: 1 - GREATER[t][g & 3] % 2) if t else 0.0, None, ADD, None,
+           [s] + SBK, ["FL%d%d" % (it[0], c) for it in items], 66 * len(items))
 
     def half(t, k):
-        return lambda a: t[:, 128 * k + a:128 * k + a + 64]
+        return lambda a, n: t[:, 128 * k + a:128 * k + a + n]
 
     def xhalf(d):
-        return half(T.XA, d - 1) if d < 4 else half(T.IB, d - 4)
+        return half(T.IE, 0) if d == 1 else half(T.XA, d - 1) if d < 4 else half(T.IB, d - 4)
 
     def judge(d, c):
         t = "T%d" % (3 * d + c - 3)
         a = fcol(d, c)
         wn = "W%d" % (d > 1)
         act = on("g%d%d" % (d, c)) == "a"
-        f = 1024 * d - 1024
-        for x, y, w in ((0, 34, "a"), (34, 64, "b")) if 10 * d + c in PAR["cut"] else ((0, 64, "ab"),):
-            src, cost, w = T.W[:, 0:4096 if d > 1 else 2048].indirect(T.FL[:, a + x:a + y]), int(16 * (y - x) * PAR["gat"]) + 60, [t + k for k in w]
-            if act:
-                cp("a", tb(t, 16 * x, 16 * y), src, [wn, "FL%d%d" % (d, c)], w, cost)
-            else:
-                tt(tb(t, 16 * x, 16 * y), src, T.FR[:, f + 16 * x:f + 16 * y], SUB, [wn, "FL%d%d" % (d, c), "FR%d" % d], w, cost)
-            if x == 0:
-                call("g%d%d" % (d, c))
-        for h, parts in enumerate((((0, 512),), ((512, 511), (1023, 1)))):
-            s, mms = slot("C"), []
-            for o, k in parts:
-                nx, out, n = o + 1 if k > 1 else 0, ps(s, o - 512 * h, o - 512 * h + k), max(k, 64)
-                if act:
-                    mms += [(out, NEG, T.FR[:, f + o:f + o + k], n), (out, EYE if k > 1 else SWQ, T.FR[:, f + nx:f + nx + k], n)]
-                mms += [(out, EYE, tb(t, o, o + k), n), (out, NEG if k > 1 else SWP, tb(t, nx, nx + k), n), None]
-            pe(mms[:-1], [t + "a", "EYE", "NEG", "SWP", "SWQ", "FR%d" % d] + [t + "b"] * h, [s])
-            size(s, c1(T.AC, 6 * d + 2 * c + h - 6), "s%d%d" % (d, c), "AC%d%d%d" % (d, c, h))
-            call("st"[h] + "%d%d" % (d, c))
+        f = 1040 * d - 1040
+        win = T.W[:, 0:4096 if d > 1 else 2048]
+        src, cost, fr, fk = win.indirect(T.FL[:, a:a + 65]), int(1040 * PAR["gat"]) + 60, T.FR[:, f:f + 1040], ["FR%d" % d, "FX%d" % d]
+        m = 3 * d + c - 3
+        mm = blk(T.MM, m, 1040)
+        e = tb(t, 0, 1040)
 
-    def size(s, acc, name, key):
-        def f(q):
-            if q == "v":
-                return V.tensor_reduce(acc, z(ps(s, 0, 512)), AxisListType.X, ADD, apply_absolute_value=True)
-            return g.scalar.activation(blk(T.JK, POOLS["C"].index(val[s]), 512), z(ps(s, 0, 512)), ACT.Abs, accum_out=acc)
-        node("op", {on(name): cyc(512) + 0.02}, f, [s], [key])
+        def sel(x, k):
+            o = 168 * k + 24 * d - 24 + 8 * (c == 1)
+            return x[:, o:o + 16]
+
+        if "g%d%d" % (d, c) in LONG["p"]:
+            for x, y, w in ((0, 34, "a"), (34, 65, "b")):
+                cp("a", tb(t, 16 * x, 16 * y), win.indirect(T.FL[:, a + x:a + y]), [wn, "FL%d%d" % (d, c)], [t + w, "~" + t + w] + ["~" + t + "a"] * (x > 0), int(16 * (y - x) * PAR["gat"]) + 60)
+                call("gh"[x > 0] + "%d%d" % (d, c))
+            for h in range(2):
+                s, x = slot("C"), 512 * h
+                o = ps(s, 0, 512)
+                pe([(o, NEG, T.FR[:, f + x:f + x + 512], 512), (o, EYE, T.FR[:, f + x + 1:f + x + 513], 512)], ["EYE", "NEG"] + fk, [s], stop=False)
+                pe([(o, EYE, tb(t, x, x + 512), 512), (o, NEG, tb(t, x + 1, x + 513), 512)], [t + "a", "EYE", "NEG"] + [t + "b"] * h, [s], start=False)
+                node("op", {"a": cyc(512) + 0.02}, lambda q, o=o, h=h: g.scalar.activation(T.MM[:, 1040 * m + 512 * h:1040 * m + 512 * h + 512], z(o), ACT.Abs, accum_out=c1(T.AC, 2 * m + h)),
+                     [s], ["AC%d%d" % (m, h)])
+                call("ab"[h] + "%d%d" % (d, c))
+
+            def sums(s, a, start, stop):
+                o = ps(s, a, a + 16)
+                mms = [[(o, u[:, x + 128 * i:x + 128 * i + 128], sel(T.GB, 1 + k), 64) for i in range(8)] for k, (u, x) in enumerate(((T.TT, 1040 * m), (T.FR, f)))]
+                pe(mms[0] + mms[1][1:], [t + "a", t + "b", "GB"] + fk, [s], start=start, stop=False)
+                pe([(ps(s, a, a + 16, 2), blk(T.AC, m, 2), sel(T.GF, 0), 64), mms[1][0]], ["AC%d0" % m, "AC%d1" % m, "GF"], [s], start=False, stop=stop)
+            return sums
+        dmas = "g%d%d" % (d, c) in LONG["d"]
+        if dmas:
+            node("op", {"a": cyc(cost)}, lambda q: g.scalar.activation(e, src, ACT.Copy, scale=-1.0), [wn, "FL%d%d" % (d, c)], [t])
+            call("g%d%d" % (d, c))
+            node("dma", {"g": PAR["gdma"]}, [(e, fr)], fk + [t], [t], PAR["dma"] + 0.4, 530e3)
+        elif act:
+            node("op", {"a": cyc(cost)}, lambda q: g.scalar.activation(mm, src, ACT.Identity, bias=32.0), [wn, "FL%d%d" % (d, c)], ["M" + t])
+            call("g%d%d" % (d, c))
+            vop(lambda: V.tensor_tensor_scan(tb(t, 0, 1026), T.FR[:, f:f + 1026], T.MM[:, 1040 * m:1040 * m + 1026], 0.0, ALU.max, SUB), ["M" + t] + fk, [t], 513)
+            call("u%d%d" % (d, c))
+        else:
+            tt(e, src, fr, SUB, [wn, "FL%d%d" % (d, c)] + fk, [t], cost)
+            call("g%d%d" % (d, c))
+        vop(lambda: V.tensor_tensor_scan(T.MM[:, 1040 * m:1040 * m + 1024], tb(t, 0, 1024), tb(t, 1, 1025), -64.0 if act else 64.0,
+                                         *((ALU.max, ALU.min) if act else (ALU.min, ALU.max))), [t], ["M" + t], 512)
+        call("s%d%d" % (d, c))
+
+        def sums(s, a, start, stop):
+            o, w = ps(s, a, a + 16), sel(T.GB, 1 + act)
+            pe([(o, T.MM[:, 1040 * m + 128 * k:1040 * m + 128 * k + 128], w, 64) for k in range(8)] + [(o, T.K256[:], w, 64)] * (act and not dmas),
+               ["M" + t, "GB", "K256"], [s], start, stop)
+        return sums
+
+    def first(d):
+        sums = judge(d, 0)
+        s = slot("C")
+        sums(s, 0, True, True)
+        cp("va", blk(T.CF, d - 1, 16), ps(s, 0, 16), [s], ["CF%d" % d])
 
     def tile_out(s, o, d, c, dst, key, other, okey):
         cp("v", blk(*dst), o, [s], [key], 128)
         tt(blk(T.NE, 2 * d + c - 3), o, other, ALU.not_equal, [s, okey], ["NE%d%d" % (d, c)], 128)
-        lists(c, [(d, half(*dst), key)])
 
-    def counts(d):
+    def counts(d, cs):
+        sums = [judge(d, c) for c in cs]
         s = slot("C")
         a = 16 * d - 16
         pe([(ps(s, 0, 8), blk(T.NE, 2 * d - 1), T.GW[:, a:a + 8], 64), None, (ps(s, 8, 24), blk(T.NE, 2 * d - 2), T.GW[:, a:a + 16], 64)],
-           ["NE%d1" % d, "NE%d2" % d, "GW%d" % d], [s])
+           ["NE%d1" % d, "NE%d2" % d, "GW%d" % d], [s], stop=False)
+        sums[0](s, 8, False, False)
+        sums[1](s, 8, False, True)
         cp("va", blk(T.CW, d - 1, 24), ps(s, 0, 24), [s], ["CW%d" % d])
 
     def scores(ph, ds):
@@ -803,18 +1405,12 @@ def rank_program(g, core, T, topo):
         k = "SS" + ph
         for m, d in enumerate(ds):
             s = slot("C")
-            gl, gg = blk(T.GL, d - 1, 8), blk(T.GL, 7 + top(d), 8)
-            mms = []
-            for c, (x, y, w) in enumerate(((0, 0, 0), (1, 2, 16), (2, 1, 8))):
-                o = ps(s, 3 * m + c, 3 * m + c + 1, 8)
-                mms += [(o, T.CW[:, 24 * d - 24 + w:24 * d - 16 + w], c1(CC, ONE), 32)]
-                mms += [(o, a, c1(T.AC, 6 * d - 6 + 2 * u + h), 32) for a, u in ((gl, x), (gg, y)) for h in range(2)] + [None]
-            pe(mms[:-1], ["CW%d" % d, "ONE", "GL%d" % d, "GG%d" % top(d)] + ["AC%d%d%d" % (d, c, h) for c in range(3) for h in range(2)], [s])
-            b = 3 * m
-            for n, (i0, i1, st, sc) in enumerate(((b, b + 3, 2, b + 1), (b, b + 2, 1, b + 2), (b + 1, b + 3, 1, b))):
-                ts(T.SS[0:8, a + 6 * m + 2 * n:a + 6 * m + 2 * n + 2], ps(s, i0, i1, 8, st), ps(s, sc, sc + 1, 8), None, SUB, None, [s, k], [k + "%d%d" % (m, n)])
+            o = ps(s, 0, 6, 8)
+            pe([(o, blk(T.CF, 2 * d - 2 + n, 8), blk(T.CO, 0, 6), 32) for n in range(2)] + [(o, blk(T.CW, 3 * d - 3 + n, 8), blk(T.CO, c, 6), 32) for n, c in enumerate((0, 2, 1))],
+               ["CW%d" % d, "CO", "CF%d" % d], [s])
+            cp("va", T.SS[0:8, a + 6 * m:a + 6 * m + 6], o, [s, k], [k + str(m)])
         ld = "LdS" + ph
-        dma("s", [(T[ld][me], T.SS[0:8, a:a + 32])], [k] + [k + "%d%d" % (m, n) for m in range(len(ds)) for n in range(3)], [ld], 1e3)
+        dma("s", [(T[ld][me], T.SS[0:8, a:a + 32])], [k] + [k + str(m) for m in range(len(ds))], [ld], 1e3)
         exchange("S" + ph, [ld], PAR["S"])
         dma("s", [(T.SC[0:64, a:a + 32], T[ld][:])], [ld, "arS" + ph], ["SC" + ph], 8e3)
 
@@ -826,7 +1422,7 @@ def rank_program(g, core, T, topo):
             mms += [(ps(s, n, n + w), T.KM[0:64, 128 * km:128 * km + 128], T.SC[0:64, a:a + w], 256), None]
             n += w
         pe(mms[:-1], ["SC" + ph, "KM0", "KM1", "KM2"], [s])
-        tt(T.DE[:, a:a + n], ps(s, 0, n), T.TH[:, th:th + n], GT, [s, "TH"], ["x" + ph])
+        tt(T.DE[:, a:a + n], ps(s, 0, n), T.TH[:, th:th + n], GT, [s] + THK, ["x" + ph])
         tt(T.DE[:, a + 20:a + 20 + n // 2], T.DE[:, a:a + n:2], T.DE[:, a + 1:a + n:2], MUL, ["x" + ph], ["y" + ph])
         return (lambda i: c1(T.DE, a + 20 + i)), "y" + ph
 
@@ -870,45 +1466,53 @@ def rank_program(g, core, T, topo):
 
     stage(1)
     dma("s", [(blk(T.IA, 1 + k), T.LdA[:, 64 * k:64 * k + 64, :]) for k in range(2)], ["LdA", "arA"], ["IA1"], 131e3)
-    dma("a", [(T.WI[0::16, :], T.LdA[:, 64:128, :])], ["LdA", "arA"], ["WI"], 65e3)
-    dma("s", [(blk(T.IA, 0), T.LdE[:])], ["LdA", "arE"], ["IA0"], 65e3)
-    for a, n, ds in ((1, 2, (2, 3)), (0, 1, (1,))):
-        addc("v", blk(T.HB, a, 128, n), blk(T.IA, a, 128, n), 2056.5, ["IA%d" % a], ["HB%d" % a], 128 * n, False)
-        ts(blk(T.AN, a, 128, n), blk(T.IA, a, 128, n), 15, None, ALU.bitwise_and, None, ["IA%d" % a], ["AN%d" % a], 128 * n)
-        cp("v", blk(T.XA, a, 128, n), blk(T.IA, a, 128, n), ["IA%d" % a], ["XA%d" % a], 128 * n)
-        addc("va", blk(T.H2, a, 128, n), blk(T.HB, a, 128, n), -2064.0, ["HB%d" % a], ["H%d" % d for d in ds], 128 * n, True)
-        cp("v", blk(T.LO, a, 128, n), blk(T.AN, a, 128, n), ["AN%d" % a], ["L%d" % d for d in ds], 128 * n)
-    wrows("WM2", [("id", 6)], ["WM2c"], "s", ["WM2"])
-    wrows("WM2", [(2, 0)], ["WM1a", "~wm"], "s", ["WM2"])
-    wrows("WM2", [(3, 1)], ["WM1b"], "a", ["WM2"])
-    s = slot("C")
-    places(s, 0, 2, 2)
-    places(s, 1, 3, 3)
-    cp("v", T.LQ[:, 0:256], ps(s, 0, 256), [s], ["LQ23"], 256)
-    dma("s", [(T.IB[:], T.LdB[:])], ["StB", "arB"], ["IB"], 135e3)
+    dma("a", [(T.WI[0::32, :], T.LdA[0::2, 64:128, :]), (T.WI[16::32, :], T.LdA[1::2, 0:64, :])], ["LdA", "arA"], ["WI"], 65e3)
+    dma("s", [(T.IE[:], T.LdE[:])], ["StE", "arE"], ["XA1"], 50e3)
+    for d in (2, 3):
+        cp("v", X(d), blk(T.IA, d - 1), ["IA1"], [xk(d)], 128)
+    for d in (2, 3, 1):
+        split(d, X(d), xk(d))
+    wrows("WM1", [(2, 0), (3, 1)], ["WM1"], "s", ["WM1"])
+    for d in (2, 3):
+        sixteen(d, X(d), xk(d))
+
+    def recode(parts, n, key):
+        s = slot("C")
+        places(s, parts)
+        ts(blk(T.LQ, n), ps(s, 0, 128), SHIFT, None, ADD, None, [s], [key], 128)
+
+    recode([(d, (d, 0), X(d), xk(d)) for d in (2, 3)], 0, "LQ0")
+    recode([(d, (d, 1), X(d), xk(d)) for d in (2, 3)], 4, "LQ1")
+    recode([(3, (3, o), X(3), xk(3)) for o in range(2)], 1, "LQ3")
     stage("w0")
-    dma("s", feats(T.W, 0, GREATER[0], lambda b: (0, 1)), ["LdF", "arF", "~wm"], ["W0"], 524e3)
+    dma("s", feats(T.W, 0, GREATER[0], lambda b: (0, 1)), ["LdF", "arF"], ["W0"], 524e3)
     stage("w1")
-    dma("s", feats(T.W, 2048, [7 - j for j in GREATER[0][:3]], lambda b: (0, 1)), ["LdF", "arF", "~wm"], ["Wy"], 393e3)
+    dma("s", feats(T.W, 2048, [7 - j for j in GREATER[0][:3]], lambda b: (0, 1)), ["LdF", "arF"], ["Wy"], 393e3)
     node("nop", {"g": 0.0}, None, ["W0", "Wy"], ["W1"])
     for d in range(1, 8):
         stage("f%d" % d)
-        dma("s", feats(T.FR, 1024 * d - 1024, [j ^ d for j in GREATER[top(d)]], lambda b: (b,)), ["LdF", "arF", "~wm"], ["FR%d" % d], 262e3)
-    stage(10)
+        f = 1040 * d - 1040
+        dma("s", feats(T.FR, f, [j ^ d for j in GREATER[top(d)]], lambda b: (b,)), ["LdF", "arF"], ["FR%d" % d], 262e3)
+        s = slot("C")
+        pe([(ps(s, 0, 16), SWQ, T.FR[:, f:f + 16], 64)], ["SWQ", "FR%d" % d], [s])
+        cp("va", T.FR[:, f + 1024:f + 1040], ps(s, 0, 16), [s], ["FX%d" % d])
+    exchange("B", ["StB", "~arE"] + PAR["Bafter"], PAR["B"])
+    dma("s", [(T.IB[:], T.LdB[:])], ["StB", "arB"], ["IB"], 135e3)
     for h in range(2):
-        cp("v", blk(T.RA, h, 1024), T.WI[:, :].indirect(blk(T.LQ, h, 64)), ["WI", "LQ23"], ["RA_%d" % h], int(1024 * PAR["gat"]) + 60)
-    gather2("RB", "WM2", ["WM1a", "WM1b", "WM2c", "WM2b"], T.LQ, 128, "LQ23", "B")
-    for c, (rb, k, dst) in enumerate((("RA", "A", (T.NT, 1)), ("RB", "B", (T.FT, 1)))):
-        turn(rb, c, 1)
+        cp("v", blk(T.RA, h, 1024), T.WI[:, :].indirect(blk(T.LQ, h, 64)), ["WI", "LQ0"], ["RA_%d" % h], int(1024 * PAR["gat"]) + 60)
+        call("R" + "ab"[h])
+    paired(turn([("RA", T.BH[:, 16:24], ["BHc"])], 8), 0, [(1, 1), (1, 2)])
+    gather2("RB", "WM1", ["WM1", "WM2b", "WM2c"], T.LQ, 512, "LQ1", "B")
+    turned(turn([("RA", T.BH[:, 0:16], ["BH0", "BH1"]), ("RB", T.BM[:, 0:16], ["BM0", "BM1"])], 16), 0, 0, 2)
+    for c, (k, dst) in enumerate((("A", (T.NT, 1)), ("B", (T.FT, 1)))):
         s, o = to_tile(c)
-        tile_out(s, o, 1, c + 1, dst, "NF"[c] + "1", (X(1), blk(T.NT, 1))[c], ("XA0", "N1")[c])
-        addc("va", blk(T.HB, POS[k]), o, 2056.5, [s], ["HB" + k], 128, False)
-        addc("va", blk(T.H2, POS[k]), blk(T.HB, POS[k]), -2064.0, ["HB" + k], ["H" + k], 128, True)
-        tt(blk(T.LO, POS[k]), o, blk(T.H2, POS[k]), SUB, [s, "H" + k], ["L" + k], 128)
-    lists(0, [(1, xhalf(1), "XA0")])
-    lists(0, [(d, xhalf(d), "XA1") for d in (2, 3)])
+        cp("v", blk(*dst), o, [s], ["NF"[c] + "1"], 128)
+        tt(blk(T.NE, c), o, (X(1), blk(T.NT, 1))[c], ALU.not_equal, [s, ("XA1", "N1")[c]], ["NE1%d" % (c + 1)], 128)
+        split(k, blk(*dst), "NF"[c] + "1")
+    lists(0, [(1, xhalf(1), "XA1")])
+    lists(0, [(d, xhalf(d), xk(d)) for d in (2, 3)])
     lists(0, [(d, xhalf(d), "IB") for d in (4, 5, 6, 7)])
-    ts(T.WF[:, 0:7], T.IB[:, 512:519], -1.0, None, MUL, None, ["IB"], ["WF"])
+    ts(T.WF[:, 0:7], T.IE[:, 128:135], -1.0, None, MUL, None, ["XA1"], ["WF"])
 
     def weigh(d):
         def f(q):
@@ -919,69 +1523,59 @@ def rank_program(g, core, T, topo):
 
     for d in range(1, 8):
         weigh(d)
-    addc("v", blk(T.HB, 3, 128, 4), T.IB[:, 0:512], 2056.5, ["IB"], ["HB3"], 512, True)
-    addc("va", blk(T.H2, 3, 128, 4), blk(T.HB, 3, 128, 4), -2064.0, ["HB3"], ["H4", "H5", "H6", "H7"], 512, True)
-    s = slot("C")
-    pe([(ps(s, 0, 512), blk(T.RT, 0), T.IB[:, 0:512], 512), (ps(s, 0, 512), NEG, blk(T.H2, 3, 128, 4), 512)], ["RT0", "NEG", "IB", "H4", "H5", "H6", "H7"], [s])
-    cp("va", blk(T.LO, 3, 128, 4), ps(s, 0, 512), [s], ["L4", "L5", "L6", "L7"], 512)
+    split(4, T.IB[:, 0:512], "IB", 4)
     stage("r1")
-    for c in (1, 2, 0):
-        judge(1, c)
-    counts(1)
+    first(1)
+    counts(1, (1, 2))
     scores("1", [1])
 
     stage(10)
     wrows("WM3", [(1, 2)], ["WM3a"], "s", ["WM3"])
     wrows("WM3", [("A", 3), ("B", 4)], ["WM3b"], "s", ["WM3"])
     stage("wm")
-    wrows("WM2", [(4, 2), (5, 3), (6, 4), (7, 5)], ["WM2b"], "s", ["WM2"])
+    wrows("WM1", [("id", 6)], ["WM2c"], "s", ["WM1"])
+    wrows("WM1", [(4, 2), (5, 3), (6, 4), (7, 5)], ["WM2b"], "s", ["WM1"])
     stage(10)
-    s = slot("C")
-    places(s, 0, 5, 5)
-    places(s, 1, 7, 7)
-    cp("v", T.LQ[:, 256:512], ps(s, 0, 256), [s], ["LQ57"], 256)
-    stage(13)
-    s = slot("C")
-    for c, k in enumerate((1, "A", "B")):
-        places(s, c, k, 1)
-    for c in range(3):
-        cp("a", T.PI1[:, c:384:3], ps(s, 128 * c, 128 * c + 128), [s], ["PI1%d" % c], 128)
+    for d in (5, 7):
+        sixteen(d, X(d), "IB")
+        recode([(d, d, X(d), "IB")], d // 2, "LQ%d" % d)
+    for c, (k, tile, key) in enumerate(((1, X(1), "XA1"), ("A", blk(T.NT, 1), "N1"), ("B", blk(T.FT, 1), "F1"))):
+        sixteen(k, tile, key)
+        s = slot("C")
+        places(s, [(k, 1, tile, key)])
+        addc("va", T.PI1[:, c:384:3], ps(s, 0, 128), SHIFT, [s], ["PI1%d" % c], 128, False)
     for m in range(3):
-        stage("rf%d" % m)
-        gather2("RF%d" % m, "WM3", ["WM3a", "WM3b"], T.LQ, 128 + 128 * m, "LQ57" if m else "LQ23", "F%d" % (2 * m + 2))
+        gather2("RF%d" % m, "WM3", ["WM3a", "WM3b"], T.LQ, 128 + 128 * m, "LQ%d" % (2 * m + 3), "F%d" % (2 * m + 2))
     for d in (2, 4, 6, 3, 5, 7):
         stage("c%d" % d)
-        judge(d, 0)
+        first(d)
 
     stage("rn")
     ind, key = decide("1", [(0, 6), (1, 6)], 0)
     pick(T.LN[:], T.PI1[:, :], 0, ind, 3, key, ["PI10", "PI11", "PI12"], ["LN"])
-    gather2("RN", "WM2", ["WM1a", "WM1b", "WM2b", "WM2c"], T.LN, 0, "LN", "N")
+    gather2("RN", "WM1", ["WM1", "WM2b", "WM2c"], T.LN, 0, "LN", "N")
     ts(c1(T.DE, 28), ind(1), ind(2), c1(CC, KH3), SUB, EQ, [key, "KH3"], ["sel"])
     dma("s", [(T.RB[12 + i::16, :], T.RN[12 + i::16, :]) for i in range(2)]
         + [(T.RB[16 * (1 - b) + 14 + i::32, :], T.RN[16 * b + 12 + i::32, :]) for b in range(2) for i in range(2)], ["RN_0", "RN_1"], ["RB_0", "RB_1"], 131e3)
-    turn("RN", 2, 3)
+    paired(turn([("RN", T.BX[:, 0:12], ["BN0", "BN1", "BN2"])], 12), 0, [(2, 1), (4, 1), (6, 1)])
+    turned(turn([("RN", T.BM[:, 16:40], ["BM2", "BM3", "BM4"])], 24), 0, 2, 3)
+    mul("va", T.BX[:, 120:156], T.BX[:, 12:48], c1(T.DE, 28), ["sel"] + ["BF%s%d" % (x, m) for x in "ab" for m in range(3)], ["BF"])
     for m in range(3):
         d = 2 * m + 2
-        stage("t%d" % d)
-        mk_b(8 + m, d + 1, c1(T.DE, 28), "sel")
-        turn("RF%d" % m, 8 + m, 1)
+        s = turn([("RF%d" % m, T.BX[:, 120 + 12 * m:132 + 12 * m], ["BF"])], 12)
+        paired(s, 0, [(d, 2)])
+        turned(s, 64, 8 + m, 1)
         s, o = to_tile(8 + m)
         cp("v", blk(T.FT, d), o, [s], ["F%d" % d], 128)
-        lists(2, [(d, half(T.FT, d), "F%d" % d)])
         s, o = to_tile(2 + m)
         tile_out(s, o, d, 1, (T.NT, d), "N%d" % d, X(d), xk(d))
         tt(blk(T.NE, 2 * d - 1), o, blk(T.FT, d), ALU.not_equal, [s, "F%d" % d], ["NE%d2" % d], 128)
-        counts(d)
-        stage("j%d" % d)
-        judge(d, 2)
-        judge(d, 1)
-        stage("s%d" % d)
+        counts(d, (2, 1))
         scores(str(d), [d])
     stage("fin")
-    final(1, 0, [scaled(X(1), "XA0", ind(2), key), scaled(blk(T.NT, 1), "N1", ind(0), key), scaled(blk(T.FT, 1), "F1", ind(1), key)])
+    final(1, 0, [scaled(X(1), "XA1", ind(2), key), scaled(blk(T.NT, 1), "N1", ind(0), key), scaled(blk(T.FT, 1), "F1", ind(1), key)])
     stage("n3")
-    turn("RN", 5, 3)
+    turned(turn([("RN", T.BM[:, 40:64], ["BM5", "BM6", "BM7"])], 24), 0, 5, 3)
     for d in (3, 5, 7):
         stage("n%d" % d)
         s, o = to_tile(4 + d // 2)
@@ -997,27 +1591,29 @@ def rank_program(g, core, T, topo):
         cp("v", blk(T.LF3, m), ps(s, 0, 128), [s], ["LF3%d" % m], 128)
         gather2("RF%d" % m, "RB", ["RB_0", "RB_1"], T.LF3, 128 * m, "LF3%d" % m, "F%d" % d)
         b = 11 + 2 * m
-        ts(blk(T.BM, b, 8, 2), blk(T.BM, b + 6, 8, 2), ind(3), None, EQ, None, ["BM%d" % (b + 6), "BM%d" % (b + 7), key], ["BM%d" % b, "BM%d" % (b + 1)])
-        turn("RF%d" % m, b, 2)
+        bo = T.BX[:, 156 + 24 * m:180 + 24 * m]
+        ts(bo, T.BX[:, 48 + 24 * m:72 + 24 * m], ind(3), None, EQ, None, ["BO%d%d%s" % (m, n, x) for n in range(2) for x in "ab"] + [key], ["BO%d" % m])
+        s = turn([("RF%d" % m, bo, ["BO%d" % m])], 24)
         a1, a2, b1 = scaled(blk(T.NT, d), "N%d" % d, ind(5), key), scaled(X(d), xk(d), ind(3), key), scaled(X(d), xk(d), ind(1), key)
+        paired(s, 320, [(d, 2)], [(half(T.SCL, int(b1[1][3:])), b1[1])])
+        paired(s, 0, [(d, 1)], [(half(T.SCL, int(t[1][3:])), t[1]) for t in (a1, a2)])
+        turned(s, 64, b, 2)
         s, o = to_tile(b, [(blk(T.RT, 0), a1[0]), (blk(T.RT, 0), a2[0])], ["RT0", a1[1], a2[1]])
         tile_out(s, o, d, 1, (T.C3, 2 * m), "A%d" % d, X(d), xk(d))
         s, o = to_tile(b + 1, [(blk(T.RT, 0), b1[0])], ["RT0", b1[1]])
         tile_out(s, o, d, 2, (T.C3, 2 * m + 1), "B%d" % d, blk(T.C3, 2 * m), "A%d" % d)
-        counts(d)
-        stage("j%d" % d)
-        judge(d, 1)
-        judge(d, 2)
+        counts(d, (1, 2))
         stage("fin")
         final(e, m + 1, [xz, nn, scaled(blk(T.FT, e), "F%d" % e, ind(1), key)])
     stage(60)
     home("O3", 0, 2)
     home("O7", 2, 3)
-    scores("7", [3, 5, 7])
-    ind, key = decide("7", [(2, 18)], 36)
-    for m in range(3):
-        pick(blk(T.YO, m), blk(T.OWN, m, 384), 1 + m, ind, 3 * m, key, ["OW%d%d" % (c, m) for c in range(3)], ["YO%d" % m])
-        dma("as", [(blk(T.ym, 2 * m + 2), blk(T.YO, m))], ["YO%d" % m], ["ym%d" % (2 * m + 3)], 65e3)
+    for ph, a, b in (("5", 0, PAR["cutS"]), ("7", PAR["cutS"], 3))[not PAR["cutS"]:]:
+        scores(ph, range(2 * a + 3, 2 * b + 3, 2))
+        ind, key = decide(ph, [(2, 6 * (b - a))], 36 + 6 * a)
+        for m in range(a, b):
+            pick(blk(T.YO, m), blk(T.OWN, m, 384), 1 + m, ind, 3 * (m - a), key, ["OW%d%d" % (c, m) for c in range(3)], ["YO%d" % m])
+            dma("as", [(blk(T.ym, 2 * m + 2), blk(T.YO, m))], ["YO%d" % m], ["ym%d" % (2 * m + 3)], 65e3)
 
     for nd in nodes:
         if nd["kind"] == "ex":
@@ -1026,7 +1622,7 @@ def rank_program(g, core, T, topo):
         tied = []
         for i, nd in enumerate(nodes):
             tied.append(dict(nd))
-        PLAN["order"], PLAN["val"] = schedule(tied)
+        PLAN["order"], PLAN["val"] = plan(tied)
     if "dry" in PAR:
         return
     val.update(PLAN["val"])
@@ -1059,11 +1655,12 @@ def rank_program(g, core, T, topo):
             continue
         need(q, toks)
         if nd["kind"] == "ex":
-            name = nd["f"]
-            total["sent"] = total.get("sent", 0) + send(g, T, topo, deal(T, topo, me, name)[0], name)
+            name, one = nd["f"]
+            total["sent"] = total.get("sent", 0) + send(g, T, topo, deal(T, topo, me, name)[0], name, one)
             s = "ar" + name
             total[s] = sum(bits(t[3]) for b in range(8) for part in deal(T, topo, b, name) for t in part if t[0] == core)
-            lastw[s] = [(s, total[s])]
+            if one != 0:
+                lastw[s] = [(s, total[s])]
             continue
         if nd["kind"] == "fold":
             n, s = nd["f"], w[0]
@@ -1080,7 +1677,7 @@ def rank_program(g, core, T, topo):
             s = "d%d" % ndma[0]
             ndma[0] += 1
             for o, y in nd["f"]:
-                Q[q].dma_start(o, y).then_inc(T.sem[s], 16)
+                (g.dma_start(o, y, accum_op=ADD) if q == "g" else Q[q].dma_start(o, y)).then_inc(T.sem[s], 16)
             total[s] = 16 * len(nd["f"])
         else:
             s = CS[q]

from concourse.bass import DstId, RemoteDMATransfer
from concourse.mybir import AluOpType, AxisListType, ActivationFunctionType

ALU = AluOpType
ACT = ActivationFunctionType
F32, BF, I32, U16, F16 = "float32", "bfloat16", "int32", "uint16", "float16"
NT = 21
PH = ["1", "2", "4", "6", "5", "7"]

SCRATCH = {
    "StA": ("dram", [8, 128, 32], I32), "LdA": ("dram", [8, 128, 32], I32), "WI": ("sbuf", [128, 2048], I32), "BH": ("sbuf", [128, 24], F16),
    "StB": ("dram", [8, 128, 64], F16), "LdB": ("dram", [8, 128, 64], F16),
    "StF": ("dram", [16, 128, 128], BF), "LdF": ("dram", [16, 128, 128], BF), "ViaF": ("dram", [6, 128, 128], BF),
    "StE": ("dram", [8, 128, 18], F16), "LdE": ("dram", [8, 128, 18], F16), "ViaE": ("dram", [6, 128, 16], I32), "ViaB": ("dram", [6, 128, 66], F16),
    "ViaY0": ("dram", [6, 128, 32], F32), "ViaY1": ("dram", [6, 128, 32], F32),
    "StO3": ("dram", [8, 128, 64], F16), "LdO3": ("dram", [8, 128, 64], F16),
    "StO7": ("dram", [8, 128, 32], F16), "LdO7": ("dram", [8, 128, 32], F16),
    "IA": ("sbuf", [128, 384], I32), "AN": ("sbuf", [128, 384], I32), "XA": ("sbuf", [128, 384], F16),
    "MPB": ("sbuf", [128, 640], I32), "BT": ("sbuf", [128, 512], F16), "IB": ("sbuf", [128, 512], F16), "ET": ("sbuf", [128, 144], F16), "IE": ("sbuf", [128, 144], F16),
    "LM": ("sbuf", [128, 8], I32), "LB": ("sbuf", [128, 8], I32), "WF": ("sbuf", [128, 8], F32),
    "W": ("sbuf", [128, 4096], BF), "FR": ("sbuf", [128, 7 * 1040], BF), "MM": ("sbuf", [128, NT * 1040], BF), "K256": ("sbuf", [128, 128], BF), "CO": ("sbuf", [128, 24], F32), "GF": ("sbuf", [128, 168], F32),
    "GB": ("sbuf", [128, 3 * 168], BF), "CF": ("sbuf", [128, 7 * 16], F32), "PH": ("sbuf", [128, 14 * 128], F16), "BS": ("sbuf", [128, 72], F32),
    "WM1": ("sbuf", [128, 2048], BF), "WM3": ("sbuf", [128, 2048], BF),
    "RA": ("sbuf", [128, 2048], F16), "RB": ("sbuf", [128, 2048], BF), "RN": ("sbuf", [128, 2048], BF),
    "RF0": ("sbuf", [128, 2048], BF), "RF1": ("sbuf", [128, 2048], BF), "RF2": ("sbuf", [128, 2048], BF),
    "TT": ("sbuf", [128, NT * 1040], BF),
    "HB": ("sbuf", [128, 10 * 128], BF), "H2": ("sbuf", [128, 10 * 128], BF), "LO": ("sbuf", [128, 10 * 128], BF),
    "NT": ("sbuf", [128, 8 * 128], F16), "FT": ("sbuf", [128, 8 * 128], F16), "C3": ("sbuf", [128, 768], F16), "OL": ("sbuf", [128, 768], F16),
    "SCL": ("sbuf", [128, 24 * 128], F16),
    "PI1": ("sbuf", [128, 384], F32), "FIN": ("sbuf", [128, 512], F32), "OWN": ("sbuf", [128, 1152], F32), "YO": ("sbuf", [128, 384], F32),
    "LQ": ("sbuf", [128, 640], U16), "LF3": ("sbuf", [128, 384], U16), "LN": ("sbuf", [128, 128], U16),
    "FL": ("sbuf", [128, 21 * 66], U16), "NE": ("sbuf", [128, 14 * 128], BF),
    "OF": ("sbuf", [128, 32], U16), "TH": ("sbuf", [128, 64], F32),
    "AC": ("sbuf", [128, 48], F32), "CW": ("sbuf", [128, 7 * 24], F32), "GW": ("sbuf", [128, 7 * 16], BF), "RR": ("sbuf", [128, 7 * 16], BF),
    "GL": ("sbuf", [128, 10 * 8], F32), "SS": ("sbuf", [128, 192], F32), "SC": ("sbuf", [128, 192], F32), "DE": ("sbuf", [128, 6 * 32], F32),
    "col": ("sbuf", [128, 208], BF), "CI": ("sbuf", [128, 192], BF), "cgr": ("sbuf", [128, 128], F32),
    "PI": ("sbuf", [128, 8], I32), "PF": ("sbuf", [128, 8], F32), "CC": ("sbuf", [128, 128], F32),
    "ZF": ("sbuf", [128, 17 * 128], F32), "ZH": ("sbuf", [128, 17 * 128], F16), "EF": ("sbuf", [128, 130], F32),
    "BX": ("sbuf", [128, 228], BF), "UC": ("sbuf", [128, 24], F32), "CH": ("sbuf", [128, 14 * 64], F16), "CZ": ("sbuf", [128, 14 * 64], F32),
    "BM": ("sbuf", [128, 23 * 8], BF), "PM": ("sbuf", [128, 3 * 128], BF), "RT": ("sbuf", [128, 8 * 128], F16),
    "FM": ("sbuf", [128, 7 * 192], F16), "KM": ("sbuf", [128, 3 * 128], F32),
}
for _k in range(8):
    SCRATCH["PS%d" % _k] = ("psum", [128, 512], F32)
for _p in PH:
    SCRATCH["LdS" + _p] = ("dram", [8, 128, 2], F32)
for _d in range(2):
    SCRATCH["StY%d" % _d] = ("dram", [8, 128, 32], F32)
    SCRATCH["LdY%d" % _d] = ("dram", [8, 128, 32], F32)
EX = ["A", "E", "F", "B", "O3", "O7", "Y0", "Y1"] + ["S" + p for p in PH]
SEMAPHORES = ["cv", "ca", "cp", "cg", "sent"] + ["ar" + x for x in EX] + ["d%d" % i for i in range(90)] + ["arM%d" % i for i in range(21)]

POOLS = {"C": ["PS%d" % k for k in range(8)], "D": []}
GREATER = [[1, 3, 5, 7], [6, 3, 2, 7], [6, 4, 5, 7]]
POS = {1: 0, 2: 1, 3: 2, 4: 3, 5: 4, 6: 5, 7: 6, "id": 7, "A": 8, "B": 9}
PAR = {"cy": 0.92e-3, "gat": 1.56, "pe": 0.46e-3, "dma": 1.62, "bw": 360e3, "sem": 0.065, "mix": 0.3, "turns": 3, "small": 5.0, "flow": 0, "look": 0.3, "ahead": 0.5, "spare": 0.3,
       "A": 7.4, "E": 7.0, "F": 6.0, "B": 1.5, "bA": 330e3, "bE": 110e3, "bF": 550e3, "bB": 500e3, "Bafter": ["W0"], "aided": [], "S": 1.1, "room": 300e3, "Y": 2.0, "O3": 2.0, "O7": 1.7, "bY": 450e3, "bO": 450e3, "gdma": 1.0, "fin": 0, "wide": [0, 2, 5, 8, 9, 10, 11, 13, 15], "widec": [],
       "moves": 85000, "cut": [11, 12, 21, 41, 61, 72, 71, 52], "mean": 0.3, "seed": 4, "heat": 0.5, "far": 4, "aim": 10, "step": 64, "quit": 0.6, "mile": 0.02, "hold": 0.5, "cutS": 2, "tries": 0, "heat2": 0.5, "reach": 120, "case": (1.0, 1.0, 1.0, 1.0, 1.0), "cases": [(1.0, 1.0, 1.0, 1.0, 1.0), (1.15, 1.22, 1.1, 1.1, 1.1), (1.0, 0.78, 1.25, 1.5, 1.3)]}
STEPS = "Ra Rb Ba Bb g11 g10 g12 g20 g30 F2b F2a g40 F4b F4a g60 F6a F6b Nb Na g22 g21 g42 g41 g62 g61 g50 g70 F3a F3b g32 g31 F5b F5a g52 g51 F7a F7b g72 g71".split()
ACT_G, VEC_X = "g12 g22 g42 g62 g32 g52 g72 g30 g50 g70".split(), "Na F7b F3b F4b pg30 pg50 pg70 pg22 pg42 pg52".split()
LONG = {}
LOADS = "WM1 W0 XA1 FR1 Wy FR2 FR3 WM3a WM2c IB WM3b FR4 FR6 WM2b FR5 FR7".split()


def share(act, vec):
    LONG["v"] = [x for x in STEPS if x in vec or (x[0] == "g" and x not in act) or x[0] in "suR"]
    LONG["a"] = [x for x in STEPS if x not in LONG["v"]]
    LONG["s"] = LOADS
    LONG["p"] = [x[1:] for x in vec if x[0] == "p" and x[1:] in act]
    LONG["d"] = [x[1:] for x in vec if x[0] == "d" and x[1:] in act and x[1:] not in LONG["p"]]


share(ACT_G, VEC_X)
PLAN = {}
PAIRED = [(1, 1), (1, 2), (2, 1), (4, 1), (6, 1), (2, 2), (4, 2), (6, 2)] + [(d, c) for d in (3, 5, 7) for c in (1, 2)]


def top(d):
    return d.bit_length() - 1


def runs(x):
    out = []
    for i, v in enumerate(x):
        if out and v > x[i - 1] and (out[-1][1] == 1 or v - x[i - 1] == out[-1][3]):
            out[-1][1] += 1
            out[-1][3] = v - x[i - 1]
        else:
            out.append([i, 1, v, 1])
    return out


def bits(m):
    return bin(m).count("1")


def helper(T, topo, r):
    c = T.cores[r]
    ok = [k for k in topo.cores_of(c) if topo.die(k) != topo.die(c) and all(topo.may_write(k, x) for x in T.cores)]
    return ok[[x for x in T.cores if topo.chip(x) == topo.chip(c)].index(c)]


def deal(T, topo, me, name):
    src, aid = T.cores[me], helper(T, topo, me)
    far = [me ^ x for x in range(1, 8) if topo.chip(T.cores[me ^ x]) != topo.chip(src)]
    near = [me ^ x for x in range(1, 8) if topo.chip(T.cores[me ^ x]) == topo.chip(src)]
    eo = topo.engines(src, T.cores[far[0]])
    ei = [e for e in topo.engines(src, aid) if e not in eo]
    eo = eo[0::2] + eo[1::4] + eo[3::4]
    n = 2 if name == "F" else 1
    ld = T["Ld" + name]
    st = (lambda a, h: ld[me]) if name[0] == "S" else (lambda a, h: T["St" + name][n * a + h])
    own = [(T.cores[a], st(a, h), ld[n * me + h], 1 << ei[-1 - h - n * k]) for k, a in enumerate(near) for h in range(n)]
    aids = []
    for h in range(n):
        if (name, h) in PAR["aided"]:
            own += [(aid, st(a, h), T["Via" + name][k], 1 << ei[k]) for k, a in enumerate(far)]
            aids += [(T.cores[a], T["Via" + name][k], ld[n * me + h], 1 << eo[k]) for k, a in enumerate(far)]
        elif h == 0:
            own += [(T.cores[a], st(a, h), ld[n * me + h], 1 << eo[k]) for k, a in enumerate(far)]
        else:
            k = len(eo) - len(far)
            own += [(T.cores[a], st(a, h), ld[n * me + h], 1 << eo[-1 - i]) for i, a in enumerate(far[:k])]
            two = sorted(eo)
            own += [(T.cores[a], st(a, h), ld[n * me + h], (1 << two[2 * i]) | (1 << two[2 * i + 1])) for i, a in enumerate(far[k:])]
    return own, aids


def send(g, T, topo, part, name, one=None):
    calls = []
    for t in part:
        free = [c for c in calls if not any(t[3] & u[3] for u in c)]
        if not free:
            calls.append([])
        (free + calls[-1:])[0].append(t)
    calls = calls if one is None else calls[one:one + 1]
    for c in calls:
        g.remote_dma_fused([RemoteDMATransfer(dst_ids=[DstId(rid=topo.addr(k)[0], pnc=topo.addr(k)[1])], dma_engine_mask=m, remote_sem=T.sem["ar" + name], src=a, dst=b)
                            for k, a, b, m in c], local_sem=T.sem.sent)
    return sum(bits(t[3]) for c in calls for t in c)


def schedule(nodes):
    n = len(nodes)
    pre = [set() for _ in nodes]
    lastw, readers = {}, {}
    for i, nd in enumerate(nodes):
        for k in nd["r"] + nd["x"] + nd["w"]:
            pre[i].update(lastw.get(k, []))
        for k in nd["w"]:
            pre[i].update(readers.get(k, []))
        for k in nd["r"] + nd["x"]:
            readers.setdefault(k, []).append(i)
        for k in nd["w"]:
            lastw[k] = [i]
            readers[k] = []
        pre[i].discard(i)
    soft = [set(j for j in pre[i] if all(k[0] == "~" for k in set(nodes[j]["w"]) & set(nodes[i]["r"] + nodes[i]["w"])) and set(nodes[j]["w"]) & set(nodes[i]["r"]))
            for i in range(n)]
    true = [set(p) for p in pre]
    named = {nd["name"]: i for i, nd in enumerate(nodes)}
    for line in (LONG["v"], LONG["a"]):
        for a, b in zip(line, line[1:]):
            if named[a] not in pre[named[b]]:
                pre[named[b]].add(named[a])
                soft[named[b]].add(named[a])
    end = {}
    post = [[] for _ in nodes]
    for i in range(n):
        for j in pre[i]:
            post[j].append(i)
    way, due = [0.0] * n, [0.0] * n
    left = [len(p) for p in post]
    line = [i for i in range(n) if not left[i]]
    for i in line:
        for j in pre[i]:
            left[j] -= 1
            if not left[j]:
                line.append(j)
    for i in line:
        nd = nodes[i]
        way[i] = min(nd["cost"].values()) + max([way[j] + (0.0 if i in soft[j] else nd["lat"] + nd["bytes"] / PAR["bw"] + PAR["sem"]) for j in post[i]] + [nd["lat"]])
        due[i] = min([nd["rank"][0]] + [due[j] for j in post[i]])
    units = {}
    unit = [nd["slots"][0] if nd["slots"] else i for i, nd in enumerate(nodes)]
    for i in range(n):
        if unit[i] == i and not nodes[i]["name"]:
            both = set(unit[j] for j in pre[i]) & set(unit[j] for j in post[i])
            unit[i] = ([u for u in both if isinstance(u, tuple)] + [i])[0]
    for i in range(n):
        units.setdefault(unit[i], []).append(i)
    outer = {u: set(unit[j] for i in m for j in pre[i]) - {u} for u, m in units.items()}
    after = {u: [] for u in units}
    for u in units:
        for v in outer[u]:
            after[v].append(u)
    rank = {u: min(PAR["mix"] * due[i] - way[i] for i in m) - (0 if any(nodes[i]["name"] or nodes[i]["bytes"] for i in m) else PAR["small"]) for u, m in units.items()}
    sem = PAR["sem"]

    def sweep(rank, back):
        before, behind = (after, outer) if back else (outer, after)
        wait = {u: len(before[u]) for u in units}
        ready = [u for u in units if not wait[u]]
        busy, val, fin, start = {}, {}, {}, {}

        def gap(q, t, d):
            for a, b in busy.get(q, []):
                if b > t:
                    if a >= t + d:
                        break
                    t = b
            return t

        def take(q, a, b):
            busy.setdefault(q, []).append((a, b))
            busy[q].sort()

        while ready:
            u = min(ready, key=lambda u: (rank[u], units[u][0]))
            ready.remove(u)
            t0 = 0.0
            while True:
                last, got = (t0, t0, None), []
                for i in units[u][::-1 if back else 1]:
                    nd = nodes[i]
                    d = nd["bytes"] / PAR["bw"]
                    if back:
                        t = max([end[j] + sem for j in post[i] if i not in soft[j]] + [0.0])
                        if d:
                            t = gap("bus", t, d)
                            take("bus", t, t + d)
                        t = max([t + d + nd["lat"], t0] + [end[j] for j in post[i]])
                    else:
                        t = max([end[j] if j in soft[i] else fin[j] + sem for j in pre[i]] + [t0])
                        if d:
                            lead = nd["lat"] + max(nd["cost"].values())
                            t = gap("bus", t + lead, d) - lead
                    t, q = min(((gap(q, max(t, last[0] if q == last[2] else last[1]), c), q) for q, c in nd["cost"].items()),
                               key=lambda x: x[0] + nd["cost"][x[1]] + (x[1] == "v") * PAR["spare"])
                    end[i] = t + nd["cost"][q]
                    fin[i] = end[i] + (0.0 if back else nd["lat"])
                    got.append((i, q, t))
                    last = (end[i], end[i] + sem, q)
                if not isinstance(u, tuple):
                    break
                a, b = got[0][2], last[1]
                t1, v = min((gap(v, a, b - a), v) for v in POOLS[u[0]])
                if t1 <= a:
                    val[u] = v
                    take(v, a, b)
                    break
                t0 = t1
            for i, q, t in got:
                take(q, t, end[i])
                start[i] = (t, i, q)
                if nodes[i]["bytes"] and not back:
                    d = nodes[i]["bytes"] / PAR["bw"]
                    t = gap("bus", fin[i], d)
                    take("bus", t, t + d)
                    fin[i] = t + d
            for v in behind[u]:
                wait[v] -= 1
                if not wait[v]:
                    ready.append(v)
        PLAN["fin"] = {str(nodes[i]["w"][0]): round(fin[i], 1) for i in fin}
        return max(fin[i] for i in range(n)), [(i, q) for t, i, q in sorted(start.values())], val, {u: -max(fin[i] for i in m) for u, m in units.items()}

    def flow():
        wait = [len(p) for p in pre]
        shut = {u: sum(len(units[v]) for v in outer[u]) for u in units}
        pool = {p: {v: 0.0 for v in vs} for p, vs in POOLS.items()}
        left = {u: len(m) for u, m in units.items()}
        val, fin, free, bank, order, at = {}, {}, {}, {}, [], {}
        ready = [i for i in range(n) if not wait[i]]
        bus = 0.0
        prev = {}
        for line in (LONG["v"], LONG["a"]):
            us = [unit[named[x]] for x in line if x[0] == "s"]
            prev.update(zip(us[1:], us))
        while ready:
            cand = []
            for i in ready:
                nd, u = nodes[i], unit[i]
                if i not in at:
                    at[i] = max([end[j] if j in soft[i] else fin[j] + sem for j in pre[i]] + [0.0])
                t = at[i]
                if isinstance(u, tuple):
                    if u not in val:
                        if (prev.get(u, u) not in val and prev.get(u, u) != u if u[0] == "D" else shut[u]) or not pool[u[0]]:
                            continue
                        t = max(t, min(pool[u[0]].values()))
                if nd["bytes"]:
                    t = max(t, bus - nd["lat"] - PAR["ahead"])
                t, q = min(((max(t, free.get(q, 0.0), bank.get(u, (0.0, q))[0] + (sem if bank.get(u, (0.0, q))[1] != q else 0.0) if nd["slots"] else 0.0), q) for q in nd["cost"]),
                           key=lambda x: x[0] + (x[1] == "v") * PAR["spare"])
                cand.append((t, i, q))
            t0, _, q0 = min(cand)
            t, i, q = min([c for c in cand if c[2] == q0 and c[0] <= t0 + PAR["look"]],
                          key=lambda c: (PAR["mix"] * due[c[1]] - way[c[1]] + (PAR["small"] if nodes[c[1]]["name"] or unit[c[1]] in val and unit[c[1]][0] == "D" else 0.0), c[1]))
            nd, u = nodes[i], unit[i]
            free[q] = end[i] = t + nd["cost"][q]
            fin[i] = end[i] + nd["lat"]
            if nd["bytes"]:
                bus = fin[i] = max(bus, fin[i]) + nd["bytes"] / PAR["bw"]
            if isinstance(u, tuple):
                if u not in val:
                    val[u] = min(pool[u[0]], key=pool[u[0]].get)
                    pool[u[0]].pop(val[u])
                if nd["slots"]:
                    bank[u] = (end[i], q)
                left[u] -= 1
                if not left[u]:
                    pool[u[0]][val[u]] = bank[u][0] + sem
            for v in after[u]:
                shut[v] -= 1
            order.append((i, q))
            PLAN.setdefault("log", []).append((round(t, 1), q, nd["name"] or str(nd["w"][0])))
            ready.remove(i)
            for j in post[i]:
                wait[j] -= 1
                if not wait[j]:
                    ready.append(j)
        PLAN["fin"] = {str(nodes[i]["w"][0]): round(fin[i], 1) for i in fin}
        PLAN["end"] = max(fin[i] for i in range(n))
        return order, val

    def polish(order):
        hard = [sorted(true[i]) for i in range(n)]
        succ = [[j for j in post[i] if i in true[j]] for i in range(n)]
        qs = {q: k for k, q in enumerate("gvaps")}
        seq, on = [i for i, q in order], [0] * n
        for i, q in order:
            on[i] = qs[q]
        alt = [[qs[q] for q in nd["cost"]] for nd in nodes]
        slots = sorted(set(s for nd in nodes for s in nd["slots"]))
        sl = [slots.index(nd["slots"][0]) if nd["slots"] else -1 for nd in nodes]
        count = [sl.count(k) for k in range(len(slots))]
        kind = [s[0] == "D" for s in slots]
        sets = []
        for fc, fl, fb in PAR["cases"]:
            sets.append(([{qs[q]: c * (fc if q in "vap" else 1.0) for q, c in nd["cost"].items()} for nd in nodes], [nd["lat"] * fl for nd in nodes],
                         [nd["bytes"] / PAR["bw"] * fb for nd in nodes], [[(j, j in soft[i]) for j in hard[i]] for i in range(n)]))

        m = len(count)
        marks = [{0: ([0.0] * 5, 0.0, [(0.0, v) for v in POOLS["C"]], list(count), [0.0] * m, [-1] * m, [None] * m), "t": ([0.0] * n, [0.0] * n)} for _ in sets]
        fresh = []

        def run(keep=None, first=0):
            total, first = 0.0, first - first % 48
            fresh[:] = []
            for (cost, lat, byt, pr), mark in zip(sets, marks):
                free, bus, p, left, last, lq, got = mark[first]
                free, p, left, last, lq, got = list(free), list(p), list(left), list(last), list(lq), list(got)
                fin, end = list(mark["t"][0]), list(mark["t"][1])
                new = {"t": (fin, end)}
                fresh.append(new)
                for a in range(first, n):
                    if not a % 48:
                        new[a] = (list(free), bus, list(p), list(left), list(last), list(lq), list(got))
                    i = seq[a]
                    q = on[i]
                    t = free[q]
                    for j, s in pr[i]:
                        u = end[j] if s else fin[j]
                        if u > t:
                            t = u
                    k = sl[i]
                    if k >= 0:
                        if got[k] is None:
                            if not p:
                                return 1e9
                            u, got[k] = p.pop(0)
                            if u > t:
                                t = u
                        elif lq[k] != q and last[k] > t:
                            t = last[k]
                    t += cost[i][q]
                    free[q] = end[i] = t
                    u = t + lat[i]
                    if byt[i]:
                        if bus > u:
                            u = bus
                        bus = u = u + byt[i]
                    fin[i] = u + sem
                    if k >= 0:
                        last[k], lq[k] = t + sem, q
                        left[k] -= 1
                        if not left[k]:
                            p.append((t + sem, got[k]))
                total += max(fin) + (PAR["mean"] * sum(fin) / n if keep is None else 0.0)
            if keep is not None:
                keep.update(zip(slots, got))
            return total / len(sets)

        def accept():
            for mark, new in zip(marks, fresh):
                mark.update(new)

        x, cur = PAR["seed"], run()
        accept()
        best = (cur, list(seq), list(on))
        for k in range(PAR["moves"]):
            x = (x * 6364136223846793005 + 1442695040888963407) % 2 ** 64
            a = (x >> 40) % n
            i = seq[a]
            room = PAR["heat"] * (1.0 - k / PAR["moves"]) * ((x >> 8) % 1000) ** 3 / 1e9
            if len(alt[i]) > 1 and (x >> 20) % 3 == 0:
                old = on[i]
                on[i] = alt[i][1] if old == alt[i][0] else alt[i][0]
                e = run(None, a)
                if e > cur + room:
                    on[i] = old
                    continue
            else:
                far, b, d = 1 + ((x >> 24) % 1000) ** 2 * PAR["far"] // 10 ** 6, a, 1 - 2 * ((x >> 21) % 2)
                go, stay = [i], []
                need = set(true[i] if d < 0 else succ[i])
                while far and 0 <= b + d < n:
                    b += d
                    j = seq[b]
                    if j in need:
                        go.append(j)
                        need.update(true[j] if d < 0 else succ[j])
                    else:
                        stay.append(j)
                        far -= on[j] == on[i]
                if not stay:
                    continue
                lo, hi = min(a, b), max(a, b) + 1
                old = seq[lo:hi]
                seq[lo:hi] = go[::-1] + stay[::-1] if d < 0 else stay + go
                e = run(None, lo)
                if e > cur + room:
                    seq[lo:hi] = old
                    continue
            accept()
            cur = e
            if e < best[0]:
                best = (e, list(seq), list(on))
        seq[:], on[:] = best[1], best[2]
        val = {}
        PLAN["end"] = run(val)
        return [(i, "gvaps"[on[i]]) for i in seq], val

    if PAR["flow"]:
        return flow()
    best = None
    for k in range(PAR["turns"]):
        got = sweep(rank, False)
        if best is None or got[0] < best[0]:
            best = got
        if k + 1 < PAR["turns"]:
            rank = sweep(got[3], True)[3]
    PLAN["end"] = best[0]
    if PAR["moves"]:
        for nd in nodes:
            nd["cost"] = nd["any"]
        return polish(best[1])
    return best[1], best[2]


def plan(nodes):
    n, sem, bw = len(nodes), PAR["sem"], PAR["bw"]
    pre = [set() for _ in nodes]
    lastw, readers = {}, {}
    for i, nd in enumerate(nodes):
        for k in nd["r"] + nd["x"] + nd["w"]:
            pre[i].update(lastw.get(k, []))
        for k in nd["w"]:
            pre[i].update(readers.get(k, []))
        for k in nd["r"] + nd["x"]:
            readers.setdefault(k, []).append(i)
        for k in nd["w"]:
            lastw[k] = [i]
            readers[k] = []
        pre[i].discard(i)
    soft = [set(j for j in pre[i] if list(nodes[i]["cost"]) == list(nodes[j]["cost"]) == ["p"]
                or all(k[0] == "~" for k in set(nodes[j]["w"]) & set(nodes[i]["r"] + nodes[i]["w"])) and set(nodes[j]["w"]) & set(nodes[i]["r"])) for i in range(n)]
    unit = [nd["slots"][0] if nd["slots"] else i for i, nd in enumerate(nodes)]
    post = [[] for _ in nodes]
    for i in range(n):
        for j in pre[i]:
            post[j].append(i)
    for i in range(n):
        if unit[i] == i:
            both = set(unit[j] for j in pre[i]) & set(unit[j] for j in post[i])
            unit[i] = ([u for u in both if isinstance(u, tuple)] + [i])[0]
    named = {nd["name"]: i for i, nd in enumerate(nodes)}
    true = [set(p) for p in pre]
    for line in (LONG["v"], LONG["a"], LONG["s"]):
        line = [x for x in line if x in named]
        for a, b in zip(line, line[1:]):
            if named[a] not in pre[named[b]]:
                pre[named[b]].add(named[a])
                soft[named[b]].add(named[a])
                post[named[a]].append(named[b])
    outer = {}
    for i in range(n):
        if isinstance(unit[i], tuple):
            outer.setdefault(unit[i], set()).update(j for j in pre[i] if unit[j] != unit[i])
    opens = [[] for _ in nodes]
    for u in outer:
        for j in outer[u]:
            opens[j].append(u)
    way = [0.0] * n
    left = [len(p) for p in post]
    line = [i for i in range(n) if not left[i]]
    for i in line:
        nd = nodes[i]
        way[i] = min(nd["cost"].values()) + max([way[j] + (0.0 if i in soft[j] else nd["lat"] + nd["bytes"] / bw + sem) for j in post[i]] + [nd["lat"]])
        for j in pre[i]:
            left[j] -= 1
            if not left[j]:
                line.append(j)
    wait = [len(p) for p in pre]
    shut = {u: len(outer[u]) for u in outer}
    left = {u: unit.count(u) for u in outer}
    pool = [(0.0, v) for v in POOLS["C"]]
    val, bank, at, free, order = {}, {}, {}, {q: 0.0 for q in "gvaps"}, []
    end, fin = [0.0] * n, [0.0] * n
    ready = [i for i in range(n) if not wait[i]]
    bus = 0.0
    PLAN["log"] = []
    while ready:
        cand = []
        for i in ready:
            nd, u = nodes[i], unit[i]
            if i not in at:
                at[i] = max([end[j] if j in soft[i] else fin[j] + sem for j in pre[i]] + [0.0])
            t = at[i]
            if nd["slots"] and u not in val:
                if shut[u] or not pool:
                    continue
                t = max(t, pool[0][0])
            if nd["bytes"]:
                t = max(t, bus - nd["lat"] - PAR["ahead"])
            best = None
            for q, c in nd["cost"].items():
                s = max(t, free[q])
                if nd["slots"] and u in bank and bank[u][1] != q:
                    s = max(s, bank[u][0])
                if best is None or s + c + (q == "v") * PAR["spare"] < best[0]:
                    best = (s + c + (q == "v") * PAR["spare"], s, q, c)
            cand.append((best[1] + best[3], best[1], i, best[2]))
        e0, _, i0, q0 = min(cand)
        both = [c for c in cand if c[3] == q0 and (c[1] < e0 or c[2] == i0)]
        t0 = min(c[1] for c in both) + PAR["look"]
        e, t, i, q = min(both, key=lambda c: (-way[c[2]] - (PAR["small"] if 9.0 < c[1] <= t0 and c[0] - c[1] < 0.4 else 0.0), c[2]))
        nd, u = nodes[i], unit[i]
        free[q] = end[i] = e
        fin[i] = e + nd["lat"]
        if nd["bytes"]:
            bus = fin[i] = max(bus, fin[i]) + nd["bytes"] / bw
        if nd["slots"]:
            if u not in val:
                val[u] = pool.pop(0)[1]
            bank[u] = (e + sem, q)
        if u in left:
            left[u] -= 1
            if not left[u]:
                pool.append((bank[u][0], val[u]))
                pool.sort()
        for v in opens[i]:
            shut[v] -= 1
        order.append((i, q))
        PLAN["log"].append((round(t, 1), q, nd["name"] or str(nd["w"][0]), round(fin[i], 1)))
        ready.remove(i)
        for j in post[i]:
            wait[j] -= 1
            if not wait[j]:
                ready.append(j)
    PLAN["end"] = max(fin) if len(order) == n else 1e9
    PLAN["way"] = max(way)
    PLAN["busy"] = {q: round(sum(nodes[i]["cost"][q] for i, x in order if x == q and end[i] > 13.2), 1) for q in free}
    if "path" in PAR:
        i = way.index(max(way))
        PLAN["path"] = []
        while post[i]:
            PLAN["path"].append((nodes[i]["name"] or str(nodes[i]["w"][0]), round(max(way) - way[i], 1)))
            i = max(post[i], key=lambda j: way[j] + (0.0 if i in soft[j] else nodes[i]["lat"] + nodes[i]["bytes"] / bw + sem))
    if PAR["tries"] and len(order) == n:
        order = place(nodes, true, soft, order)
    if PAR["moves"] and len(order) == n:
        return polish(nodes, true, soft, order)
    return order, val


def place(nodes, pre, soft, order):
    n, sem, bw = len(nodes), PAR["sem"], PAR["bw"]
    pre = [set(p) for p in pre]
    last = {}
    for i, nd in enumerate(nodes):
        for s in nd["slots"]:
            if s in last:
                pre[i].add(last[s][1])
            last[s] = (last.get(s, (i, i))[0], i)
    above = [0] * n
    for i in range(n):
        for j in pre[i]:
            above[i] |= above[j] | 1 << j
    late = [[] for _ in nodes]
    lead = {}
    for i, nd in enumerate(nodes):
        for s in nd["slots"]:
            a = last[s][0]
            late[a] += [(j, lead.get(s, 0.0) + PAR["hold"]) for j in pre[i] if j != a and not above[j] >> a & 1 and j not in pre[a]]
            lead[s] = lead.get(s, 0.0) + min(nd["any"].values()) + sem
    true = [set(p) for p in pre]
    for i in range(n):
        pre[i].update(j for j, t in late[i])
    post = [[] for _ in nodes]
    for i in range(n):
        for j in pre[i]:
            post[j].append(i)
    fc, fg, fl, fe, fb = PAR["case"]
    qs = {q: k for k, q in enumerate("gvaps")}
    cost = [[(qs[q], c * (fc * (fg if c > 0.7 else 1.0) if q in "va" else fc if q == "p" else 1.0)) for q, c in nd["any"].items()] for nd in nodes]
    lat = [nd["lat"] * (fl if nd["kind"] == "dma" else fe) for nd in nodes]
    byt = [nd["bytes"] / bw * fb for nd in nodes]
    pr = [[(j, j in soft[i]) for j in sorted(true[i])] for i in range(n)]
    miles = [i for i, nd in enumerate(nodes) if nd["kind"] == "ex"]
    seq, done = [], set()

    def put(i):
        if i not in done:
            done.add(i)
            for j in sorted(pre[i]):
                put(j)
            seq.append(i)

    for i, q in order:
        put(i)
    pick = [0] * n
    spans = list(last.values())

    def room(a, b, t, d):
        lo, hi = 0, len(b)
        while lo < hi:
            m = (lo + hi) // 2
            if b[m] <= t:
                lo = m + 1
            else:
                hi = m
        while lo < len(a) and a[lo] < t + d - 1e-9:
            t = b[lo]
            lo += 1
        return t, lo

    skip = [0, None]

    def run():
        if skip[1]:
            a, b, end, fin, on, why = [[list(x) for x in y] for y in skip[1][:2]] + [list(y) for y in skip[1][2:]]
        else:
            a, b = [[] for _ in range(6)], [[] for _ in range(6)]
            end, fin, on, why = [0.0] * n, [0.0] * n, [0] * n, [-1] * n
        for i in seq[skip[0]:]:
            t, y = 0.0, -1
            for j, s in pr[i]:
                u = end[j] if s else fin[j]
                if u > t:
                    t, y = u, j
            for j, s in late[i]:
                if fin[j] - s > t:
                    t = fin[j] - s
            c = cost[i]
            if byt[i]:
                lead = lat[i] + c[0][1]
                t = room(a[5], b[5], t + lead, byt[i])[0] - lead
            q, d = c[pick[i] - 1] if pick[i] else c[0]
            u, k = room(a[q], b[q], t, d)
            if len(c) > 1 and not pick[i]:
                q2, d2 = c[1]
                u2, k2 = room(a[q2], b[q2], t, d2)
                if u2 + d2 <= u + d + PAR["spare"]:
                    q, d, u, k = q2, d2, u2, k2
            a[q].insert(k, u)
            b[q].insert(k, u + d)
            end[i] = u = u + d
            u += lat[i]
            if byt[i]:
                u, k = room(a[5], b[5], u, byt[i])
                a[5].insert(k, u)
                u += byt[i]
                b[5].insert(k, u)
            fin[i], on[i], why[i] = u + sem, q, y
        ev = sorted([(end[i] - cost[i][0][1], 1) for i, j in spans] + [(fin[j], -1) for i, j in spans])
        over = use = 0
        for t, k in ev:
            use += k
            if use > 8:
                over += 1
        return max(fin) + PAR["mean"] * sum(fin) / n + PAR["mile"] * sum(fin[i] for i in miles) + over, end, fin, on, (a, b, end, fin, on, why)

    got = run()
    early = [i for i in seq if got[1][i] < 9.0]
    seq[:] = early + [i for i in seq if got[1][i] >= 9.0]
    full, seq[:] = list(seq), early
    skip[1] = run()[4]
    seq[:], skip[0] = full, len(early)
    got = run()
    cur, best, x = got[0], (got, list(seq)), PAR["seed"]
    big = [i for i in full[skip[0]:] if cost[i][0][1] > 0.4 or byt[i]]
    for k in range(PAR["tries"]):
        x = (x * 6364136223846793005 + 1442695040888963407) % 2 ** 64
        heat = PAR["heat2"] * (1.0 - k / PAR["tries"]) * ((x >> 8) % 1000) ** 3 / 1e9
        kind = (x >> 20) % 8
        i = big[(x >> 40) % len(big)] if kind < 5 else full[skip[0] + (x >> 40) % (n - skip[0])]
        if kind == 0 and len(cost[i]) > 1:
            old = pick[i]
            pick[i] = (old + 1 + (x >> 30) % 2) % 3
            new = run()
            if new[0] > cur + heat:
                pick[i] = old
                continue
        else:
            a = seq.index(i)
            d = 1 - 2 * ((x >> 35) % 2)
            b = min(n - 1, max(skip[0], a + d * (1 + ((x >> 24) % 1000) ** 2 * PAR["reach"] // 10 ** 6)))
            if a == b:
                continue
            link = post if d > 0 else pre
            go, stay, need = [i], [], set(link[i])
            for c in range(a + d, b + d, d):
                j = seq[c]
                if j in need:
                    go.append(j)
                    need.update(link[j])
                else:
                    stay.append(j)
            lo, hi = min(a, b), max(a, b) + 1
            old = seq[lo:hi]
            seq[lo:hi] = go[::-1] + stay[::-1] if d < 0 else stay + go
            new = run()
            if new[0] > cur + heat:
                seq[lo:hi] = old
                continue
        cur = new[0]
        if cur < best[0][0]:
            best = (new, list(seq))
    got, seq = best
    PLAN["placed"] = (round(max(got[2]), 1), round(got[0], 1))
    rank = {i: k for k, i in enumerate(seq)}
    start = {i: got[1][i] - dict(cost[i])[got[3][i]] for i in seq}
    return [(i, "gvaps"[got[3][i]]) for i in sorted(seq, key=lambda i: (round(start[i], 6), rank[i]))]


def polish(nodes, pre, soft, order):
    n, sem, step = len(nodes), PAR["sem"], PAR["step"]
    post = [[] for _ in nodes]
    for i in range(n):
        for j in pre[i]:
            post[j].append(i)
    qs = {q: k for k, q in enumerate("gvaps")}
    seq, on = [i for i, q in order], [0] * n
    for i, q in order:
        on[i] = qs[q]
    alt = [[qs[q] for q in nd["any"]] for nd in nodes]
    slots = sorted(set(s for nd in nodes for s in nd["slots"]))
    sl = [slots.index(nd["slots"][0]) if nd["slots"] else -1 for nd in nodes]
    count = [sl.count(k) for k in range(len(slots))]
    pr = [[(j, j in soft[i]) for j in sorted(pre[i])] for i in range(n)]
    sets = [([{qs[q]: c * (fc * (fg if c > 0.7 else 1.0) if q in "va" else fc if q == "p" else 1.0) for q, c in nd["any"].items()} for nd in nodes],
             [nd["lat"] * (fl if nd["kind"] == "dma" else fe) for nd in nodes], [nd["bytes"] / PAR["bw"] * fb for nd in nodes]) for fc, fg, fl, fe, fb in PAR["cases"]]
    m = len(count)
    marks = [{0: ([0.0] * 5, [-1] * 5, 0.0, -1, [(0.0, 0, -1) for v in POOLS["C"]], list(count), [0.0] * m, [-1] * m, [None] * m), "t": ([0.0] * n, [0.0] * n, [-1] * n)} for _ in sets]
    fresh = []
    miles = [i for i, nd in enumerate(nodes) if nd["kind"] == "ex"]

    at = [0] * n
    for a, i in enumerate(seq):
        at[i] = a

    def run(first, upto=n):
        total, first = 0.0, first - first % step
        fresh[:] = []
        for (cost, lat, byt), mark in zip(sets, marks):
            free, who, bus, bw, p, left, last, lq, got = mark[first]
            free, who, p, left, last, lq, got = list(free), list(who), list(p), list(left), list(last), list(lq), list(got)
            fin, end, why = list(mark["t"][0]), list(mark["t"][1]), list(mark["t"][2])
            new = {"t": (fin, end, why), "got": got}
            fresh.append(new)
            reach = upto
            for a in range(first, n):
                if not a % step:
                    new[a] = (list(free), list(who), bus, bw, list(p), list(left), list(last), list(lq), list(got))
                    if a > reach and new[a] == mark[a]:
                        new["got"] = mark["got"]
                        break
                i = seq[a]
                q = on[i]
                t, y = free[q], who[q]
                for j, s in pr[i]:
                    u = end[j] if s else fin[j]
                    if u > t:
                        t, y = u, j
                k = sl[i]
                if k >= 0:
                    if got[k] is None:
                        if not p:
                            return 1e9
                        u, got[k], j = p.pop(0)
                        if u > t:
                            t, y = u, j
                    elif on[lq[k]] != q and last[k] > t:
                        t, y = last[k], lq[k]
                t += cost[i][q]
                free[q] = t
                who[q] = i
                u = t + lat[i]
                if byt[i]:
                    if bus > u:
                        u, y = bus, bw
                    bus = u = u + byt[i]
                    bw = i
                u += sem
                if u != fin[i] or t != end[i]:
                    end[i], fin[i] = t, u
                    for j in post[i]:
                        if at[j] > reach:
                            reach = at[j]
                why[i] = y
                if k >= 0:
                    last[k], lq[k] = t + sem, i
                    left[k] -= 1
                    if not left[k]:
                        p.append((t + sem, got[k], i))
                        last[k] = lq[k] = 0
            new["sum"] = max(fin) + PAR["mean"] * sum(fin) / n + PAR["mile"] * sum(fin[i] for i in miles)
            if new["sum"] > mark.get("sum", 1e9) + PAR["quit"]:
                return 1e9
            total += new["sum"]
        return total / len(sets)

    def accept():
        for mark, new in zip(marks, fresh):
            mark.update(new)

    def held():
        out = []
        for mark in marks:
            fin, end, why = mark["t"]
            i = fin.index(max(fin))
            while why[i] >= 0:
                out.append((i, why[i]))
                i = why[i]
        return [x for x in out if x[1] not in pre[x[0]]], [x[0] for x in out if len(alt[x[0]]) > 1]

    def shift(a, b):
        d = 1 if b > a else -1
        link = post if d > 0 else pre
        go, stay, need = [seq[a]], [], set(link[seq[a]])
        for c in range(a + d, b + d, d):
            j = seq[c]
            if j in need:
                go.append(j)
                need.update(link[j])
            else:
                stay.append(j)
        return go[::-1] + stay[::-1] if d < 0 else stay + go

    x, cur = PAR["seed"], run(0)
    accept()
    best = (cur, list(seq), list(on))
    arcs, flex = held()
    skip = sum(t < 9.0 for t in marks[0]["t"][1])
    for k in range(PAR["moves"]):
        x = (x * 6364136223846793005 + 1442695040888963407) % 2 ** 64
        room = PAR["heat"] * (1.0 - k / PAR["moves"]) * ((x >> 8) % 1000) ** 3 / 1e9
        kind = (x >> 20) % 16
        if kind < 3:
            i = flex[(x >> 40) % len(flex)] if kind and flex else seq[(x >> 40) % n]
            if len(alt[i]) < 2:
                continue
            old = on[i]
            on[i] = alt[i][0] + alt[i][1] - old
            e = run(at[i], at[i])
            if e > cur + room:
                on[i] = old
                continue
        else:
            if kind < 3 + PAR["aim"] and arcs:
                i, j = arcs[(x >> 40) % len(arcs)]
                a, b = at[i], at[j]
                if kind % 2:
                    a, b = b, a
            else:
                a = skip + (x >> 40) % (n - skip)
                b = a
            far, d = ((x >> 24) % 1000) ** 2 * PAR["far"] * (1 if (x >> 36) % 8 else 6) // 10 ** 6 + (a == b), (1 if b > a else -1) if a != b else 1 - 2 * ((x >> 35) % 2)
            while far and 0 <= b + d < n:
                b += d
                far -= on[seq[b]] == on[seq[a]]
            if a == b:
                continue
            lo, hi = min(a, b), max(a, b) + 1
            old = seq[lo:hi]
            seq[lo:hi] = shift(a, b)
            if seq[lo:hi] == old:
                continue
            e = run(lo, hi)
            if e > cur + room:
                seq[lo:hi] = old
                continue
            for a in range(lo, hi):
                at[seq[a]] = a
        accept()
        if e != cur or not k % 8:
            arcs, flex = held()
        cur = e
        if e < best[0]:
            best = (e, list(seq), list(on))
    seq[:], on[:] = best[1], best[2]
    for mark in marks:
        mark.pop("sum")
        mark[0][4][:] = [(0.0, v, -1) for v in POOLS["C"]]
    run(0)
    accept()
    PLAN["ends"] = [round(max(mark["t"][0]), 1) for mark in marks]
    PLAN["end"] = sum(PLAN["ends"]) / len(sets)
    fin, end, why = marks[0]["t"]
    i, PLAN["path"] = fin.index(max(fin)), []
    while i >= 0:
        PLAN["path"].append("%s%s:%s@%.1f" % ("" if why[i] in pre[i] else "*", "gvaps"[on[i]], (nodes[i]["name"] or str(nodes[i]["w"][0])).strip("()'").replace("C', ", "#"), end[i]))
        i = why[i]
    PLAN["log"] = [(round(end[i] - sets[0][0][i][on[i]], 1), "gvaps"[on[i]], nodes[i]["name"] or str(nodes[i]["w"][0]), round(fin[i], 1)) for i in seq]
    PLAN["busy"] = {q: round(sum(sets[0][0][i][on[i]] for i in seq if on[i] == qs[q] and end[i] > 13.2), 1) for q in qs}
    return [(i, "gvaps"[on[i]]) for i in seq], dict(zip(slots, marks[0]["got"]))


def rank_program(g, core, T, topo):
    me = T.rank_of(core)
    if me is None:
        for r in range(8):
            if helper(T, topo, r) == core and PAR["aided"]:
                n = 0
                for name, h in PAR["aided"]:
                    own, aids = deal(T, topo, r, name)
                    g.wait_ge(T.sem["ar" + name], sum(bits(t[3]) for t in own if t[0] == core))
                    n += send(g, T, topo, aids, name)
                g.wait_ge(T.sem.sent, n)
        return
    Q = {"g": g, "v": g.vector, "a": g.scalar, "p": g.tensor, "s": g.sync}
    CS = {"g": "cg", "v": "cv", "a": "ca", "p": "cp"}
    nodes = []
    val = {}
    ns = [0]
    lvl = [99]

    def stage(x):
        lvl[0] = PAR.get(x, 99)

    CY = PAR["cy"]
    V = g.vector

    def slot(p):
        ns[0] += 1
        return (p, ns[0])

    def z(x):
        if isinstance(x, tuple) and x[0] == "lazy":
            return x[1](val[x[2]])
        return x

    def ps(s, a, b, p1=128, step=1, p0=0):
        return ("lazy", lambda v: T[v][p0:p1, a:b:step], s)

    def tb(s, a, b):
        return T.TT[:, 1040 * int(s[1:]) + a:1040 * int(s[1:]) + b]

    def node(kind, cost, f, r, w, lat=0.0, nbytes=0, push=0.0):
        x = [k for k in r if isinstance(k, tuple)]
        r = [k for k in r if k not in x]
        slots = sorted(set(k for k in r + x + list(w) if isinstance(k, tuple)))
        nodes.append({"kind": kind, "cost": cost, "f": f, "r": r, "x": x, "w": list(w), "lat": lat, "bytes": nbytes, "slots": slots, "push": push,
                      "rank": (lvl[0], len(nodes)), "name": "", "any": cost})

    def on(name):
        return "v" if name in LONG["v"] else "a"

    def call(name):
        nodes[-1]["name"] = name
        if name[0] in "BFN":
            nodes[-1]["any"] = {q: min(nodes[-1]["cost"].values()) for q in "va"}

    def cyc(n):
        return max(64, n) * CY

    def vop(f, r, w, n=64):
        node("op", {"v": cyc(n)}, lambda q: f(), r, w)

    def gop(f, n, r, w):
        node("op", {"g": 0.14 + 2 * n * CY}, lambda q: f(), r, w)

    def memset(ap, v, w, n=64):
        vop(lambda: V.memset(ap, v), [], w, n)

    def pe(mms, r, w, start=True, stop=True):
        out = []
        for i, m in enumerate(mms):
            if m is not None:
                out.append((m[0], m[1], m[2], mms[i - 1] is None if i else start, stop if i == len(mms) - 1 else mms[i + 1] is None, m[3]))
        node("pe", {"p": sum(m[5] + 8 for m in out) * PAR["pe"]}, out, r, w)

    def dma(qs, moves, r, w, nbytes, push=0.0):
        node("dma", {q: 0.07 * len(moves) for q in qs}, moves, r, w, PAR["dma"], nbytes, push)
        nodes[-1]["name"] = w[0]

    def exchange(name, r, lat, call=None):
        node("ex", {"g": 0.7}, (name, call), r, ["ar" + name + "0" * (call == 0)], lat, PAR["room"] if name[0] == "S" else PAR.get("b" + name[0], 0) / (1 + (name == "O7")))

    def aff(out, in_, a, b, r, w, n=64):
        def f(q):
            if q == "v":
                return V.tensor_scalar(out, in_, a, b, ALU.mult, ALU.add)
            return g.scalar.activation(out, in_, ACT.Identity, bias=b, scale=a)
        node("op", {"a": cyc(n), "v": cyc(n)}, f, r, w)

    def fill(out, v, w, n):
        aff(out, T.col[:, 0:n], 0.0, v, ["col"], w, n)

    def ts(out, in0, s1, s2, o0, o1, r, w, n=64):
        if o1 is None:
            vop(lambda: V.tensor_scalar(z(out), z(in0), z(s1), None, o0), r, w, n)
        else:
            vop(lambda: V.tensor_scalar(z(out), z(in0), z(s1), z(s2), o0, o1), r, w, n)

    def tt(out, a, b, o, r, w, n=64):
        vop(lambda: V.tensor_tensor(z(out), z(a), z(b), o), r, w, n)

    def cp(qs, out, in_, r, w, n=64):
        def f(q):
            if q == "v":
                return V.tensor_copy(z(out), z(in_))
            return g.scalar.activation(z(out), z(in_), ACT.Copy)
        node("op", {q: cyc(n) for q in qs}, f, r, w)

    def addc(qs, out, in_, c, r, w, n, half):
        def f(q):
            if q == "v":
                return V.tensor_scalar(z(out), z(in_), c, None, ALU.add)
            return g.scalar.activation(z(out), z(in_), ACT.Identity, bias=c)
        node("op", {q: cyc(n // 2 if half and q == "v" else n) for q in qs}, f, r, w)

    def mul(qs, out, in_, c, r, w):
        def f(q):
            if q == "v":
                return V.tensor_scalar(out, in_, c, None, ALU.mult)
            return g.scalar.activation(out, in_, ACT.Copy, scale=c)
        node("op", {q: cyc(64) for q in qs}, f, r, w)

    def blk(t, k, n=128, m=1):
        return t[:, k * n:(k + m) * n]

    def c1(t, k):
        return t[:, k:k + 1]

    EQ, MUL, ADD, SUB, GT = ALU.is_equal, ALU.mult, ALU.add, ALU.subtract, ALU.is_gt
    mine = slice(16 * me, 16 * me + 16)

    gop(lambda: g.iota(T.PI[:, 0:1], [[0, 1]], 0, 1), 1, [], ["PI0", "~g0"])
    gop(lambda: g.iota(T.col[:], [[1, 208]], -16, 0, allow_small_or_imprecise_dtypes=True), 208, ["~g0"], ["col", "~g1"])
    gop(lambda: g.iota(T.cgr[:], [[1, 8], [0, 16]], 0, 0, allow_small_or_imprecise_dtypes=True), 128, ["~g1"], ["cgr", "~g2"])
    dma("s", [(T.StA[:, 64 * k:64 * k + 64, :], blk(T.mp, 1 + k)) for k in range(2)], [], ["StA", "~s0"], 131e3)
    dma("a", [(T.IA[:, 0:128], blk(T.mp, 0))], [], ["IA0", "~a0"], 65e3)
    dma("s", [(T.StF[h::2], T.ft[:, 1024 * h:1024 * h + 1024]) for h in range(2)], ["~s0"], ["StF", "~s1"], 524e3)
    dma("s", [(T.MPB[:], T.mp[:, 256:896])], ["~s1"], ["MPB", "~s2"], 328e3)
    dma("s", [(T.LdA[me, 64 * k:64 * k + 64, :], T.mp[mine, 128 + 128 * k:256 + 128 * k]) for k in range(2)], ["~s2"], ["LdA", "~s3"], 16e3)
    dma("s", [(T.LdF[2 * me + h], T.ft[mine, 1024 * h:1024 * h + 1024]) for h in range(2)], ["~s3"], ["LdF"], 65e3)
    dma("a", [(T.LM[0:1, 0:7], T.lam[0:1, :])], ["~a0"], ["LM", "~a1"], 1e3)
    exchange("A", ["StA", "~g2"], PAR["A"])
    exchange("F", ["StF", "~arA"], PAR["F"], 0)
    gop(lambda: g.partition_broadcast(T.LB[:, 0:7], T.LM[0:1, 0:7], 128), 14, ["LM", "~arF0"], ["LB", "~g3"])
    gop(lambda: g.iota(T.WI[:], [[0, 2048]], 0, 0), 2048, ["~g3"], ["WI", "~g4"])
    exchange("F", ["StF", "arA", "~g4"], PAR["B"], 1)
    ts(T.ET[:, 128:144], T.col[:, 0:16], 0.0, None, MUL, None, ["col"], ["ETw"])
    cp("v", T.ET[:, 0:128], T.IA[:, 0:128], ["IA0"], ["ET"], 128)
    cp("v", T.ET[:, 128:135], T.LB[:, 0:7], ["LB"], ["ETw"])
    dma("s", [(T.StE[:], T.ET[:]), (T.LdE[me], T.ET[mine, :])], ["ET", "ETw"], ["StE"], 60e3)
    exchange("E", ["StE", "~arF"], PAR["B"])
    cp("v", T.BT[:], T.MPB[:, 128:640], ["MPB"], ["BT"], 512)
    dma("s", [(T.StB[:], T.BT[:]), (T.LdB[me], T.BT[mine, :])], ["BT"], ["StB"], 160e3)

    stage(2)
    CC, PF = T.CC, T.PF
    TG, TB, RM, FK, BT6, SB, TP, I3, UB, ONE, KH3, KK = 0, 8, 16, 24, 28, 36, 66, 74, 82, 90, 91, 92

    def col(a, n):
        return T.col[:, 16 + a:16 + a + n]

    for k in range(3):
        ts(c1(T.PI, 1 + k), c1(T.PI, 0), 4 + k, 1, ALU.logical_shift_right, ALU.bitwise_and, ["PI0"], ["PI%d" % (1 + k)])
    ts(c1(T.PI, 4), c1(T.PI, 0), 15, None, ALU.bitwise_and, None, ["PI0"], ["PI4"])
    ts(c1(T.PI, 5), c1(T.PI, 0), 1, 7, ALU.logical_shift_right, ALU.bitwise_and, ["PI0"], ["PI5"])
    ts(c1(T.PI, 6), c1(T.PI, 0), 7, None, ALU.bitwise_and, None, ["PI0"], ["PI6"])
    ts(c1(T.PI, 7), c1(T.PI, 0), 1, None, ALU.bitwise_and, None, ["PI0"], ["PI7"])
    cp("v", PF[:], T.PI[:], ["PI%d" % k for k in range(8)], ["PF"])
    P0, I16, KH, K7, K1 = c1(PF, 0), c1(PF, 4), c1(PF, 5), c1(PF, 6), c1(PF, 7)
    ts(CC[:, FK:FK + 3], PF[:, 1:4], -2.0, 1.0, MUL, ADD, ["PF"], ["FK"])
    cp("v", c1(CC, TG), P0, ["PF"], ["TG0"])
    for k in range(3):
        ts(c1(CC, TP + k), c1(CC, FK + k), 16.0 * 2 ** k, None, MUL, None, ["FK"], ["TP%d" % k])
        ts(CC[:, TG + 2 ** k:TG + 2 ** (k + 1)], CC[:, TG:TG + 2 ** k], c1(CC, TP + k), None, ADD, None, ["TG%d" % i for i in range(k + 1)] + ["TP%d" % k], ["TG%d" % (k + 1)])
    TGK = ["TG0", "TG1", "TG2", "TG3"]
    ts(CC[:, TB:TB + 8], CC[:, TG:TG + 8], I16, 15.0, SUB, ADD, TGK + ["PF"], ["TB"])
    ts(CC[:, RM:RM + 8], col(0, 8), KH, None, EQ, None, ["col", "PF"], ["RM"])

    def onehot(out, x, wt, w):
        ts(out, col(0, 128), c1(CC, TG + x), wt, EQ, MUL, ["col"] + TGK, w)

    def mk_b(n, x, mask, key):
        ts(blk(T.BM, n, 8), T.col[:, 31:144:16], c1(CC, TB + x), mask, EQ, MUL, ["col", "TB", key], ["BM%d" % n])

    memset(T.WM1[:], 0.0, ["WM1"], 1024)
    for t, k in ((T.WM3[:], "WM3"), (T.W[:, 2048:4096], "Wy")):
        cp("a", t, T.WM1[:], ["WM1", "~a1"], [k], 2048)
    EYE, NEG, SWQ = [blk(T.PM, k) for k in range(3)]
    for k, name in enumerate(("EYE", "NEG", "SWQ")):
        onehot(blk(T.PM, k), 4 * (k // 2), 1.0 - 2 * (k % 2), [name])
    for x in (0, 2, 3, 4, 5, 6, 7):
        onehot(blk(T.RT, x), x, 1.0, ["RT%d" % x])
    MASKS, SCALES = [1, 2, 4, 3, 6, 5], [1, 2, 4, 16, 32, 2048]
    BS = T.BS
    cp("v", BS[:, 0:3], PF[:, 1:4], ["PF"], ["B6a"])
    tt(BS[:, 3:5], PF[:, 1:3], PF[:, 2:4], ALU.not_equal, ["PF"], ["B6b"])
    tt(BS[:, 5:6], PF[:, 1:2], PF[:, 3:4], ALU.not_equal, ["PF"], ["B6c"])
    ts(BS[:, 6:12], BS[:, 0:6], -1.0, 1.0, MUL, ADD, ["B6a", "B6b", "B6c"], ["SB1"])
    for n, s in enumerate(SCALES[1:]):
        ts(blk(BS, n + 1, 12), BS[:, 0:12], float(s), None, MUL, None, ["SB1"], ["SB%d" % s])

    def bit(s, f, on=range(8)):
        for k in range(12):
            if all((bin(a & MASKS[k % 6]).count("1") + k // 6) % 2 == f(a) for a in on):
                return c1(BS, 12 * SCALES.index(s) + k)

    SBK = ["SB%d" % s for s in SCALES]
    cp("v", T.RT[:, 128:130], T.RT[:, 0:2], ["RT0"], ["RT1"])
    pm = {(2, 0): 0, (3, 0): 2, (2, 1): 4, (3, 1): 6, 1: 8, 5: 10, 7: 12}
    par = BS[:, 0:7:6]
    for k, v in enumerate((1.0 / 16 - 128, 128.0)):
        ts(CC[:, 100 + 2 * k:102 + 2 * k], par, v, None, MUL, None, SBK, ["PW%d" % k])
        for x in pm:
            y, wt = (x[0], c1(CC, 101 + 2 * k - x[1])) if isinstance(x, tuple) else (x, v)
            ts(blk(T.PH, pm[x] + k), col(0, 128), c1(CC, TG + y), wt, EQ, MUL, ["col", "PW%d" % k] + TGK, ["PM%d" % (pm[x] + k)])
    ts(c1(CC, 96), I16, 0.0, None, EQ, None, ["PF"], ["R0"])
    ts(CC[:, 104:106], par, c1(CC, 96), None, MUL, None, SBK + ["R0"], ["R0p"])
    for k in range(2):
        ts(blk(T.BH, k, 8), T.col[:, 31:144:16], c1(CC, TB + 2 + k), c1(CC, 105 - k), EQ, MUL, ["col", "TB", "R0p"], ["BH%d" % k])
        ts(c1(CC, 106 + k), c1(CC, RM + 1 - k), c1(BS, 6 * k), None, MUL, None, SBK + ["RM"], ["RMp%d" % k])
        mk_b(k, 2 + k, c1(CC, 106 + k), "RMp%d" % k)
    ts(c1(CC, 108), bit(1, lambda a: 1 - (a >> 1 & 1)), bit(2, lambda a: a >> 2), bit(4, lambda a: a & 1), ADD, ADD, SBK, ["BHi"])
    ts(T.BH[:, 16:24], col(0, 8), c1(CC, 108), c1(CC, 96), EQ, MUL, ["col", "BHi", "R0"], ["BHc"])
    ts(T.CI[:], col(0, 192), I16, -64.0, SUB, ADD, ["col", "PF"], ["CI"], 96)
    for d in range(1, 8):
        t = top(d)
        lo, hi = [k for k in range(3) if k != t]
        less = [a for a in range(8) if not a >> t & 1]
        ts(c1(CC, UB + d), bit(1, lambda a: a >> t & 1), 1000.0, bit(32, lambda a: GREATER[t].index(a ^ d) >> 1, less), MUL, ADD, SBK, ["UB%d" % d])
        ts(blk(T.FM, d - 1, 192), T.CI[:], bit(16, lambda a: GREATER[t].index(a ^ d) & 1, less), c1(CC, UB + d), SUB, EQ, ["CI", "UB%d" % d] + SBK, ["FM%d" % d], 96)
        ts(blk(T.GL, d - 1, 8), col(0, 8), bit(2 ** lo, lambda a: (GREATER[t][a & 3] ^ d) >> lo & 1), bit(2 ** hi, lambda a: (GREATER[t][a & 3] ^ d) >> hi & 1),
           SUB, EQ, ["col"] + SBK, ["GL%d" % d])
        if d == 1:
            ts(T.RR[:, 0:8], T.col[:, 31:144:16], c1(CC, TB), None, EQ, None, ["col", "TB"], ["RRa1"])
        else:
            cp("av", T.RR[:, 16 * d - 16:16 * d - 8], T.RR[:, 0:8], ["RRa1"], ["RRa%d" % d])
        ts(T.RR[:, 16 * d - 8:16 * d], T.col[:, 31:144:16], c1(CC, TB + d), None, EQ, None, ["col", "TB"], ["RRb%d" % d])
    for t in range(3):
        lo, hi = [k for k in range(3) if k != t]
        ts(blk(T.GL, 7 + t, 8), col(-2 ** t, 8), bit(2 ** lo, lambda a: GREATER[t][a & 3] >> lo & 1), bit(2 ** hi, lambda a: GREATER[t][a & 3] >> hi & 1),
           SUB, EQ, ["col"] + SBK, ["GG%d" % t])
    for d in range(1, 8):
        for n, (k, key) in enumerate(((d - 1, "GL%d" % d), (7 + top(d), "GG%d" % top(d)), (d - 1, "GL%d" % d))):
            cp("a", blk(T.GF, 3 * d - 3 + n, 8), blk(T.GL, k, 8), [key], ["GF%d%d" % (d, n)])
    gf = ["GF%d%d" % (d, n) for n in range(3) for d in range(1, 8)]
    node("nop", {"g": 0.0}, None, gf, ["GF"])
    for k, v in ((1, 2.0), (2, -2.0)):
        node("op", {"a": cyc(168)}, lambda q, k=k, v=v: g.scalar.activation(blk(T.GB, k, 168), T.GF[:], ACT.Copy, scale=v), gf + ["GB1"] * (k - 1), [("GB1", "GB")[k - 1]])
    fill(T.K256[:], 256.0, ["K256"], 128)
    fill(T.CO[:], 0.0, ["CO"], 24)
    for x, v, n in ((slice(0, 3, 2), 1.0, 2), (slice(9, 11), 1.0, 2), (slice(13, 18, 4), 1.0, 2), (slice(4, 8), -1.0, 4), (slice(14, 16), -1.0, 2)):
        fill(T.CO[:, x], v, ["CO"], n)
    onehot(T.EF[:, 0:128], 0, 1.0, ["EF"])
    cp("a", T.EF[:, 128:130], T.EF[:, 0:2], ["EF"], ["EF1"])
    for n, e in enumerate((2, 4, 6, 3, 5, 7)):
        mk_b(2 + n, 1, c1(CC, RM + (e ^ 1) - 2), "RM")
    aff(T.UC[:, 16:24], CC[:, RM:RM + 8], -2048.0, 2048.0, ["RM"], ["NM"])
    nuc = [0]

    def by_pair(a, d, x, row, w):
        t, k = top(d), nuc[0]
        nuc[0] += 1
        less = [y for y in range(8) if not (y ^ x) >> t & 1]
        ts(c1(T.UC, k), bit(2, lambda y: GREATER[t].index(y ^ x ^ d) >> 1, less), bit(2048, lambda y: (y ^ x) >> t & 1), 0.0 if row is None else c1(T.UC, 16 + row),
           ADD, ADD, SBK + ["NM"], ["UC%d" % k])
        ts(T.BX[:, a:a + 4], col(0, 4), bit(1, lambda y: GREATER[t].index(y ^ x ^ d) & 1, less), c1(T.UC, k), SUB, EQ, ["col", "UC%d" % k] + SBK, w)

    def by_rank(a, x, mask, w):
        ts(T.BX[:, a:a + 8], T.col[:, 31:144:16], c1(CC, TB + x), mask, EQ, MUL, ["col", "TB", "RM"], w)

    for m in range(3):
        e = 2 * m + 2
        by_pair(4 * m, e, 1, e - 1, ["BN%d" % m])
        by_pair(12 + 12 * m, e, e + 1, None, ["BFa%d" % m])
        by_rank(16 + 12 * m, e + 1, 1.0, ["BFb%d" % m])
        for n, v in enumerate((-4.0, -5.0)):
            a, k = 48 + 24 * m, "BO%d%d" % (m, n)
            by_pair(a + 20 * n, e + 1, e + n, 7 - n, [k + "a"])
            by_rank(a + 4 + 8 * n, e + n, c1(CC, RM + 7 - n), [k + "b"])
            aff(T.BX[:, a + 12 * n:a + 12 * n + 12], T.BX[:, a + 12 * n:a + 12 * n + 12], v, 5.0, [], [k + "a", k + "b"])
    fill(T.SS[:], 0.0, ["SS" + p for p in PH], 192)
    aff(c1(CC, KH3), KH, 1.0, -3.0, ["PF"], ["KH3"])
    aff(c1(CC, KK), K1, -2.0, K7, ["PF"], ["KKa"])
    ts(c1(CC, KK + 1), K7, float(me), None, EQ, None, ["PF"], ["KKb"])
    aff(c1(CC, KK + 2), I16, 3.0, 1.0, ["PF"], ["KKc"])
    ts(T.KM[0:64, 0:128], T.cgr[0:64, :], PF[0:64, 6:7], None, EQ, None, ["cgr", "PF"], ["KM0"], 128)
    ts(T.KM[0:64, 128:256], T.cgr[0:64, :], -1.0, CC[0:64, KK:KK + 1], ADD, EQ, ["cgr", "KKa"], ["KM1"], 128)
    aff(T.KM[0:64, 256:384], T.cgr[0:64, :], 0.0, CC[0:64, KK + 1:KK + 2], ["cgr", "KKb"], ["KM2"], 128)
    aff(CC[:, I3:I3 + 8], col(0, 8), 48.0, c1(CC, KK + 2), ["col", "KKc"], ["I3"])
    fill(T.TH[:, 0:54:2], 0.0, ["TH"], 27)
    fill(T.TH[:, 4:54:6], -0.5, ["TH"], 9)
    fill(T.TH[:, 5:54:6], -0.5, ["TH5"], 9)
    for t in range(3):
        for v in range(2):
            f = t == 0 and v == 1
            aff(T.TH[:, 12 * t + 6 * v + 1:12 * t + 6 * v + 4:2], BS[:, t:t + 7:6], -0.5 if f else 0.5, 0.0 if f else -0.5, SBK, ["TH%d%d" % (t, v)])
    for m in range(3):
        aff(T.TH[:, 37 + 6 * m:40 + 6 * m:2], col(0, 2), *((0.5, -0.5) if me < (me ^ (2 * m + 3)) else (-0.5, 0.0)), ["col"], ["TH3%d" % m])
    THK = ["TH", "TH5"] + ["TH%d%d" % (t, v) for t in range(4) for v in range(2 + (t == 3))]
    aff(blk(T.H2, 7), col(0, 128), 16.0, 0.0, ["col"], ["Hid"], 128)
    aff(blk(T.LO, 7), col(0, 128), 0.0, I16, ["col", "PF"], ["Lid"], 128)
    for m in range(3):
        cp("v", T.OWN[:, 384 * m:384 * m + 384:3], blk(T.MPB, 2 * m), ["MPB"], ["OW0%d" % m], 128)

    def X(d):
        return blk(T.IE, 0) if d == 1 else blk(T.XA, d - 1) if d < 4 else blk(T.IB, d - 4)

    def xk(d):
        return "XA%d" % d if d < 4 else "IB"

    def wrows(win, items, key, qs="s", r=()):
        mv, r = [], list(r)
        for k, row in items:
            mv += [(T[win][2 * row::16, :], blk(T.H2, POS[k])), (T[win][2 * row + 1::16, :], blk(T.LO, POS[k]))]
            r += ["H%s" % k, "L%s" % k]
        dma(qs, mv, r, key, 90e3 * len(mv))

    def split(k, tile, key, n=1):
        h, l, ks = blk(T.H2, POS[k], 128, n), blk(T.LO, POS[k], 128, n), [k] if n == 1 else range(k, k + n)
        ts(h, tile, 8.0, None, ADD, None, [key], ["H%s" % x for x in ks], 64 * n)
        vop(lambda: V.tensor_tensor_scan(l, tile, h, 0.0, ALU.max, SUB), [key, "H%s" % k], ["L%s" % x for x in ks], 64 * n)

    SHIFT = 2064 * (128 - 1.0 / 16)

    def sixteen(k, tile, key):
        ts(blk(T.HB, POS[k]), tile, 2056.5, None, ADD, None, [key], ["HB%s" % k])

    def places(s, parts):
        o = ps(s, 0, 128)
        pe([m for k, x, tile, key in parts for m in ((o, blk(T.PH, pm[x] + 1), tile, 128), (o, blk(T.PH, pm[x]), blk(T.HB, POS[k]), 128))],
           [y for k, x, tile, key in parts for y in ("PM%d" % pm[x], "PM%d" % (pm[x] + 1), "HB%s" % k, key)], [s])

    def gather2(out, win, wk, lst, a, lk, name):
        for h in range(2):
            cp(on(name + "ab"[h]), T[out][:, 1024 * h:1024 * h + 1024], T[win][:, :].indirect(lst[:, a + 64 * h:a + 64 * h + 64]), wk + [lk], ["%s_%d" % (out, h)],
               int(1024 * PAR["gat"]) + 60)
            call(name + "ab"[h])

    def turn(parts, n):
        s = slot("C")
        mms = []
        for i in range(16):
            mms += [(ps(s, i, 16 * n, 128, 16), T[rb][:, i::16], m, 64) for rb, m, k in parts] + [None]
        pe(mms[:-1], [y for rb, m, k in parts for y in [rb + "_0", rb + "_1"] + k], [s])
        return s

    def turned(s, a, b, n):
        wide = b in PAR["wide"]
        cp("a" if wide else "v", blk(T.ZF if wide else T.ZH, b, 128, n), ps(s, a, a + 128 * n), [s], ["Z%d" % (b + k) for k in range(n)], 128 * n)
        for k in range(n):
            zt[b + k] = wide

    def paired(s, a, items, more=()):
        k = [PAIRED.index(x) for x in items]
        wide = items[0] in PAR["widec"]
        zb, eye, ek, f = (T.CZ, T.EF, ["EF", "EF1"], 4) if wide else (T.CH, T.RT, ["RT0", "RT1"], 1)
        cp("a" if wide else "v", blk(zb, k[0], 64, len(k)), ps(s, a, a + 64 * len(k)), [s], ["C%d%d" % x for x in items], 64 * len(k))
        for n, (d, c) in zip(k, items):
            s, fm, mms = slot("C"), T.FM[:, 192 * d - 128:192 * d - 64], []
            for b, o, x, w in ((0, 0, 0, 66), (1, 0, 64, 64), (1, 64, 0, 2)) if more else ((0, 0, 0, 66), (1, 0, 64, 66)):
                out = ps(s, o, o + w, 64 * b + 64, 1, 64 * b)
                mms += [(out, fm, t(x, w), 64) for t, tk in more] + [(out, blk(zb, n, 64), eye[:, x:x + w], 66 * f), None]
            pe(mms[:-1], ["C%d%d" % (d, c), "FM%d" % d] + ek + [tk for t, tk in more], [s])
            t = top(d)
            ts(T.FL[:, fcol(d, c):fcol(d, c) + 66], ps(s, 0, 66), bit(2048, lambda y: 1 - GREATER[t][y & 3] % 2) if t else 0.0, None, ADD, None, [s] + SBK, ["FL%d%d" % (d, c)], 66)

    zt = {}

    def to_tile(b, more=(), mk=()):
        s = slot("C")
        o = ps(s, 0, 128)
        pe([(o, blk(T.ZF, b), T.EF[:, 0:128], 512) if zt[b] else (o, blk(T.ZH, b), blk(T.RT, 0), 128)] + [(o, a, c, 128) for a, c in more], ["Z%d" % b, "RT0", "EF"] + list(mk), [s])
        return s, o

    def fcol(d, c):
        return 66 * (7 * c + d - 1)

    def lists(c, items):
        s = slot("C")
        for n, (d, tile, key) in enumerate(items):
            f, o = 192 * (d - 1), 66 * n
            lo, hi = T.FM[:, f + 64:f + 192], T.FM[:, f:f + 128]
            pe([(ps(s, o, o + 64), lo, tile(0, 64), 64), (ps(s, o, o + 64), hi, tile(64, 64), 64), None,
                (ps(s, o + 64, o + 66), lo, tile(64, 2), 64), (ps(s, o + 64, o + 66), hi, tile(0, 2), 64)], ["FM%d" % d, key], [s])
        a = fcol(items[0][0], c)
        t = top(items[0][0])
        ts(T.FL[:, a:a + 66 * len(items)], ps(s, 0, 66 * len(items)), bit(2048, lambda g: 1 - GREATER[t][g & 3] % 2) if t else 0.0, None, ADD, None,
           [s] + SBK, ["FL%d%d" % (it[0], c) for it in items], 66 * len(items))

    def half(t, k):
        return lambda a, n: t[:, 128 * k + a:128 * k + a + n]

    def xhalf(d):
        return half(T.IE, 0) if d == 1 else half(T.XA, d - 1) if d < 4 else half(T.IB, d - 4)

    def judge(d, c):
        t = "T%d" % (3 * d + c - 3)
        a = fcol(d, c)
        wn = "W%d" % (d > 1)
        act = on("g%d%d" % (d, c)) == "a"
        f = 1040 * d - 1040
        win = T.W[:, 0:4096 if d > 1 else 2048]
        src, cost, fr, fk = win.indirect(T.FL[:, a:a + 65]), int(1040 * PAR["gat"]) + 60, T.FR[:, f:f + 1040], ["FR%d" % d, "FX%d" % d]
        m = 3 * d + c - 3
        mm = blk(T.MM, m, 1040)
        e = tb(t, 0, 1040)

        def sel(x, k):
            o = 168 * k + 24 * d - 24 + 8 * (c == 1)
            return x[:, o:o + 16]

        if "g%d%d" % (d, c) in LONG["p"]:
            for x, y, w in ((0, 34, "a"), (34, 65, "b")):
                cp("a", tb(t, 16 * x, 16 * y), win.indirect(T.FL[:, a + x:a + y]), [wn, "FL%d%d" % (d, c)], [t + w, "~" + t + w] + ["~" + t + "a"] * (x > 0), int(16 * (y - x) * PAR["gat"]) + 60)
                call("gh"[x > 0] + "%d%d" % (d, c))
            for h in range(2):
                s, x = slot("C"), 512 * h
                o = ps(s, 0, 512)
                pe([(o, NEG, T.FR[:, f + x:f + x + 512], 512), (o, EYE, T.FR[:, f + x + 1:f + x + 513], 512)], ["EYE", "NEG"] + fk, [s], stop=False)
                pe([(o, EYE, tb(t, x, x + 512), 512), (o, NEG, tb(t, x + 1, x + 513), 512)], [t + "a", "EYE", "NEG"] + [t + "b"] * h, [s], start=False)
                node("op", {"a": cyc(512) + 0.02}, lambda q, o=o, h=h: g.scalar.activation(T.MM[:, 1040 * m + 512 * h:1040 * m + 512 * h + 512], z(o), ACT.Abs, accum_out=c1(T.AC, 2 * m + h)),
                     [s], ["AC%d%d" % (m, h)])
                call("ab"[h] + "%d%d" % (d, c))

            def sums(s, a, start, stop):
                o = ps(s, a, a + 16)
                mms = [[(o, u[:, x + 128 * i:x + 128 * i + 128], sel(T.GB, 1 + k), 64) for i in range(8)] for k, (u, x) in enumerate(((T.TT, 1040 * m), (T.FR, f)))]
                pe(mms[0] + mms[1][1:], [t + "a", t + "b", "GB"] + fk, [s], start=start, stop=False)
                pe([(ps(s, a, a + 16, 2), blk(T.AC, m, 2), sel(T.GF, 0), 64), mms[1][0]], ["AC%d0" % m, "AC%d1" % m, "GF"], [s], start=False, stop=stop)
            return sums
        dmas = "g%d%d" % (d, c) in LONG["d"]
        if dmas:
            node("op", {"a": cyc(cost)}, lambda q: g.scalar.activation(e, src, ACT.Copy, scale=-1.0), [wn, "FL%d%d" % (d, c)], [t])
            call("g%d%d" % (d, c))
            node("dma", {"g": PAR["gdma"]}, [(e, fr)], fk + [t], [t], PAR["dma"] + 0.4, 530e3)
        elif act:
            node("op", {"a": cyc(cost)}, lambda q: g.scalar.activation(mm, src, ACT.Identity, bias=32.0), [wn, "FL%d%d" % (d, c)], ["M" + t])
            call("g%d%d" % (d, c))
            vop(lambda: V.tensor_tensor_scan(tb(t, 0, 1026), T.FR[:, f:f + 1026], T.MM[:, 1040 * m:1040 * m + 1026], 0.0, ALU.max, SUB), ["M" + t] + fk, [t], 513)
            call("u%d%d" % (d, c))
        else:
            tt(e, src, fr, SUB, [wn, "FL%d%d" % (d, c)] + fk, [t], cost)
            call("g%d%d" % (d, c))
        vop(lambda: V.tensor_tensor_scan(T.MM[:, 1040 * m:1040 * m + 1024], tb(t, 0, 1024), tb(t, 1, 1025), -64.0 if act else 64.0,
                                         *((ALU.max, ALU.min) if act else (ALU.min, ALU.max))), [t], ["M" + t], 512)
        call("s%d%d" % (d, c))

        def sums(s, a, start, stop):
            o, w = ps(s, a, a + 16), sel(T.GB, 1 + act)
            pe([(o, T.MM[:, 1040 * m + 128 * k:1040 * m + 128 * k + 128], w, 64) for k in range(8)] + [(o, T.K256[:], w, 64)] * (act and not dmas),
               ["M" + t, "GB", "K256"], [s], start, stop)
        return sums

    def first(d):
        sums = judge(d, 0)
        s = slot("C")
        sums(s, 0, True, True)
        cp("va", blk(T.CF, d - 1, 16), ps(s, 0, 16), [s], ["CF%d" % d])

    def tile_out(s, o, d, c, dst, key, other, okey):
        cp("v", blk(*dst), o, [s], [key], 128)
        tt(blk(T.NE, 2 * d + c - 3), o, other, ALU.not_equal, [s, okey], ["NE%d%d" % (d, c)], 128)

    def counts(d, cs):
        sums = [judge(d, c) for c in cs]
        s = slot("C")
        a = 16 * d - 16
        pe([(ps(s, 0, 8), blk(T.NE, 2 * d - 1), T.GW[:, a:a + 8], 64), None, (ps(s, 8, 24), blk(T.NE, 2 * d - 2), T.GW[:, a:a + 16], 64)],
           ["NE%d1" % d, "NE%d2" % d, "GW%d" % d], [s], stop=False)
        sums[0](s, 8, False, False)
        sums[1](s, 8, False, True)
        cp("va", blk(T.CW, d - 1, 24), ps(s, 0, 24), [s], ["CW%d" % d])

    def scores(ph, ds):
        a = 32 * PH.index(ph)
        k = "SS" + ph
        for m, d in enumerate(ds):
            s = slot("C")
            o = ps(s, 0, 6, 8)
            pe([(o, blk(T.CF, 2 * d - 2 + n, 8), blk(T.CO, 0, 6), 32) for n in range(2)] + [(o, blk(T.CW, 3 * d - 3 + n, 8), blk(T.CO, c, 6), 32) for n, c in enumerate((0, 2, 1))],
               ["CW%d" % d, "CO", "CF%d" % d], [s])
            cp("va", T.SS[0:8, a + 6 * m:a + 6 * m + 6], o, [s, k], [k + str(m)])
        ld = "LdS" + ph
        dma("s", [(T[ld][me], T.SS[0:8, a:a + 32])], [k] + [k + str(m) for m in range(len(ds))], [ld], 1e3)
        exchange("S" + ph, [ld], PAR["S"])
        dma("s", [(T.SC[0:64, a:a + 32], T[ld][:])], [ld, "arS" + ph], ["SC" + ph], 8e3)

    def decide(ph, views, th):
        s = slot("C")
        a = 32 * PH.index(ph)
        mms, n = [], 0
        for km, w in views:
            mms += [(ps(s, n, n + w), T.KM[0:64, 128 * km:128 * km + 128], T.SC[0:64, a:a + w], 256), None]
            n += w
        pe(mms[:-1], ["SC" + ph, "KM0", "KM1", "KM2"], [s])
        tt(T.DE[:, a:a + n], ps(s, 0, n), T.TH[:, th:th + n], GT, [s] + THK, ["x" + ph])
        tt(T.DE[:, a + 20:a + 20 + n // 2], T.DE[:, a:a + n:2], T.DE[:, a + 1:a + n:2], MUL, ["x" + ph], ["y" + ph])
        return (lambda i: c1(T.DE, a + 20 + i)), "y" + ph

    def pick(out, win, m, ind, i, key, r, w):
        ts(blk(T.OF, m, 8), CC[:, I3:I3 + 8], ind(i + 1), ind(i + 2), ADD, SUB, ["I3", key], ["OF%d" % m])
        cp("va" if m else "v", out, win.indirect(blk(T.OF, m, 8)), r + ["OF%d" % m], w, int(128 * PAR["gat"]) + 60)

    nsc = [0]

    def scaled(tile, tk, ind, key):
        n = nsc[0]
        nsc[0] += 1
        ts(blk(T.SCL, n), tile, ind, None, MUL, None, [tk, key], ["SCL%d" % n])
        return blk(T.SCL, n), "SCL%d" % n

    def final(d, n, terms):
        s = slot("C")
        pe([(ps(s, 0, 128), blk(T.RT, 0), t, 128) for t, k in terms], ["RT0"] + [k for t, k in terms], [s])
        cp("va", blk(T.FIN, n), ps(s, 0, 128), [s], ["FIN%d" % d], 128)
        y, k = "Y%d" % (n // 2), 64 * (n % 2)
        st, ld = T["St" + y], T["Ld" + y]
        dma("s", [(st[:, k:k + 64, :], blk(T.FIN, n)), (ld[me, k:k + 64, :], T.FIN[mine, 128 * n:128 * n + 128])], ["FIN%d" % d], ["StY%d" % d], 70e3)
        if k:
            ds = (d - 2 + (d == 2), d)
            exchange(y, ["StY%d" % e for e in ds], PAR["Y"])
            dma("s", [(blk(T.ym, e - 1), ld[:, 64 * i:64 * i + 64, :]) for i, e in enumerate(ds)], ["StY%d" % e for e in ds] + ["ar" + y], ["ym%d" % d], 131e3)

    def home(name, a, b):
        st, ld = T["St" + name], T["Ld" + name]
        ks = ["%s%d" % (x, 2 * m + 3) for m in range(a, b) for x in "AB"]
        dma("s", [(st[:], T.C3[:, 256 * a:256 * b]), (ld[me], T.C3[mine, 256 * a:256 * b])], ks, ["St" + name], 70e3 * (b - a))
        exchange(name, ["St" + name], PAR[name])
        dma("s", [(T.OL[:, 256 * a:256 * b], ld[:])], ["St" + name, "ar" + name], ["OL" + name], 65e3 * (b - a))
        for m in range(a, b):
            for c in range(2):
                cp("v", T.OWN[:, 384 * m + 1 + c:384 * m + 384:3], blk(T.OL, 2 * m + c), ["OL" + name], ["OW%d%d" % (c + 1, m)], 128)

    def feats(dst, o, ranks, hs):
        return [(dst[64 * b + 16 * u:64 * b + 16 * (u + cnt), o + 1024 * i:o + 1024 * i + 1024], T.LdF[2 * v + h:2 * (v + s * (cnt - 1)) + h + 1:2 * s])
                for b in range(2) for i, h in enumerate(hs(b)) for u, cnt, v, s in runs(ranks)]

    stage(1)
    dma("s", [(blk(T.IA, 1 + k), T.LdA[:, 64 * k:64 * k + 64, :]) for k in range(2)], ["LdA", "arA"], ["IA1"], 131e3)
    dma("a", [(T.WI[0::32, :], T.LdA[0::2, 64:128, :]), (T.WI[16::32, :], T.LdA[1::2, 0:64, :])], ["LdA", "arA"], ["WI"], 65e3)
    dma("s", [(T.IE[:], T.LdE[:])], ["StE", "arE"], ["XA1"], 50e3)
    for d in (2, 3):
        cp("v", X(d), blk(T.IA, d - 1), ["IA1"], [xk(d)], 128)
    for d in (2, 3, 1):
        split(d, X(d), xk(d))
    wrows("WM1", [(2, 0), (3, 1)], ["WM1"], "s", ["WM1"])
    for d in (2, 3):
        sixteen(d, X(d), xk(d))

    def recode(parts, n, key):
        s = slot("C")
        places(s, parts)
        ts(blk(T.LQ, n), ps(s, 0, 128), SHIFT, None, ADD, None, [s], [key], 128)

    recode([(d, (d, 0), X(d), xk(d)) for d in (2, 3)], 0, "LQ0")
    recode([(d, (d, 1), X(d), xk(d)) for d in (2, 3)], 4, "LQ1")
    recode([(3, (3, o), X(3), xk(3)) for o in range(2)], 1, "LQ3")
    stage("w0")
    dma("s", feats(T.W, 0, GREATER[0], lambda b: (0, 1)), ["LdF", "arF"], ["W0"], 524e3)
    stage("w1")
    dma("s", feats(T.W, 2048, [7 - j for j in GREATER[0][:3]], lambda b: (0, 1)), ["LdF", "arF"], ["Wy"], 393e3)
    node("nop", {"g": 0.0}, None, ["W0", "Wy"], ["W1"])
    for d in range(1, 8):
        stage("f%d" % d)
        f = 1040 * d - 1040
        dma("s", feats(T.FR, f, [j ^ d for j in GREATER[top(d)]], lambda b: (b,)), ["LdF", "arF"], ["FR%d" % d], 262e3)
        s = slot("C")
        pe([(ps(s, 0, 16), SWQ, T.FR[:, f:f + 16], 64)], ["SWQ", "FR%d" % d], [s])
        cp("va", T.FR[:, f + 1024:f + 1040], ps(s, 0, 16), [s], ["FX%d" % d])
    exchange("B", ["StB", "~arE"] + PAR["Bafter"], PAR["B"])
    dma("s", [(T.IB[:], T.LdB[:])], ["StB", "arB"], ["IB"], 135e3)
    for h in range(2):
        cp("v", blk(T.RA, h, 1024), T.WI[:, :].indirect(blk(T.LQ, h, 64)), ["WI", "LQ0"], ["RA_%d" % h], int(1024 * PAR["gat"]) + 60)
        call("R" + "ab"[h])
    paired(turn([("RA", T.BH[:, 16:24], ["BHc"])], 8), 0, [(1, 1), (1, 2)])
    gather2("RB", "WM1", ["WM1", "WM2b", "WM2c"], T.LQ, 512, "LQ1", "B")
    turned(turn([("RA", T.BH[:, 0:16], ["BH0", "BH1"]), ("RB", T.BM[:, 0:16], ["BM0", "BM1"])], 16), 0, 0, 2)
    for c, (k, dst) in enumerate((("A", (T.NT, 1)), ("B", (T.FT, 1)))):
        s, o = to_tile(c)
        cp("v", blk(*dst), o, [s], ["NF"[c] + "1"], 128)
        tt(blk(T.NE, c), o, (X(1), blk(T.NT, 1))[c], ALU.not_equal, [s, ("XA1", "N1")[c]], ["NE1%d" % (c + 1)], 128)
        split(k, blk(*dst), "NF"[c] + "1")
    lists(0, [(1, xhalf(1), "XA1")])
    lists(0, [(d, xhalf(d), xk(d)) for d in (2, 3)])
    lists(0, [(d, xhalf(d), "IB") for d in (4, 5, 6, 7)])
    ts(T.WF[:, 0:7], T.IE[:, 128:135], -1.0, None, MUL, None, ["XA1"], ["WF"])

    def weigh(d):
        def f(q):
            if q == "v":
                return V.tensor_scalar(blk(T.GW, d - 1, 16), blk(T.RR, d - 1, 16), c1(T.WF, d - 1), None, MUL)
            return g.scalar.activation(blk(T.GW, d - 1, 16), blk(T.RR, d - 1, 16), ACT.Copy, scale=c1(T.WF, d - 1))
        node("op", {"v": cyc(1), "a": cyc(1)}, f, ["RRa%d" % d, "RRb%d" % d, "WF"], ["GW%d" % d])

    for d in range(1, 8):
        weigh(d)
    split(4, T.IB[:, 0:512], "IB", 4)
    stage("r1")
    first(1)
    counts(1, (1, 2))
    scores("1", [1])

    stage(10)
    wrows("WM3", [(1, 2)], ["WM3a"], "s", ["WM3"])
    wrows("WM3", [("A", 3), ("B", 4)], ["WM3b"], "s", ["WM3"])
    stage("wm")
    wrows("WM1", [("id", 6)], ["WM2c"], "s", ["WM1"])
    wrows("WM1", [(4, 2), (5, 3), (6, 4), (7, 5)], ["WM2b"], "s", ["WM1"])
    stage(10)
    for d in (5, 7):
        sixteen(d, X(d), "IB")
        recode([(d, d, X(d), "IB")], d // 2, "LQ%d" % d)
    for c, (k, tile, key) in enumerate(((1, X(1), "XA1"), ("A", blk(T.NT, 1), "N1"), ("B", blk(T.FT, 1), "F1"))):
        sixteen(k, tile, key)
        s = slot("C")
        places(s, [(k, 1, tile, key)])
        addc("va", T.PI1[:, c:384:3], ps(s, 0, 128), SHIFT, [s], ["PI1%d" % c], 128, False)
    for m in range(3):
        gather2("RF%d" % m, "WM3", ["WM3a", "WM3b"], T.LQ, 128 + 128 * m, "LQ%d" % (2 * m + 3), "F%d" % (2 * m + 2))
    for d in (2, 4, 6, 3, 5, 7):
        stage("c%d" % d)
        first(d)

    stage("rn")
    ind, key = decide("1", [(0, 6), (1, 6)], 0)
    pick(T.LN[:], T.PI1[:, :], 0, ind, 3, key, ["PI10", "PI11", "PI12"], ["LN"])
    gather2("RN", "WM1", ["WM1", "WM2b", "WM2c"], T.LN, 0, "LN", "N")
    ts(c1(T.DE, 28), ind(1), ind(2), c1(CC, KH3), SUB, EQ, [key, "KH3"], ["sel"])
    dma("s", [(T.RB[12 + i::16, :], T.RN[12 + i::16, :]) for i in range(2)]
        + [(T.RB[16 * (1 - b) + 14 + i::32, :], T.RN[16 * b + 12 + i::32, :]) for b in range(2) for i in range(2)], ["RN_0", "RN_1"], ["RB_0", "RB_1"], 131e3)
    paired(turn([("RN", T.BX[:, 0:12], ["BN0", "BN1", "BN2"])], 12), 0, [(2, 1), (4, 1), (6, 1)])
    turned(turn([("RN", T.BM[:, 16:40], ["BM2", "BM3", "BM4"])], 24), 0, 2, 3)
    mul("va", T.BX[:, 120:156], T.BX[:, 12:48], c1(T.DE, 28), ["sel"] + ["BF%s%d" % (x, m) for x in "ab" for m in range(3)], ["BF"])
    for m in range(3):
        d = 2 * m + 2
        s = turn([("RF%d" % m, T.BX[:, 120 + 12 * m:132 + 12 * m], ["BF"])], 12)
        paired(s, 0, [(d, 2)])
        turned(s, 64, 8 + m, 1)
        s, o = to_tile(8 + m)
        cp("v", blk(T.FT, d), o, [s], ["F%d" % d], 128)
        s, o = to_tile(2 + m)
        tile_out(s, o, d, 1, (T.NT, d), "N%d" % d, X(d), xk(d))
        tt(blk(T.NE, 2 * d - 1), o, blk(T.FT, d), ALU.not_equal, [s, "F%d" % d], ["NE%d2" % d], 128)
        counts(d, (2, 1))
        scores(str(d), [d])
    stage("fin")
    final(1, 0, [scaled(X(1), "XA1", ind(2), key), scaled(blk(T.NT, 1), "N1", ind(0), key), scaled(blk(T.FT, 1), "F1", ind(1), key)])
    stage("n3")
    turned(turn([("RN", T.BM[:, 40:64], ["BM5", "BM6", "BM7"])], 24), 0, 5, 3)
    for d in (3, 5, 7):
        stage("n%d" % d)
        s, o = to_tile(4 + d // 2)
        cp("v", blk(T.NT, d), o, [s], ["N%d" % d], 128)

    for m in range(3):
        d, e = 2 * m + 3, 2 * m + 2
        stage("t%d" % d)
        ind, key = decide(str(e), [(0, 6), (1, 6)], 12 * top(e))
        xz, nn, nf = scaled(X(e), xk(e), ind(2), key), scaled(blk(T.NT, e), "N%d" % e, ind(0), key), scaled(blk(T.NT, e), "N%d" % e, ind(4), key)
        s = slot("C")
        pe([(ps(s, 0, 128), blk(T.RT, x), t[0], 128) for x, t in ((d, xz), (d, nn), (e, nf))], ["RT%d" % d, "RT%d" % e, xz[1], nn[1], nf[1]], [s])
        cp("v", blk(T.LF3, m), ps(s, 0, 128), [s], ["LF3%d" % m], 128)
        gather2("RF%d" % m, "RB", ["RB_0", "RB_1"], T.LF3, 128 * m, "LF3%d" % m, "F%d" % d)
        b = 11 + 2 * m
        bo = T.BX[:, 156 + 24 * m:180 + 24 * m]
        ts(bo, T.BX[:, 48 + 24 * m:72 + 24 * m], ind(3), None, EQ, None, ["BO%d%d%s" % (m, n, x) for n in range(2) for x in "ab"] + [key], ["BO%d" % m])
        s = turn([("RF%d" % m, bo, ["BO%d" % m])], 24)
        a1, a2, b1 = scaled(blk(T.NT, d), "N%d" % d, ind(5), key), scaled(X(d), xk(d), ind(3), key), scaled(X(d), xk(d), ind(1), key)
        paired(s, 320, [(d, 2)], [(half(T.SCL, int(b1[1][3:])), b1[1])])
        paired(s, 0, [(d, 1)], [(half(T.SCL, int(t[1][3:])), t[1]) for t in (a1, a2)])
        turned(s, 64, b, 2)
        s, o = to_tile(b, [(blk(T.RT, 0), a1[0]), (blk(T.RT, 0), a2[0])], ["RT0", a1[1], a2[1]])
        tile_out(s, o, d, 1, (T.C3, 2 * m), "A%d" % d, X(d), xk(d))
        s, o = to_tile(b + 1, [(blk(T.RT, 0), b1[0])], ["RT0", b1[1]])
        tile_out(s, o, d, 2, (T.C3, 2 * m + 1), "B%d" % d, blk(T.C3, 2 * m), "A%d" % d)
        counts(d, (1, 2))
        stage("fin")
        final(e, m + 1, [xz, nn, scaled(blk(T.FT, e), "F%d" % e, ind(1), key)])
    stage(60)
    home("O3", 0, 2)
    home("O7", 2, 3)
    for ph, a, b in (("5", 0, PAR["cutS"]), ("7", PAR["cutS"], 3))[not PAR["cutS"]:]:
        scores(ph, range(2 * a + 3, 2 * b + 3, 2))
        ind, key = decide(ph, [(2, 6 * (b - a))], 36 + 6 * a)
        for m in range(a, b):
            pick(blk(T.YO, m), blk(T.OWN, m, 384), 1 + m, ind, 3 * (m - a), key, ["OW%d%d" % (c, m) for c in range(3)], ["YO%d" % m])
            dma("as", [(blk(T.ym, 2 * m + 2), blk(T.YO, m))], ["YO%d" % m], ["ym%d" % (2 * m + 3)], 65e3)

    for nd in nodes:
        if nd["kind"] == "ex":
            nd["w"] = nd["w"] + ["~" + nd["w"][0]]
    if "order" not in PLAN:
        tied = []
        for i, nd in enumerate(nodes):
            tied.append(dict(nd))
        PLAN["order"], PLAN["val"] = plan(tied)
    if "dry" in PAR:
        return
    val.update(PLAN["val"])
    waited = {q: {} for q in Q}
    lastw, readers, total = {}, {}, {}
    ndma = [0]

    def need(q, toks):
        best = {}
        for s, n in toks:
            if not (q == "p" and s == "cp"):
                best[s] = max(best.get(s, 0), n)
        for s, n in best.items():
            if waited[q].get(s, 0) < n:
                Q[q].wait_ge(T.sem[s], n)
                waited[q][s] = n

    for i, q in PLAN["order"]:
        nd = nodes[i]
        r, x, w = [[val.get(k, k) for k in nd[y] if k[0] != "~"] for y in "rxw"]
        toks = []
        for k in r + x + w:
            toks += lastw.get(k, [])
        for k in w:
            toks += readers.get(k, [])
        for k in x:
            toks += [tk for tk in readers.get(k, []) if tk[0] != CS[q]]
        if nd["kind"] == "nop":
            lastw[w[0]] = [tk for k in r for tk in lastw[k]]
            continue
        need(q, toks)
        if nd["kind"] == "ex":
            name, one = nd["f"]
            total["sent"] = total.get("sent", 0) + send(g, T, topo, deal(T, topo, me, name)[0], name, one)
            s = "ar" + name
            total[s] = sum(bits(t[3]) for b in range(8) for part in deal(T, topo, b, name) for t in part if t[0] == core)
            if one != 0:
                lastw[s] = [(s, total[s])]
            continue
        if nd["kind"] == "fold":
            n, s = nd["f"], w[0]
            sib = T.cores[me ^ 1]
            m = sum(1 << e for e in topo.engines(core, sib)[-PAR["Me"]:])
            g.remote_dma_fused([RemoteDMATransfer(dst_ids=[DstId(rid=topo.addr(sib)[0], pnc=topo.addr(sib)[1])], dma_engine_mask=m, remote_sem=T.sem[s], alu_op=2,
                                                  srcs=[T.TT[:, 1024 * n + k:1024 * n + k + 1023] for k in range(2)], dsts=[T.MM[:, 1024 * n:1024 * n + 1023]])],
                               local_sem=T.sem.sent)
            total["sent"] += bits(m)
            total[s] = bits(m)
            lastw[s] = [(s, total[s])]
            continue
        if nd["kind"] == "dma":
            s = "d%d" % ndma[0]
            ndma[0] += 1
            for o, y in nd["f"]:
                (g.dma_start(o, y, accum_op=ADD) if q == "g" else Q[q].dma_start(o, y)).then_inc(T.sem[s], 16)
            total[s] = 16 * len(nd["f"])
        else:
            s = CS[q]
            total[s] = total.get(s, 0) + 1
            if nd["kind"] == "pe":
                for m in nd["f"]:
                    last = g.tensor.matmul(z(m[0]), z(m[1]), z(m[2]), m[3], m[4])
                last.then_inc(T.sem.cp, 1)
            else:
                nd["f"](q).then_inc(T.sem[s], 1)
        for k in r + x:
            readers.setdefault(k, []).append((s, total[s]))
        for k in w:
            lastw[k] = [(s, total[s])]
            readers[k] = []
    need("g", list(total.items()))
